import numpy as np
import ml_dtypes


def mxq(x, axis, fmt="e4m3"):
    dtype, down = {"e4m3": (ml_dtypes.float8_e4m3fn, 7), "e5m2": (ml_dtypes.float8_e5m2, 14)}[fmt]
    v = np.moveaxis(np.asarray(x, np.float32).astype(ml_dtypes.bfloat16).astype(np.float64), axis, -1)
    blocks = v.reshape(v.shape[:-1] + (-1, 32))
    amax = np.abs(blocks).max(-1, keepdims=True)
    byte = np.maximum(np.where(amax > 0, np.frexp(amax)[1] - 1 + 127, 0) - down, 1)
    scale = np.exp2(byte - 127.0)
    codes = (blocks / scale).astype(np.float32).astype(dtype).astype(np.float64)
    return np.moveaxis((codes * scale).reshape(v.shape), -1, axis)


WIDE = False


def mx_kscale(k):
    if not WIDE:
        return np.ones(k)
    levels = np.array([24, -24, 12, -12, 0])
    if k % 512:
        return np.exp2(np.random.permutation(np.resize(levels, k // 32))).repeat(32)
    a = np.empty((k // 512, 16))
    for p in range(k // 512):
        a[p, :8] = np.random.permutation(np.resize(levels, 8))
        for g in range(8):
            far = levels[np.abs(levels - a[p, g]) >= 10]
            a[p, g + 8] = far[np.random.randint(len(far))]
    return np.exp2(a.ravel()).repeat(32)


def f64(x):
    return np.asarray(x).astype(np.float64)


def striped(idx):
    return np.tile(idx.reshape(-1, 16).T, (8, 1)).astype(np.uint16)


def unstriped(offs):
    return offs[:16].T.reshape(-1).astype(np.int64)


E2M1 = np.array([0.0, 0.5, 1.0, 1.5, 2.0, 3.0, 4.0, 6.0, -0.0, -0.5, -1.0, -1.5, -2.0, -3.0, -4.0, -6.0])


def pack_weight(w, fmt):
    k, n = w.shape
    w = f64(np.asarray(w, np.float32).astype(ml_dtypes.bfloat16)).reshape(k // 32, 32, n)
    amax = np.abs(w).max(1)
    if fmt == "e4m3":
        byte = np.frexp(amax)[1] - 1 + 127 - 7
    else:
        mant, ex = np.frexp(amax / 6.0)
        byte = np.where(mant > 0.5, ex, ex - 1) + 127
    byte = np.clip(np.where(amax > 0, byte, 1), 1, 254)
    scaled = (w * np.exp2(127.0 - byte)[:, None, :]).reshape(k, n).astype(np.float32)
    by_word = np.ascontiguousarray(scaled.reshape(k // 512, 128, 4, n).transpose(0, 1, 3, 2))
    if fmt == "e4m3":
        words = by_word.astype(ml_dtypes.float8_e4m3fn).view(np.uint8)
    else:
        c = by_word.astype(ml_dtypes.float4_e2m1fn).view(np.uint8) & 0xF
        words = (c[..., 0::2] | (c[..., 1::2] << 4)).reshape(k // 512, 128, 2 * n)
    return np.ascontiguousarray(words), np.ascontiguousarray(byte.astype(np.uint8).reshape(k // 512, 16, n))


def unpack_weight(words, scales, fmt):
    g, _, n = scales.shape
    words = np.ascontiguousarray(words).reshape(g, 128, n, -1)
    if fmt == "e4m3":
        vals = words.view(ml_dtypes.float8_e4m3fn).astype(np.float64)
    else:
        nib = np.empty((g, 128, n, 4), np.uint8)
        nib[..., 0::2] = words & 0xF
        nib[..., 1::2] = words >> 4
        vals = E2M1[nib]
    vals = vals * np.repeat(np.exp2(scales.astype(np.float64) - 127.0), 8, axis=1)[..., None]
    return vals.transpose(0, 1, 3, 2).reshape(g * 512, n)


def planes(y):
    n, m = y.shape
    v = y.astype(np.float32).astype(ml_dtypes.bfloat16).astype(np.float64).reshape(n // 32, 32, m)
    top = np.abs(v).max(1)
    byte = np.clip(np.where(top > 0, np.frexp(top)[1] - 1 + 127 - 7, 1), 1, 254)
    codes = (v * np.exp2(127.0 - byte)[:, None, :]).reshape(n, m).astype(np.float32).astype(ml_dtypes.float8_e4m3fn).view(np.uint8)
    words = codes.reshape(n // 512, 128, 4, m).transpose(0, 1, 3, 2)
    return np.ascontiguousarray(words), np.ascontiguousarray(byte.astype(np.uint8).reshape(n // 512, 16, m))


def sigm(f):
    return 1.0 / (1.0 + np.exp(-np.maximum(f, -700.0)))


K, N, T, J = 512, 512, 2048, 1024


def setup_inputs():
    n = np.random.standard_normal
    s = mx_kscale(K)[:, None]
    p_tab = pack_weight(n((K, T)) * s, "e4m3")
    p_wc = pack_weight(n((K, N)) / np.sqrt(K) / s, "e2m1")
    return {
        "tab_words": p_tab[0],
        "tab_scales": p_tab[1],
        "wa": (n((K, N)) / np.sqrt(2 * K) / s).astype(np.float32),
        "wb": (n((K, N)) / np.sqrt(2 * K) / s).astype(np.float32),
        "wc_words": p_wc[0],
        "wc_scales": p_wc[1],
        "wo": (n((K, N)) / np.sqrt(K) / s).astype(np.float32),
        "rT": (n((N, T))).astype(np.float32),
        "wgo": np.tile(np.random.uniform(0.5, 2.0, J), (128, 1)).astype(np.float32),
        "offs": striped(np.random.permutation(T)[:J]),
        "offs2": striped(np.random.permutation(T)[:J]),
    }


def reference(tab_words, tab_scales, wa, wb, wc_words, wc_scales, wo, rT, wgo, offs, offs2):
    idx = unstriped(offs)
    idx2 = unstriped(offs2)
    tab_ = unpack_weight(tab_words, tab_scales, "e4m3")[:, idx]
    tabb_ = unpack_weight(tab_words, tab_scales, "e4m3")[:, idx2]
    wa_ = mxq(f64(wa), 0, "e4m3")
    wb_ = mxq(f64(wb), 0, "e4m3")
    za = wa_.T @ tabb_ + wb_.T @ tab_
    eta = sigm(za)
    wc_ = unpack_weight(wc_words, wc_scales, "e2m1")
    ms = wc_.T @ tab_
    wo_ = mxq(f64(wo), 0, "e4m3")
    ow = wo_.T @ tabb_
    out = np.zeros((N, T))
    out[:, idx2] = f64(wgo)[0] * (ow + eta * ms + f64(rT)[:, idx2])
    return (out,) + planes(out)

@@ -1,0 +1,245 @@
+from contextlib import ExitStack
+
+import concourse.mybir as mybir
+from concourse.masks import make_identity
+
+K, N, T, J = 512, 512, 2048, 1024
+FLOPS = 4 * 2 * K * N * J
+
+F32 = mybir.dt.float32
+BF16 = mybir.dt.bfloat16
+I32 = mybir.dt.int32
+U32 = mybir.dt.uint32
+U16 = mybir.dt.uint16
+U8 = mybir.dt.uint8
+FP8X4 = mybir.dt.float8_e4m3fn_x4
+FP4X4 = mybir.dt.float4_e2m1fn_x4
+MULT = mybir.AluOpType.mult
+ADD = mybir.AluOpType.add
+COPY = mybir.ActivationFunctionType.Copy
+SIGMOID = mybir.ActivationFunctionType.Sigmoid
+
+P = 128
+PACK = 4
+EDGE_TILES = J // P
+HALF = J // 2
+CHUNK = 512
+WINDOWS = 3
+ORDER = (0, 2, 3, 1)
+
+
+def tile_list_rgg_ownLP_kernel(
+    tc, tab_words, tab_scales, wa, wb, wc_words, wc_scales, wo, rT, wgo, offs, offs2, out_0, out_1, out_2
+):
+    nc = tc.nc
+    with ExitStack() as ctx:
+        keep = ctx.enter_context(tc.tile_pool(name="keep", bufs=1))
+        ring = ctx.enter_context(tc.tile_pool(name="ring", bufs=3))
+        psum = ctx.enter_context(tc.psum_pool(name="psum", bufs=2))
+
+        def held(name, shape, dtype):
+            return keep.tile(shape, dtype, name=name, align_bytes=64)
+
+        def load_scale_rows(plane, rows):
+            for q in range(4):
+                nc.sync.dma_start(out=plane[32 * q : 32 * q + 4, :].bitcast(I32), in_=rows.bitcast(I32)[4 * q : 4 * q + 4, :])
+
+        src = held("src", [P, J // 16], U16)
+        dst = held("dst", [P, J // 16], U16)
+        tab_plane = held("tab_plane", [P, T], U8)
+        tab_codes = held("tab_codes", [P, T], I32)
+        nc.vector.memset(tab_plane[:].bitcast(I32), 0)
+        nc.sync.dma_start(dst[:], offs2)
+        nc.sync.dma_start(src[:], offs)
+        nc.sync.dma_start(out=tab_codes[:], in_=tab_words[0].rearrange("p t i -> p (t i)").bitcast(I32))
+        load_scale_rows(tab_plane, tab_scales[0])
+
+        warm = held("warm", [P, 2], F32)
+        nc.gpsimd.memset(warm[:, 0:1], 0.0)
+        nc.scalar.activation(warm[:, 1:2], warm[:, 0:1], SIGMOID)
+
+        ident = held("ident", [P, P], F32)
+        make_identity(nc, ident[:])
+        wc_plane = held("wc_plane", [P, N], U8)
+        wc_codes = held("wc_codes", [P, 2 * N], U8)
+        nc.gpsimd.memset(wc_plane[:].bitcast(I32), 0)
+
+        windows = [held("window%d" % i, [P, T], F32) for i in range(WINDOWS - 1)]
+        for w in windows:
+            nc.vector.memset(w[:], 0.0)
+
+        raw = {}
+        for name, w in (("wa", wa), ("wb", wb), ("wo", wo)):
+            raw[name] = held("raw_" + name, [P, PACK, N], F32)
+            nc.sync.dma_start(out=raw[name][:], in_=w.rearrange("(p i) n -> p i n", i=PACK))
+        wg_row = held("wg_row", [P, J], F32)
+        nc.sync.dma_start(out=wg_row[:], in_=wgo)
+        nc.sync.dma_start(out=wc_codes[:].bitcast(I32), in_=wc_words[0].bitcast(I32))
+        load_scale_rows(wc_plane, wc_scales[0])
+        r_rows = rT.rearrange("(p t) c -> t p c", t=PACK)
+        state = {}
+        for t in ORDER:
+            state[t] = held("state%d" % t, [P, T], F32)
+            nc.sync.dma_start(out=state[t][:], in_=r_rows[t])
+
+        picked_plane = {}
+        picked_codes = {}
+
+        def gather_planes():
+            for name, lst in (("src", src), ("dst", dst)):
+                picked_plane[name] = held("plane_" + name, [P, J], U8)
+                nc.vector.tensor_copy(picked_plane[name][:], tab_plane[:].indirect(lst[:]))
+
+        def gather_codes(h):
+            for name, lst in (("dst", dst), ("src", src)):
+                picked_codes[name, h] = held("codes_%s%d" % (name, h), [P, HALF], U32)
+                nc.vector.tensor_copy(
+                    picked_codes[name, h][:], tab_codes[:].bitcast(U32).indirect(lst[:, 32 * h : 32 * (h + 1)])
+                )
+
+        w_codes = {}
+        w_plane = {}
+
+        def quantise_weight(name):
+            grouped = keep.tile([P, N, PACK], BF16, name="grouped_" + name, tag="grouped_" + name, align_bytes=64)
+            nc.scalar.copy(
+                grouped[:].rearrange("p (c e) i -> p c i e", e=4), raw[name][:].rearrange("p i (c e) -> p c i e", e=4)
+            )
+            w_codes[name] = held("wcodes_" + name, [P, N], U32)
+            w_plane[name] = held("wplane_" + name, [P, N], U8)
+            nc.vector.quantize_mx(
+                out=w_codes[name][:].bitcast(FP8X4), scales=w_plane[name][:], in_=grouped[:].rearrange("p n i -> p (n i)")
+            )
+
+        gather_codes(0)
+        gather_codes(1)
+        gather_planes()
+        quantise_weight("wa")
+        quantise_weight("wb")
+
+        wg_col = held("wg_col", [P, EDGE_TILES], F32)
+        for b in range(EDGE_TILES // PACK):
+            turned = psum.tile([P, PACK, P], F32, name="turned")
+            for u in range(PACK):
+                e = PACK * b + u
+                nc.tensor.transpose(turned[:, u, :], wg_row[:, P * e : P * (e + 1)], ident[:])
+            nc.scalar.copy(wg_col[:, PACK * b : PACK * (b + 1)], turned[:, :, 0])
+
+        quantise_weight("wo")
+        windows.append(keep.tile([P, T], F32, name="window_last", tag="grouped_wo", align_bytes=64))
+        nc.gpsimd.memset(windows[-1][:], 0.0)
+
+        summed = held("summed", [P, PACK, J], F32)
+        picked_state = [held("picked_state%d" % s, [P, J], F32) for s in range(PACK - 1)]
+        spare = [held("spare%d" % i, [P, HALF], F32) for i in range(3)]
+
+        def piece(k):
+            s, h = divmod(k, 2)
+            if s < PACK - 1:
+                return picked_state[s][:, HALF * h : HALF * (h + 1)]
+            return spare[0][:] if h == 0 else picked_state[PACK - 2][:, HALF:]
+
+        def eta_place(e):
+            if e < 5:
+                return piece(e + 1)
+            return spare[(e - 4) % 3][:]
+
+        def dealt(bank):
+            return bank[:].rearrange("p (m t) -> p t m", t=PACK)
+
+        def product(bank, side, e, codes, plane, start, stop):
+            h, c = divmod(P * e, HALF)
+            nc.tensor.matmul_mx(
+                out=bank[:],
+                lhsT=picked_codes[side, h][:, c : c + P].bitcast(FP8X4),
+                lhsT_scale=picked_plane[side][:, P * e : P * (e + 1)],
+                rhs=codes,
+                rhs_scale=plane,
+                start=start,
+                stop=stop,
+            )
+
+        gated = {}
+        own = {}
+
+        def edge_products(e):
+            ms = psum.tile([P, N], F32, name="ms")
+            za = psum.tile([P, N], F32, name="za")
+            ow = psum.tile([P, N], F32, name="ow")
+            product(ms, "src", e, wc_codes[:].bitcast(FP4X4), wc_plane[:], True, True)
+            product(za, "src", e, w_codes["wb"][:].bitcast(FP8X4), w_plane["wb"][:], True, False)
+            product(za, "dst", e, w_codes["wa"][:].bitcast(FP8X4), w_plane["wa"][:], False, True)
+            product(ow, "dst", e, w_codes["wo"][:].bitcast(FP8X4), w_plane["wo"][:], True, True)
+            eta = eta_place(e).rearrange("p (t m) -> p t m", t=PACK)
+            nc.scalar.activation(eta, dealt(za), SIGMOID)
+            gated[e] = ring.tile([P, PACK, P], F32, name="gated")
+            nc.vector.scalar_tensor_tensor(gated[e][:], dealt(ms), wg_col[:, e : e + 1], eta, MULT, MULT)
+            own[e] = ring.tile([P, PACK, P], F32, name="own")
+            nc.scalar.activation(own[e][:], dealt(ow), COPY, scale=wg_col[:, e : e + 1])
+
+        def turn_and_add(e):
+            turned = psum.tile([P, PACK, P], F32, name="turned")
+            for t in range(PACK):
+                nc.tensor.matmul(turned[:, t, :], own[e][:, t, :], ident[:], start=True, stop=False, is_transpose=True)
+                nc.tensor.matmul(turned[:, t, :], gated[e][:, t, :], ident[:], start=False, stop=True, is_transpose=True)
+            nc.scalar.copy(summed[:, :, P * e : P * (e + 1)], turned[:])
+
+        def gather_state(k):
+            s, h = divmod(k, 2)
+            nc.vector.tensor_tensor(
+                piece(k), state[ORDER[s]][:].indirect(dst[:, 32 * h : 32 * (h + 1)]), wg_row[:, HALF * h : HALF * (h + 1)], MULT
+            )
+
+        def scatter(s, lo, hi, picked):
+            nc.vector.tensor_tensor(
+                windows[s % WINDOWS][:].indirect(dst[:, lo // 16 : hi // 16]), picked, summed[:, ORDER[s], lo:hi], ADD
+            )
+
+        gather_state(0)
+        for e in range(EDGE_TILES + 1):
+            if e < EDGE_TILES:
+                edge_products(e)
+            if e > 0:
+                turn_and_add(e - 1)
+            if e < 5:
+                gather_state(e + 1)
+            if e == 5:
+                scatter(0, 0, 256, picked_state[0][:, 0:256])
+            if e == 6:
+                scatter(0, 256, 512, picked_state[0][:, 256:512])
+            if e == 7:
+                gather_state(6)
+
+        y_rows = out_0.rearrange("(p t) c -> t p c", t=PACK)
+        rounded = [held("rounded%d" % c, [P, CHUNK, PACK], BF16) for c in range(T // CHUNK)]
+        y_codes = held("y_codes", [P, T], I32)
+        y_plane = held("y_plane", [P, T], U8)
+        code_rows = out_1[0].rearrange("p t i -> p (t i)").bitcast(I32)
+
+        for s in range(PACK):
+            t = ORDER[s]
+            if s == 0:
+                scatter(s, HALF, J, piece(1))
+            elif s < PACK - 1:
+                scatter(s, 0, J, picked_state[s][:])
+            else:
+                gather_state(7)
+                scatter(s, 0, HALF, piece(6))
+                scatter(s, HALF, J, piece(7))
+            win = windows[s % WINDOWS]
+            nc.sync.dma_start(out=y_rows[t], in_=win[:])
+            for c in range(T // CHUNK):
+                cols = slice(CHUNK * c, CHUNK * (c + 1))
+                if s == PACK - 1 and c < 2:
+                    nc.vector.tensor_copy(rounded[c][:, :, t], win[:, cols])
+                else:
+                    nc.scalar.copy(rounded[c][:, :, t], win[:, cols])
+        for c in range(T // CHUNK):
+            cols = slice(CHUNK * c, CHUNK * (c + 1))
+            nc.vector.quantize_mx(
+                out=y_codes[:, cols].bitcast(FP8X4), scales=y_plane[:, cols], in_=rounded[c][:].rearrange("p c i -> p (c i)")
+            )
+            nc.sync.dma_start(out=code_rows[:, cols], in_=y_codes[:, cols])
+        for q in range(4):
+            eng = nc.scalar if q % 2 else nc.sync
+            eng.dma_start(out=out_2[0].bitcast(I32)[4 * q : 4 * q + 4, :], in_=y_plane[32 * q : 32 * q + 4, :].bitcast(I32))

@@ -37,45 +37,54 @@ def tile_list_rgg_ownLP_kernel(
         ring = ctx.enter_context(tc.tile_pool(name="ring", bufs=3))
         psum = ctx.enter_context(tc.psum_pool(name="psum", bufs=2))
 
-        def held(name, shape, dtype):
-            return keep.tile(shape, dtype, name=name, align_bytes=64)
+        def held(name, shape, dtype, tag=None):
+            return keep.tile(shape, dtype, name=name, tag=tag or name, align_bytes=64)
 
-        def load_scale_rows(plane, rows):
+        def load_scale_rows(queue, plane, rows):
             for q in range(4):
-                nc.sync.dma_start(out=plane[32 * q : 32 * q + 4, :].bitcast(I32), in_=rows.bitcast(I32)[4 * q : 4 * q + 4, :])
+                queue.dma_start(out=plane[32 * q : 32 * q + 4, :].bitcast(I32), in_=rows.bitcast(I32)[4 * q : 4 * q + 4, :])
 
         src = held("src", [P, J // 16], U16)
         dst = held("dst", [P, J // 16], U16)
         tab_plane = held("tab_plane", [P, T], U8)
         tab_codes = held("tab_codes", [P, T], I32)
-        nc.vector.memset(tab_plane[:].bitcast(I32), 0)
+        nc.gpsimd.memset(tab_plane[:].bitcast(I32), 0)
         nc.sync.dma_start(dst[:], offs2)
         nc.sync.dma_start(src[:], offs)
         nc.sync.dma_start(out=tab_codes[:], in_=tab_words[0].rearrange("p t i -> p (t i)").bitcast(I32))
-        load_scale_rows(tab_plane, tab_scales[0])
+        load_scale_rows(nc.sync, tab_plane, tab_scales[0])
 
-        warm = held("warm", [P, 2], F32)
-        nc.gpsimd.memset(warm[:, 0:1], 0.0)
-        nc.scalar.activation(warm[:, 1:2], warm[:, 0:1], SIGMOID)
+        warm_in = held("warm_in", [P, 1], F32)
+        warm_out = held("warm_out", [P, 1], F32)
+        nc.vector.memset(warm_in[:], 0.0)
+        nc.scalar.activation(warm_out[:], warm_in[:], SIGMOID)
 
         ident = held("ident", [P, P], F32)
         make_identity(nc, ident[:])
+        wg_cut = held("wg_cut", [P, P], F32)
+        nc.gpsimd.memset(wg_cut[:], 0.0)
         wc_plane = held("wc_plane", [P, N], U8)
         wc_codes = held("wc_codes", [P, 2 * N], U8)
-        nc.gpsimd.memset(wc_plane[:].bitcast(I32), 0)
 
         windows = [held("window%d" % i, [P, T], F32) for i in range(WINDOWS - 1)]
         for w in windows:
             nc.vector.memset(w[:], 0.0)
+        nc.vector.memset(wc_plane[:].bitcast(I32), 0)
 
         raw = {}
-        for name, w in (("wa", wa), ("wb", wb), ("wo", wo)):
+
+        def load_weight(name, w):
             raw[name] = held("raw_" + name, [P, PACK, N], F32)
             nc.sync.dma_start(out=raw[name][:], in_=w.rearrange("(p i) n -> p i n", i=PACK))
+
+        load_weight("wa", wa)
+        load_weight("wb", wb)
+        nc.sync.dma_start(out=wg_cut[0:EDGE_TILES, :], in_=wgo[0].rearrange("(e j) -> e j", j=P))
+        nc.sync.dma_start(out=wc_codes[:].bitcast(I32), in_=wc_words[0].bitcast(I32))
+        load_scale_rows(nc.sync, wc_plane, wc_scales[0])
+        load_weight("wo", wo)
         wg_row = held("wg_row", [P, J], F32)
         nc.sync.dma_start(out=wg_row[:], in_=wgo)
-        nc.sync.dma_start(out=wc_codes[:].bitcast(I32), in_=wc_words[0].bitcast(I32))
-        load_scale_rows(wc_plane, wc_scales[0])
         r_rows = rT.rearrange("(p t) c -> t p c", t=PACK)
         state = {}
         for t in ORDER:
@@ -90,18 +99,19 @@ def tile_list_rgg_ownLP_kernel(
                 picked_plane[name] = held("plane_" + name, [P, J], U8)
                 nc.vector.tensor_copy(picked_plane[name][:], tab_plane[:].indirect(lst[:]))
 
-        def gather_codes(h):
-            for name, lst in (("dst", dst), ("src", src)):
-                picked_codes[name, h] = held("codes_%s%d" % (name, h), [P, HALF], U32)
+        def gather_codes(h, tag):
+            both = held("codes%d" % h, [P, 2, HALF], U32, tag)
+            for i, (name, lst) in enumerate((("src", src), ("dst", dst))):
+                picked_codes[name, h] = both[:, i, :]
                 nc.vector.tensor_copy(
-                    picked_codes[name, h][:], tab_codes[:].bitcast(U32).indirect(lst[:, 32 * h : 32 * (h + 1)])
+                    picked_codes[name, h], tab_codes[:].bitcast(U32).indirect(lst[:, 32 * h : 32 * (h + 1)])
                 )
 
         w_codes = {}
         w_plane = {}
 
         def quantise_weight(name):
-            grouped = keep.tile([P, N, PACK], BF16, name="grouped_" + name, tag="grouped_" + name, align_bytes=64)
+            grouped = held("grouped_" + name, [P, N, PACK], BF16)
             nc.scalar.copy(
                 grouped[:].rearrange("p (c e) i -> p c i e", e=4), raw[name][:].rearrange("p i (c e) -> p c i e", e=4)
             )
@@ -111,38 +121,35 @@ def tile_list_rgg_ownLP_kernel(
                 out=w_codes[name][:].bitcast(FP8X4), scales=w_plane[name][:], in_=grouped[:].rearrange("p n i -> p (n i)")
             )
 
-        gather_codes(0)
-        gather_codes(1)
+        gather_codes(0, None)
         gather_planes()
         quantise_weight("wa")
         quantise_weight("wb")
+        gather_codes(1, "grouped_wb")
 
         wg_col = held("wg_col", [P, EDGE_TILES], F32)
-        for b in range(EDGE_TILES // PACK):
-            turned = psum.tile([P, PACK, P], F32, name="turned")
-            for u in range(PACK):
-                e = PACK * b + u
-                nc.tensor.transpose(turned[:, u, :], wg_row[:, P * e : P * (e + 1)], ident[:])
-            nc.scalar.copy(wg_col[:, PACK * b : PACK * (b + 1)], turned[:, :, 0])
+        wg_turned = psum.tile([P, PACK, P], F32, name="turned")
+        nc.tensor.transpose(wg_turned[:, 0, :], wg_cut[:], ident[:])
+        nc.scalar.copy(wg_col[:], wg_turned[:, 0, 0:EDGE_TILES])
 
         quantise_weight("wo")
-        windows.append(keep.tile([P, T], F32, name="window_last", tag="grouped_wo", align_bytes=64))
+        windows.append(held("window_last", [P, T], F32, "grouped_wo"))
         nc.gpsimd.memset(windows[-1][:], 0.0)
 
         summed = held("summed", [P, PACK, J], F32)
-        picked_state = [held("picked_state%d" % s, [P, J], F32) for s in range(PACK - 1)]
-        spare = [held("spare%d" % i, [P, HALF], F32) for i in range(3)]
+        picked_state = [held("picked_state0", [P, J], F32, "raw_wo"), held("picked_state1", [P, J], F32)]
+        shared = held("picked_shared", [P, 3 * HALF], F32)
+        picked = [picked_state[0][:], picked_state[1][:], shared[:, HALF:], shared[:, 0:J]]
+        spare = held("spare", [P, HALF], F32)
 
         def piece(k):
             s, h = divmod(k, 2)
-            if s < PACK - 1:
-                return picked_state[s][:, HALF * h : HALF * (h + 1)]
-            return spare[0][:] if h == 0 else picked_state[PACK - 2][:, HALF:]
+            return picked[s][:, HALF * h : HALF * (h + 1)]
 
         def eta_place(e):
-            if e < 5:
-                return piece(e + 1)
-            return spare[(e - 4) % 3][:]
+            if e < 6:
+                return piece(e)
+            return spare[:] if e == 6 else piece(6)
 
         def dealt(bank):
             return bank[:].rearrange("p (m t) -> p t m", t=PACK)
@@ -190,23 +197,22 @@ def tile_list_rgg_ownLP_kernel(
                 piece(k), state[ORDER[s]][:].indirect(dst[:, 32 * h : 32 * (h + 1)]), wg_row[:, HALF * h : HALF * (h + 1)], MULT
             )
 
-        def scatter(s, lo, hi, picked):
+        def scatter(s, lo, hi):
             nc.vector.tensor_tensor(
-                windows[s % WINDOWS][:].indirect(dst[:, lo // 16 : hi // 16]), picked, summed[:, ORDER[s], lo:hi], ADD
+                windows[s % WINDOWS][:].indirect(dst[:, lo // 16 : hi // 16]), picked[s][:, lo:hi], summed[:, ORDER[s], lo:hi], ADD
             )
 
-        gather_state(0)
         for e in range(EDGE_TILES + 1):
             if e < EDGE_TILES:
                 edge_products(e)
             if e > 0:
                 turn_and_add(e - 1)
-            if e < 5:
-                gather_state(e + 1)
+            if e < 6:
+                gather_state(e)
             if e == 5:
-                scatter(0, 0, 256, picked_state[0][:, 0:256])
+                scatter(0, 0, 256)
             if e == 6:
-                scatter(0, 256, 512, picked_state[0][:, 256:512])
+                scatter(0, 256, 512)
             if e == 7:
                 gather_state(6)
 
@@ -218,14 +224,9 @@ def tile_list_rgg_ownLP_kernel(
 
         for s in range(PACK):
             t = ORDER[s]
-            if s == 0:
-                scatter(s, HALF, J, piece(1))
-            elif s < PACK - 1:
-                scatter(s, 0, J, picked_state[s][:])
-            else:
+            if s == PACK - 1:
                 gather_state(7)
-                scatter(s, 0, HALF, piece(6))
-                scatter(s, HALF, J, piece(7))
+            scatter(s, HALF if s == 0 else 0, J)
             win = windows[s % WINDOWS]
             nc.sync.dma_start(out=y_rows[t], in_=win[:])
             for c in range(T // CHUNK):

@@ -24,8 +24,8 @@ PACK = 4
 EDGE_TILES = J // P
 HALF = J // 2
 CHUNK = 512
-WINDOWS = 3
-ORDER = (0, 2, 3, 1)
+WINDOWS = 2
+ORDER = (0, 2, 1, 3)
 
 
 def tile_list_rgg_ownLP_kernel(
@@ -48,6 +48,8 @@ def tile_list_rgg_ownLP_kernel(
         dst = held("dst", [P, J // 16], U16)
         tab_plane = held("tab_plane", [P, T], U8)
         tab_codes = held("tab_codes", [P, T], I32)
+        wc_rows = held("wc_rows", [P, N], U8)
+        wc_raw = held("wc_raw", [P, 2 * N], U8)
         nc.gpsimd.memset(tab_plane[:].bitcast(I32), 0)
         nc.sync.dma_start(dst[:], offs2)
         nc.sync.dma_start(src[:], offs)
@@ -66,10 +68,10 @@ def tile_list_rgg_ownLP_kernel(
         wc_plane = held("wc_plane", [P, N], U8)
         wc_codes = held("wc_codes", [P, 2 * N], U8)
 
-        windows = [held("window%d" % i, [P, T], F32) for i in range(WINDOWS - 1)]
+        windows = [held("window%d" % i, [P, T], F32) for i in range(WINDOWS)]
         for w in windows:
             nc.vector.memset(w[:], 0.0)
-        nc.vector.memset(wc_plane[:].bitcast(I32), 0)
+        nc.vector.memset(wc_rows[:].bitcast(I32), 0)
 
         raw = {}
 
@@ -80,8 +82,8 @@ def tile_list_rgg_ownLP_kernel(
         load_weight("wa", wa)
         load_weight("wb", wb)
         nc.sync.dma_start(out=wg_cut[0:EDGE_TILES, :], in_=wgo[0].rearrange("(e j) -> e j", j=P))
-        nc.sync.dma_start(out=wc_codes[:].bitcast(I32), in_=wc_words[0].bitcast(I32))
-        load_scale_rows(nc.sync, wc_plane, wc_scales[0])
+        nc.sync.dma_start(out=wc_raw[:].bitcast(I32), in_=wc_words[0].bitcast(I32))
+        load_scale_rows(nc.sync, wc_rows, wc_scales[0])
         load_weight("wo", wo)
         wg_row = held("wg_row", [P, J], F32)
         nc.sync.dma_start(out=wg_row[:], in_=wgo)
@@ -113,7 +115,7 @@ def tile_list_rgg_ownLP_kernel(
         def quantise_weight(name):
             grouped = held("grouped_" + name, [P, N, PACK], BF16)
             nc.scalar.copy(
-                grouped[:].rearrange("p (c e) i -> p c i e", e=4), raw[name][:].rearrange("p i (c e) -> p c i e", e=4)
+                grouped[:].rearrange("p (t m) i -> p m i t", t=PACK), raw[name][:].rearrange("p i (m t) -> p m i t", t=PACK)
             )
             w_codes[name] = held("wcodes_" + name, [P, N], U32)
             w_plane[name] = held("wplane_" + name, [P, N], U8)
@@ -124,6 +126,13 @@ def tile_list_rgg_ownLP_kernel(
         gather_codes(0, None)
         gather_planes()
         quantise_weight("wa")
+        nc.vector.tensor_copy(
+            wc_codes[:].bitcast(U16).rearrange("p (t m) -> p t m", t=PACK),
+            wc_raw[:].bitcast(U16).rearrange("p (m t) -> p t m", t=PACK),
+        )
+        nc.vector.tensor_copy(
+            wc_plane[:].rearrange("p (t m) -> p t m", t=PACK), wc_rows[:].rearrange("p (m t) -> p t m", t=PACK)
+        )
         quantise_weight("wb")
         gather_codes(1, "grouped_wb")
 
@@ -133,26 +142,16 @@ def tile_list_rgg_ownLP_kernel(
         nc.scalar.copy(wg_col[:], wg_turned[:, 0, 0:EDGE_TILES])
 
         quantise_weight("wo")
-        windows.append(held("window_last", [P, T], F32, "grouped_wo"))
-        nc.gpsimd.memset(windows[-1][:], 0.0)
 
         summed = held("summed", [P, PACK, J], F32)
-        picked_state = [held("picked_state0", [P, J], F32, "raw_wo"), held("picked_state1", [P, J], F32)]
-        shared = held("picked_shared", [P, 3 * HALF], F32)
-        picked = [picked_state[0][:], picked_state[1][:], shared[:, HALF:], shared[:, 0:J]]
-        spare = held("spare", [P, HALF], F32)
-
-        def piece(k):
-            s, h = divmod(k, 2)
-            return picked[s][:, HALF * h : HALF * (h + 1)]
+        picked = [held("picked%d" % s, [P, J], F32, "raw_wo" if s == 0 else None) for s in range(PACK)]
 
         def eta_place(e):
-            if e < 6:
-                return piece(e)
-            return spare[:] if e == 6 else piece(6)
+            s, h = divmod(e, 2)
+            return picked[s][:, HALF * h : HALF * (h + 1)]
 
         def dealt(bank):
-            return bank[:].rearrange("p (m t) -> p t m", t=PACK)
+            return bank[:].rearrange("p (t m) -> p t m", t=PACK)
 
         def product(bank, side, e, codes, plane, start, stop):
             h, c = divmod(P * e, HALF)
@@ -191,10 +190,9 @@ def tile_list_rgg_ownLP_kernel(
                 nc.tensor.matmul(turned[:, t, :], gated[e][:, t, :], ident[:], start=False, stop=True, is_transpose=True)
             nc.scalar.copy(summed[:, :, P * e : P * (e + 1)], turned[:])
 
-        def gather_state(k):
-            s, h = divmod(k, 2)
+        def gather_state(s, lo, hi):
             nc.vector.tensor_tensor(
-                piece(k), state[ORDER[s]][:].indirect(dst[:, 32 * h : 32 * (h + 1)]), wg_row[:, HALF * h : HALF * (h + 1)], MULT
+                picked[s][:, lo:hi], state[ORDER[s]][:].indirect(dst[:, lo // 16 : hi // 16]), wg_row[:, lo:hi], MULT
             )
 
         def scatter(s, lo, hi):
@@ -208,15 +206,16 @@ def tile_list_rgg_ownLP_kernel(
             if e > 0:
                 turn_and_add(e - 1)
             if e < 6:
-                gather_state(e)
+                gather_state(e // 2, HALF * (e % 2), HALF * (e % 2 + 1))
+            if e == 3:
+                scatter(0, 0, 3 * P)
             if e == 5:
-                scatter(0, 0, 256)
-            if e == 6:
-                scatter(0, 256, 512)
+                scatter(0, 3 * P, 5 * P)
             if e == 7:
-                gather_state(6)
+                gather_state(PACK - 1, 0, J)
 
         y_rows = out_0.rearrange("(p t) c -> t p c", t=PACK)
+        pairs = [held("pairs%d" % h, [P, 2, T // 2, 2], BF16) for h in range(2)]
         rounded = [held("rounded%d" % c, [P, CHUNK, PACK], BF16) for c in range(T // CHUNK)]
         y_codes = held("y_codes", [P, T], I32)
         y_plane = held("y_plane", [P, T], U8)
@@ -224,17 +223,20 @@ def tile_list_rgg_ownLP_kernel(
 
         for s in range(PACK):
             t = ORDER[s]
-            if s == PACK - 1:
-                gather_state(7)
-            scatter(s, HALF if s == 0 else 0, J)
+            scatter(s, 5 * P if s == 0 else 0, J)
             win = windows[s % WINDOWS]
             nc.sync.dma_start(out=y_rows[t], in_=win[:])
-            for c in range(T // CHUNK):
-                cols = slice(CHUNK * c, CHUNK * (c + 1))
-                if s == PACK - 1 and c < 2:
-                    nc.vector.tensor_copy(rounded[c][:, :, t], win[:, cols])
-                else:
-                    nc.scalar.copy(rounded[c][:, :, t], win[:, cols])
+            for h in range(2):
+                move = nc.vector.tensor_copy if (s == PACK - 1 and h == 0) else nc.scalar.copy
+                move(pairs[h][:, t // 2, :, t % 2], win[:, T // 2 * h : T // 2 * (h + 1)])
+        for c in range(T // CHUNK):
+            h, k = divmod(c, 2)
+            move = nc.vector.tensor_copy if h == 0 else nc.scalar.copy
+            words = pairs[h][:].rearrange("p u c e -> p u (c e)").bitcast(F32)
+            move(
+                rounded[c][:].rearrange("p c i -> p (c i)").bitcast(F32).rearrange("p (c u) -> p c u", u=2),
+                words[:, :, CHUNK * k : CHUNK * (k + 1)].rearrange("p u c -> p c u"),
+            )
         for c in range(T // CHUNK):
             cols = slice(CHUNK * c, CHUNK * (c + 1))
             nc.vector.quantize_mx(

@@ -144,11 +144,10 @@ def tile_list_rgg_ownLP_kernel(
         quantise_weight("wo")
 
         summed = held("summed", [P, PACK, J], F32)
-        picked = [held("picked%d" % s, [P, J], F32, "raw_wo" if s == 0 else None) for s in range(PACK)]
+        picked = held("picked", [P, PACK * J + HALF // 2], F32, "raw_wo")
 
         def eta_place(e):
-            s, h = divmod(e, 2)
-            return picked[s][:, HALF * h : HALF * (h + 1)]
+            return picked[:, HALF * e + HALF // 2 : HALF * (e + 1) + HALF // 2]
 
         def dealt(bank):
             return bank[:].rearrange("p (t m) -> p t m", t=PACK)
@@ -179,7 +178,10 @@ def tile_list_rgg_ownLP_kernel(
             eta = eta_place(e).rearrange("p (t m) -> p t m", t=PACK)
             nc.scalar.activation(eta, dealt(za), SIGMOID)
             gated[e] = ring.tile([P, PACK, P], F32, name="gated")
-            nc.vector.scalar_tensor_tensor(gated[e][:], dealt(ms), wg_col[:, e : e + 1], eta, MULT, MULT)
+            for lo in (0, 2):
+                nc.vector.scalar_tensor_tensor(
+                    gated[e][:, lo : lo + 2, :], dealt(ms)[:, lo : lo + 2, :], wg_col[:, e : e + 1], eta[:, lo : lo + 2, :], MULT, MULT
+                )
             own[e] = ring.tile([P, PACK, P], F32, name="own")
             nc.scalar.activation(own[e][:], dealt(ow), COPY, scale=wg_col[:, e : e + 1])
 
@@ -192,12 +194,12 @@ def tile_list_rgg_ownLP_kernel(
 
         def gather_state(s, lo, hi):
             nc.vector.tensor_tensor(
-                picked[s][:, lo:hi], state[ORDER[s]][:].indirect(dst[:, lo // 16 : hi // 16]), wg_row[:, lo:hi], MULT
+                picked[:, J * s + lo : J * s + hi], state[ORDER[s]][:].indirect(dst[:, lo // 16 : hi // 16]), wg_row[:, lo:hi], MULT
             )
 
         def scatter(s, lo, hi):
             nc.vector.tensor_tensor(
-                windows[s % WINDOWS][:].indirect(dst[:, lo // 16 : hi // 16]), picked[s][:, lo:hi], summed[:, ORDER[s], lo:hi], ADD
+                windows[s % WINDOWS][:].indirect(dst[:, lo // 16 : hi // 16]), picked[:, J * s + lo : J * s + hi], summed[:, ORDER[s], lo:hi], ADD
             )
 
         for e in range(EDGE_TILES + 1):
@@ -212,37 +214,47 @@ def tile_list_rgg_ownLP_kernel(
             if e == 5:
                 scatter(0, 3 * P, 5 * P)
             if e == 7:
-                gather_state(PACK - 1, 0, J)
+                gather_state(PACK - 1, 0, HALF)
+                gather_state(PACK - 1, HALF, J)
+                scatter(0, 5 * P, 7 * P)
 
         y_rows = out_0.rearrange("(p t) c -> t p c", t=PACK)
-        pairs = [held("pairs%d" % h, [P, 2, T // 2, 2], BF16) for h in range(2)]
-        rounded = [held("rounded%d" % c, [P, CHUNK, PACK], BF16) for c in range(T // CHUNK)]
+        chunks = T // CHUNK
+        pairs = [held("pairs%d" % c, [P, 2, CHUNK, 2], BF16) for c in range(chunks // 2)]
+        rounded = [held("rounded%d" % c, [P, CHUNK, PACK], BF16) for c in range(chunks)]
         y_codes = held("y_codes", [P, T], I32)
         y_plane = held("y_plane", [P, T], U8)
         code_rows = out_1[0].rearrange("p t i -> p (t i)").bitcast(I32)
 
         for s in range(PACK):
             t = ORDER[s]
-            scatter(s, 5 * P if s == 0 else 0, J)
+            scatter(s, 7 * P if s == 0 else 0, J)
             win = windows[s % WINDOWS]
             nc.sync.dma_start(out=y_rows[t], in_=win[:])
-            for h in range(2):
-                move = nc.vector.tensor_copy if (s == PACK - 1 and h == 0) else nc.scalar.copy
-                move(pairs[h][:, t // 2, :, t % 2], win[:, T // 2 * h : T // 2 * (h + 1)])
-        for c in range(T // CHUNK):
-            h, k = divmod(c, 2)
-            move = nc.vector.tensor_copy if h == 0 else nc.scalar.copy
-            words = pairs[h][:].rearrange("p u c e -> p u (c e)").bitcast(F32)
-            move(
+            for c in range(chunks):
+                cols = slice(CHUNK * c, CHUNK * (c + 1))
+                if c < len(pairs):
+                    move = nc.vector.tensor_copy if s == PACK - 1 else nc.scalar.copy
+                    move(pairs[c][:, t // 2, :, t % 2], win[:, cols])
+                else:
+                    nc.scalar.copy(rounded[c][:, :, t], win[:, cols])
+        for c in range(len(pairs)):
+            nc.vector.tensor_copy(
                 rounded[c][:].rearrange("p c i -> p (c i)").bitcast(F32).rearrange("p (c u) -> p c u", u=2),
-                words[:, :, CHUNK * k : CHUNK * (k + 1)].rearrange("p u c -> p c u"),
+                pairs[c][:].rearrange("p u c e -> p u (c e)").bitcast(F32).rearrange("p u c -> p c u"),
             )
-        for c in range(T // CHUNK):
+
+        def store_scale_rows(lo, hi):
+            for q in range(4):
+                queue = nc.scalar if q % 2 else nc.sync
+                queue.dma_start(
+                    out=out_2[0][4 * q : 4 * q + 4, lo:hi].bitcast(I32), in_=y_plane[32 * q : 32 * q + 4, lo:hi].bitcast(I32)
+                )
+
+        for c in range(chunks):
             cols = slice(CHUNK * c, CHUNK * (c + 1))
             nc.vector.quantize_mx(
                 out=y_codes[:, cols].bitcast(FP8X4), scales=y_plane[:, cols], in_=rounded[c][:].rearrange("p c i -> p (c i)")
             )
             nc.sync.dma_start(out=code_rows[:, cols], in_=y_codes[:, cols])
-        for q in range(4):
-            eng = nc.scalar if q % 2 else nc.sync
-            eng.dma_start(out=out_2[0].bitcast(I32)[4 * q : 4 * q + 4, :], in_=y_plane[32 * q : 32 * q + 4, :].bitcast(I32))
+        store_scale_rows(0, T)

@@ -24,8 +24,8 @@ PACK = 4
 EDGE_TILES = J // P
 HALF = J // 2
 CHUNK = 512
-WINDOWS = 2
-ORDER = (0, 2, 1, 3)
+ORDER = (0, 2, 3, 1)
+PIECES = (0, 2, 4, 6, 7)
 
 
 def tile_list_rgg_ownLP_kernel(
@@ -48,13 +48,17 @@ def tile_list_rgg_ownLP_kernel(
         dst = held("dst", [P, J // 16], U16)
         tab_plane = held("tab_plane", [P, T], U8)
         tab_codes = held("tab_codes", [P, T], I32)
-        wc_rows = held("wc_rows", [P, N], U8)
-        wc_raw = held("wc_raw", [P, 2 * N], U8)
+        wc_plane = held("wc_plane", [P, N], U8)
+        wc_codes = held("wc_codes", [P, 2 * N], U8)
+        wg_cut = held("wg_cut", [P, P], F32)
         nc.gpsimd.memset(tab_plane[:].bitcast(I32), 0)
-        nc.sync.dma_start(dst[:], offs2)
+        nc.gpsimd.memset(wg_cut[:], 0.0)
+        nc.gpsimd.memset(wc_plane[:].bitcast(I32), 0)
         nc.sync.dma_start(src[:], offs)
-        nc.sync.dma_start(out=tab_codes[:], in_=tab_words[0].rearrange("p t i -> p (t i)").bitcast(I32))
+        nc.sync.dma_start(dst[:], offs2)
         load_scale_rows(nc.sync, tab_plane, tab_scales[0])
+        nc.sync.dma_start(out=wg_cut[0:EDGE_TILES, :], in_=wgo[0].rearrange("(e j) -> e j", j=P))
+        nc.sync.dma_start(out=tab_codes[:], in_=tab_words[0].rearrange("p t i -> p (t i)").bitcast(I32))
 
         warm_in = held("warm_in", [P, 1], F32)
         warm_out = held("warm_out", [P, 1], F32)
@@ -63,30 +67,20 @@ def tile_list_rgg_ownLP_kernel(
 
         ident = held("ident", [P, P], F32)
         make_identity(nc, ident[:])
-        wg_cut = held("wg_cut", [P, P], F32)
-        nc.gpsimd.memset(wg_cut[:], 0.0)
-        wc_plane = held("wc_plane", [P, N], U8)
-        wc_codes = held("wc_codes", [P, 2 * N], U8)
-
-        windows = [held("window%d" % i, [P, T], F32) for i in range(WINDOWS)]
-        for w in windows:
-            nc.vector.memset(w[:], 0.0)
-        nc.vector.memset(wc_rows[:].bitcast(I32), 0)
 
         raw = {}
 
         def load_weight(name, w):
-            raw[name] = held("raw_" + name, [P, PACK, N], F32)
-            nc.sync.dma_start(out=raw[name][:], in_=w.rearrange("(p i) n -> p i n", i=PACK))
+            rows = w.rearrange("(p i) n -> p i n", i=PACK)
+            for h in range(2):
+                raw[name, h] = held("raw_%s%d" % (name, h), [P, PACK, N // 2], F32)
+                nc.sync.dma_start(out=raw[name, h][:], in_=rows[:, :, N // 2 * h : N // 2 * (h + 1)])
 
-        load_weight("wa", wa)
         load_weight("wb", wb)
-        nc.sync.dma_start(out=wg_cut[0:EDGE_TILES, :], in_=wgo[0].rearrange("(e j) -> e j", j=P))
-        nc.sync.dma_start(out=wc_raw[:].bitcast(I32), in_=wc_words[0].bitcast(I32))
-        load_scale_rows(nc.sync, wc_rows, wc_scales[0])
+        load_weight("wa", wa)
+        nc.sync.dma_start(out=wc_codes[:].bitcast(I32), in_=wc_words[0].bitcast(I32))
+        load_scale_rows(nc.sync, wc_plane, wc_scales[0])
         load_weight("wo", wo)
-        wg_row = held("wg_row", [P, J], F32)
-        nc.sync.dma_start(out=wg_row[:], in_=wgo)
         r_rows = rT.rearrange("(p t) c -> t p c", t=PACK)
         state = {}
         for t in ORDER:
@@ -95,56 +89,55 @@ def tile_list_rgg_ownLP_kernel(
 
         picked_plane = {}
         picked_codes = {}
+        for name, lst in (("src", src), ("dst", dst)):
+            picked_plane[name] = held("plane_" + name, [P, J], U8)
+            nc.vector.tensor_copy(picked_plane[name][:], tab_plane[:].indirect(lst[:]))
 
-        def gather_planes():
-            for name, lst in (("src", src), ("dst", dst)):
-                picked_plane[name] = held("plane_" + name, [P, J], U8)
-                nc.vector.tensor_copy(picked_plane[name][:], tab_plane[:].indirect(lst[:]))
+        def gather_codes(name, lst, h, tag):
+            picked_codes[name, h] = held("codes_%s%d" % (name, h), [P, HALF], U32, tag)
+            nc.vector.tensor_copy(
+                picked_codes[name, h][:], tab_codes[:].bitcast(U32).indirect(lst[:, 32 * h : 32 * (h + 1)])
+            )
 
-        def gather_codes(h, tag):
-            both = held("codes%d" % h, [P, 2, HALF], U32, tag)
-            for i, (name, lst) in enumerate((("src", src), ("dst", dst))):
-                picked_codes[name, h] = both[:, i, :]
-                nc.vector.tensor_copy(
-                    picked_codes[name, h], tab_codes[:].bitcast(U32).indirect(lst[:, 32 * h : 32 * (h + 1)])
-                )
+        gather_codes("src", src, 0, None)
+        gather_codes("dst", dst, 0, None)
+        gather_codes("src", src, 1, None)
+
+        wg_col = held("wg_col", [P, EDGE_TILES], F32)
+        wg_turned = psum.tile([P, PACK, P], F32, name="turned")
+        nc.tensor.transpose(wg_turned[:, 0, :], wg_cut[:], ident[:])
+        nc.scalar.copy(wg_col[:], wg_turned[:, 0, 0:EDGE_TILES])
+        wg_row = held("wg_row", [P, J], F32)
+        for h in range(2):
+            spread = psum.tile([P, PACK, P], F32, name="turned")
+            for i in range(PACK):
+                e = PACK * h + i
+                nc.tensor.transpose(spread[:, i, :], wg_col[:, e : e + 1].to_broadcast([P, P]), ident[:])
+            nc.scalar.copy(wg_row[:, HALF * h : HALF * (h + 1)], spread[:].rearrange("p i j -> p (i j)"))
 
         w_codes = {}
         w_plane = {}
 
         def quantise_weight(name):
             grouped = held("grouped_" + name, [P, N, PACK], BF16)
-            nc.scalar.copy(
-                grouped[:].rearrange("p (t m) i -> p m i t", t=PACK), raw[name][:].rearrange("p i (m t) -> p m i t", t=PACK)
-            )
+            for h in range(2):
+                nc.scalar.copy(
+                    grouped[:].rearrange("p (t m) i -> p m i t", t=PACK)[:, P // 2 * h : P // 2 * (h + 1)],
+                    raw[name, h][:].rearrange("p i (m t) -> p m i t", t=PACK),
+                )
             w_codes[name] = held("wcodes_" + name, [P, N], U32)
             w_plane[name] = held("wplane_" + name, [P, N], U8)
             nc.vector.quantize_mx(
                 out=w_codes[name][:].bitcast(FP8X4), scales=w_plane[name][:], in_=grouped[:].rearrange("p n i -> p (n i)")
             )
 
-        gather_codes(0, None)
-        gather_planes()
-        quantise_weight("wa")
-        nc.vector.tensor_copy(
-            wc_codes[:].bitcast(U16).rearrange("p (t m) -> p t m", t=PACK),
-            wc_raw[:].bitcast(U16).rearrange("p (m t) -> p t m", t=PACK),
-        )
-        nc.vector.tensor_copy(
-            wc_plane[:].rearrange("p (t m) -> p t m", t=PACK), wc_rows[:].rearrange("p (m t) -> p t m", t=PACK)
-        )
         quantise_weight("wb")
-        gather_codes(1, "grouped_wb")
-
-        wg_col = held("wg_col", [P, EDGE_TILES], F32)
-        wg_turned = psum.tile([P, PACK, P], F32, name="turned")
-        nc.tensor.transpose(wg_turned[:, 0, :], wg_cut[:], ident[:])
-        nc.scalar.copy(wg_col[:], wg_turned[:, 0, 0:EDGE_TILES])
-
+        quantise_weight("wa")
+        gather_codes("dst", dst, 1, "raw_wa1")
         quantise_weight("wo")
 
         summed = held("summed", [P, PACK, J], F32)
-        picked = held("picked", [P, PACK * J + HALF // 2], F32, "raw_wo")
+        picked = held("picked", [P, HALF * EDGE_TILES + HALF // 2], F32, "raw_wo1")
 
         def eta_place(e):
             return picked[:, HALF * e + HALF // 2 : HALF * (e + 1) + HALF // 2]
@@ -180,7 +173,7 @@ def tile_list_rgg_ownLP_kernel(
             gated[e] = ring.tile([P, PACK, P], F32, name="gated")
             for lo in (0, 2):
                 nc.vector.scalar_tensor_tensor(
-                    gated[e][:, lo : lo + 2, :], dealt(ms)[:, lo : lo + 2, :], wg_col[:, e : e + 1], eta[:, lo : lo + 2, :], MULT, MULT
+                    gated[e][:, lo : lo + 2, :], ms[:].rearrange("p (m t) -> p t m", t=PACK)[:, lo : lo + 2, :], wg_col[:, e : e + 1], eta[:, lo : lo + 2, :], MULT, MULT
                 )
             own[e] = ring.tile([P, PACK, P], F32, name="own")
             nc.scalar.activation(own[e][:], dealt(ow), COPY, scale=wg_col[:, e : e + 1])
@@ -199,62 +192,77 @@ def tile_list_rgg_ownLP_kernel(
 
         def scatter(s, lo, hi):
             nc.vector.tensor_tensor(
-                windows[s % WINDOWS][:].indirect(dst[:, lo // 16 : hi // 16]), picked[:, J * s + lo : J * s + hi], summed[:, ORDER[s], lo:hi], ADD
+                windows[s % 3][:].indirect(dst[:, lo // 16 : hi // 16]), picked[:, J * s + lo : J * s + hi], summed[:, ORDER[s], lo:hi], ADD
             )
 
+        windows = {}
+
+        def clear_window(i, tag):
+            windows[i] = held("window%d" % i, [P, T], F32, tag)
+            nc.gpsimd.memset(windows[i][:], 0.0)
+
+        clear_window(0, "grouped_wo")
         for e in range(EDGE_TILES + 1):
             if e < EDGE_TILES:
                 edge_products(e)
             if e > 0:
                 turn_and_add(e - 1)
-            if e < 6:
+            if e < EDGE_TILES:
                 gather_state(e // 2, HALF * (e % 2), HALF * (e % 2 + 1))
-            if e == 3:
-                scatter(0, 0, 3 * P)
-            if e == 5:
-                scatter(0, 3 * P, 5 * P)
-            if e == 7:
-                gather_state(PACK - 1, 0, HALF)
-                gather_state(PACK - 1, HALF, J)
-                scatter(0, 5 * P, 7 * P)
+            if e in (1, 3):
+                clear_window(1 + e // 2, "state%d" % ORDER[e // 2])
+            if e in PIECES[1:]:
+                scatter(0, P * PIECES[PIECES.index(e) - 1], P * e)
 
         y_rows = out_0.rearrange("(p t) c -> t p c", t=PACK)
-        chunks = T // CHUNK
-        pairs = [held("pairs%d" % c, [P, 2, CHUNK, 2], BF16) for c in range(chunks // 2)]
-        rounded = [held("rounded%d" % c, [P, CHUNK, PACK], BF16) for c in range(chunks)]
+        rounded = [held("rounded%d" % h, [P, T // 2, PACK], BF16) for h in range(2)]
         y_codes = held("y_codes", [P, T], I32)
-        y_plane = held("y_plane", [P, T], U8)
+        y_plane = held("y_plane", [P, T // 2], U8)
         code_rows = out_1[0].rearrange("p t i -> p (t i)").bitcast(I32)
 
+        def woven(lo, hi):
+            h = lo // (T // 2)
+            return rounded[h][:, lo - T // 2 * h : hi - T // 2 * h, :]
+
+        def round_columns(move, s, lo, hi):
+            move(woven(lo, hi)[:, :, ORDER[s]], windows[s % 3][:, lo:hi])
+
         for s in range(PACK):
-            t = ORDER[s]
-            scatter(s, 7 * P if s == 0 else 0, J)
-            win = windows[s % WINDOWS]
-            nc.sync.dma_start(out=y_rows[t], in_=win[:])
-            for c in range(chunks):
-                cols = slice(CHUNK * c, CHUNK * (c + 1))
-                if c < len(pairs):
-                    move = nc.vector.tensor_copy if s == PACK - 1 else nc.scalar.copy
-                    move(pairs[c][:, t // 2, :, t % 2], win[:, cols])
-                else:
-                    nc.scalar.copy(rounded[c][:, :, t], win[:, cols])
-        for c in range(len(pairs)):
-            nc.vector.tensor_copy(
-                rounded[c][:].rearrange("p c i -> p (c i)").bitcast(F32).rearrange("p (c u) -> p c u", u=2),
-                pairs[c][:].rearrange("p u c e -> p u (c e)").bitcast(F32).rearrange("p u c -> p c u"),
-            )
+            scatter(s, P * PIECES[-1] if s == 0 else 0, J)
+            nc.sync.dma_start(out=y_rows[ORDER[s]], in_=windows[s % 3][:])
+            if s < PACK - 1:
+                for h in range(2):
+                    round_columns(nc.scalar.copy, s, T // 2 * h, T // 2 * (h + 1))
+        last = PACK - 1
+        round_columns(nc.vector.tensor_copy, last, 0, CHUNK)
+        round_columns(nc.vector.tensor_copy, last, CHUNK, 2 * CHUNK)
+        cuts = (2 * CHUNK, 3 * CHUNK, T - CHUNK // 2, T)
+        for lo, hi in zip(cuts, cuts[1:]):
+            round_columns(nc.scalar.copy, last, lo, hi)
 
-        def store_scale_rows(lo, hi):
-            for q in range(4):
-                queue = nc.scalar if q % 2 else nc.sync
-                queue.dma_start(
-                    out=out_2[0][4 * q : 4 * q + 4, lo:hi].bitcast(I32), in_=y_plane[32 * q : 32 * q + 4, lo:hi].bitcast(I32)
-                )
-
-        for c in range(chunks):
-            cols = slice(CHUNK * c, CHUNK * (c + 1))
+        def quantise_columns(lo, hi):
+            h = lo // (T // 2)
             nc.vector.quantize_mx(
-                out=y_codes[:, cols].bitcast(FP8X4), scales=y_plane[:, cols], in_=rounded[c][:].rearrange("p c i -> p (c i)")
+                out=y_codes[:, lo:hi].bitcast(FP8X4),
+                scales=y_plane[4 * h : P, lo - T // 2 * h : hi - T // 2 * h],
+                in_=woven(lo, hi).rearrange("p c i -> p (c i)"),
             )
-            nc.sync.dma_start(out=code_rows[:, cols], in_=y_codes[:, cols])
-        store_scale_rows(0, T)
+
+        def store_codes(lo, hi):
+            nc.sync.dma_start(out=code_rows[:, lo:hi], in_=y_codes[:, lo:hi])
+
+        quantise_columns(0, CHUNK)
+        quantise_columns(CHUNK, 2 * CHUNK)
+        store_codes(0, 2 * CHUNK)
+        quantise_columns(2 * CHUNK, 3 * CHUNK)
+        quantise_columns(3 * CHUNK, T - CHUNK // 2)
+        store_codes(2 * CHUNK, T - CHUNK // 2)
+        quantise_columns(T - CHUNK // 2, T)
+        store_codes(T - CHUNK // 2, T)
+        scale_rows = out_2[0].bitcast(I32)
+        for q in range(4):
+            queue = nc.scalar if q % 2 else nc.sync
+            queue.dma_start(
+                out=scale_rows[4 * q : 4 * q + 4, :].rearrange("r (h j) -> h r j", h=2),
+                in_=y_plane[32 * q : 32 * q + 8, :].bitcast(I32),
+            )

@@ -25,7 +25,7 @@ EDGE_TILES = J // P
 HALF = J // 2
 CHUNK = 512
 ORDER = (0, 2, 3, 1)
-PIECES = (0, 2, 4, 6, 7)
+PIECES = (0, 2, 4, 5, 7)
 
 
 def tile_list_rgg_ownLP_kernel(
@@ -55,9 +55,20 @@ def tile_list_rgg_ownLP_kernel(
         nc.gpsimd.memset(wg_cut[:], 0.0)
         nc.gpsimd.memset(wc_plane[:].bitcast(I32), 0)
         nc.sync.dma_start(src[:], offs)
-        nc.sync.dma_start(dst[:], offs2)
         load_scale_rows(nc.sync, tab_plane, tab_scales[0])
+        nc.sync.dma_start(dst[:], offs2)
         nc.sync.dma_start(out=wg_cut[0:EDGE_TILES, :], in_=wgo[0].rearrange("(e j) -> e j", j=P))
+        raw = {}
+
+        def load_weight(name, w, parts):
+            rows = w.rearrange("(p i) n -> p i n", i=PACK)
+            width = N // parts
+            raw[name] = []
+            for h in range(parts):
+                raw[name].append(held("raw_%s%d" % (name, h), [P, PACK, width], F32))
+                nc.sync.dma_start(out=raw[name][h][:], in_=rows[:, :, width * h : width * (h + 1)])
+
+        load_weight("wb", wb, 1)
         nc.sync.dma_start(out=tab_codes[:], in_=tab_words[0].rearrange("p t i -> p (t i)").bitcast(I32))
 
         warm_in = held("warm_in", [P, 1], F32)
@@ -68,19 +79,10 @@ def tile_list_rgg_ownLP_kernel(
         ident = held("ident", [P, P], F32)
         make_identity(nc, ident[:])
 
-        raw = {}
-
-        def load_weight(name, w):
-            rows = w.rearrange("(p i) n -> p i n", i=PACK)
-            for h in range(2):
-                raw[name, h] = held("raw_%s%d" % (name, h), [P, PACK, N // 2], F32)
-                nc.sync.dma_start(out=raw[name, h][:], in_=rows[:, :, N // 2 * h : N // 2 * (h + 1)])
-
-        load_weight("wb", wb)
-        load_weight("wa", wa)
+        load_weight("wa", wa, 2)
         nc.sync.dma_start(out=wc_codes[:].bitcast(I32), in_=wc_words[0].bitcast(I32))
         load_scale_rows(nc.sync, wc_plane, wc_scales[0])
-        load_weight("wo", wo)
+        load_weight("wo", wo, 2)
         r_rows = rT.rearrange("(p t) c -> t p c", t=PACK)
         state = {}
         for t in ORDER:
@@ -107,6 +109,9 @@ def tile_list_rgg_ownLP_kernel(
         wg_turned = psum.tile([P, PACK, P], F32, name="turned")
         nc.tensor.transpose(wg_turned[:, 0, :], wg_cut[:], ident[:])
         nc.scalar.copy(wg_col[:], wg_turned[:, 0, 0:EDGE_TILES])
+        picked = held("picked", [P, PACK * J], F32)
+        wg_own = picked[:].rearrange("p (e c) -> p e c", c=HALF)[:, :, 0]
+        nc.scalar.copy(wg_own, wg_turned[:, 0, 0:EDGE_TILES])
         wg_row = held("wg_row", [P, J], F32)
         for h in range(2):
             spread = psum.tile([P, PACK, P], F32, name="turned")
@@ -120,10 +125,11 @@ def tile_list_rgg_ownLP_kernel(
 
         def quantise_weight(name):
             grouped = held("grouped_" + name, [P, N, PACK], BF16)
-            for h in range(2):
+            share = P // len(raw[name])
+            for h, part in enumerate(raw[name]):
                 nc.scalar.copy(
-                    grouped[:].rearrange("p (t m) i -> p m i t", t=PACK)[:, P // 2 * h : P // 2 * (h + 1)],
-                    raw[name, h][:].rearrange("p i (m t) -> p m i t", t=PACK),
+                    grouped[:].rearrange("p (t m) i -> p m i t", t=PACK)[:, share * h : share * (h + 1)],
+                    part[:].rearrange("p i (m t) -> p m i t", t=PACK),
                 )
             w_codes[name] = held("wcodes_" + name, [P, N], U32)
             w_plane[name] = held("wplane_" + name, [P, N], U8)
@@ -137,10 +143,7 @@ def tile_list_rgg_ownLP_kernel(
         quantise_weight("wo")
 
         summed = held("summed", [P, PACK, J], F32)
-        picked = held("picked", [P, HALF * EDGE_TILES + HALF // 2], F32, "raw_wo1")
-
-        def eta_place(e):
-            return picked[:, HALF * e + HALF // 2 : HALF * (e + 1) + HALF // 2]
+        gates = held("gates", [P, EDGE_TILES, PACK, P], F32, "raw_wo1")
 
         def dealt(bank):
             return bank[:].rearrange("p (t m) -> p t m", t=PACK)
@@ -168,15 +171,14 @@ def tile_list_rgg_ownLP_kernel(
             product(za, "src", e, w_codes["wb"][:].bitcast(FP8X4), w_plane["wb"][:], True, False)
             product(za, "dst", e, w_codes["wa"][:].bitcast(FP8X4), w_plane["wa"][:], False, True)
             product(ow, "dst", e, w_codes["wo"][:].bitcast(FP8X4), w_plane["wo"][:], True, True)
-            eta = eta_place(e).rearrange("p (t m) -> p t m", t=PACK)
+            eta = gates[:, e]
             nc.scalar.activation(eta, dealt(za), SIGMOID)
             gated[e] = ring.tile([P, PACK, P], F32, name="gated")
-            for lo in (0, 2):
-                nc.vector.scalar_tensor_tensor(
-                    gated[e][:, lo : lo + 2, :], ms[:].rearrange("p (m t) -> p t m", t=PACK)[:, lo : lo + 2, :], wg_col[:, e : e + 1], eta[:, lo : lo + 2, :], MULT, MULT
-                )
+            nc.vector.scalar_tensor_tensor(
+                gated[e][:], ms[:].rearrange("p (m t) -> p t m", t=PACK), wg_col[:, e : e + 1], eta, MULT, MULT
+            )
             own[e] = ring.tile([P, PACK, P], F32, name="own")
-            nc.scalar.activation(own[e][:], dealt(ow), COPY, scale=wg_col[:, e : e + 1])
+            nc.scalar.activation(own[e][:], dealt(ow), COPY, scale=wg_own[:, e : e + 1])
 
         def turn_and_add(e):
             turned = psum.tile([P, PACK, P], F32, name="turned")
@@ -227,15 +229,25 @@ def tile_list_rgg_ownLP_kernel(
         def round_columns(move, s, lo, hi):
             move(woven(lo, hi)[:, :, ORDER[s]], windows[s % 3][:, lo:hi])
 
+        pairs = held("pairs", [P, 2, CHUNK, 2], BF16)
+
+        def round_pairs(move, s):
+            move(pairs[:, ORDER[s] // 2, :, ORDER[s] % 2], windows[s % 3][:, 0:CHUNK])
+
         for s in range(PACK):
             scatter(s, P * PIECES[-1] if s == 0 else 0, J)
             nc.sync.dma_start(out=y_rows[ORDER[s]], in_=windows[s % 3][:])
             if s < PACK - 1:
-                for h in range(2):
-                    round_columns(nc.scalar.copy, s, T // 2 * h, T // 2 * (h + 1))
+                round_pairs(nc.scalar.copy, s)
+                round_columns(nc.scalar.copy, s, CHUNK, T // 2)
+                round_columns(nc.scalar.copy, s, T // 2, T)
         last = PACK - 1
-        round_columns(nc.vector.tensor_copy, last, 0, CHUNK)
+        round_pairs(nc.vector.tensor_copy, last)
         round_columns(nc.vector.tensor_copy, last, CHUNK, 2 * CHUNK)
+        nc.vector.tensor_copy(
+            woven(0, CHUNK).rearrange("p c i -> p (c i)").bitcast(F32).rearrange("p (c u) -> p c u", u=2),
+            pairs[:].rearrange("p u c e -> p u (c e)").bitcast(F32).rearrange("p u c -> p c u"),
+        )
         cuts = (2 * CHUNK, 3 * CHUNK, T - CHUNK // 2, T)
         for lo, hi in zip(cuts, cuts[1:]):
             round_columns(nc.scalar.copy, last, lo, hi)

@@ -25,7 +25,8 @@ EDGE_TILES = J // P
 HALF = J // 2
 CHUNK = 512
 ORDER = (0, 2, 3, 1)
-PIECES = (0, 2, 4, 5, 7)
+ON_VECTOR = 4
+PAIR = 2 * P
 
 
 def tile_list_rgg_ownLP_kernel(
@@ -78,6 +79,9 @@ def tile_list_rgg_ownLP_kernel(
 
         ident = held("ident", [P, P], F32)
         make_identity(nc, ident[:])
+        windows = [held("window%d" % i, [P, T], F32) for i in range(3)]
+        for window in windows:
+            nc.gpsimd.memset(window[:], 0.0)
 
         load_weight("wa", wa, 2)
         nc.sync.dma_start(out=wc_codes[:].bitcast(I32), in_=wc_words[0].bitcast(I32))
@@ -109,9 +113,13 @@ def tile_list_rgg_ownLP_kernel(
         wg_turned = psum.tile([P, PACK, P], F32, name="turned")
         nc.tensor.transpose(wg_turned[:, 0, :], wg_cut[:], ident[:])
         nc.scalar.copy(wg_col[:], wg_turned[:, 0, 0:EDGE_TILES])
-        picked = held("picked", [P, PACK * J], F32)
-        wg_own = picked[:].rearrange("p (e c) -> p e c", c=HALF)[:, :, 0]
-        nc.scalar.copy(wg_own, wg_turned[:, 0, 0:EDGE_TILES])
+        picked_all = held("picked", [P, 3, J], F32)
+        wg_own = picked_all[:].rearrange("p s (h c) -> p (s h) c", h=2)[:, 0:ON_VECTOR, 0]
+        nc.scalar.copy(wg_own, wg_turned[:, 0, 0:ON_VECTOR])
+
+        def picked(s, lo, hi):
+            return picked_all[:, s % 3, lo:hi]
+
         wg_row = held("wg_row", [P, J], F32)
         for h in range(2):
             spread = psum.tile([P, PACK, P], F32, name="turned")
@@ -162,6 +170,10 @@ def tile_list_rgg_ownLP_kernel(
 
         gated = {}
         own = {}
+        late = {}
+
+        def by_tile(part):
+            return part.rearrange("p (t m) -> p t m", t=PACK)
 
         def edge_products(e):
             ms = psum.tile([P, N], F32, name="ms")
@@ -173,12 +185,21 @@ def tile_list_rgg_ownLP_kernel(
             product(ow, "dst", e, w_codes["wo"][:].bitcast(FP8X4), w_plane["wo"][:], True, True)
             eta = gates[:, e]
             nc.scalar.activation(eta, dealt(za), SIGMOID)
-            gated[e] = ring.tile([P, PACK, P], F32, name="gated")
-            nc.vector.scalar_tensor_tensor(
-                gated[e][:], ms[:].rearrange("p (m t) -> p t m", t=PACK), wg_col[:, e : e + 1], eta, MULT, MULT
-            )
-            own[e] = ring.tile([P, PACK, P], F32, name="own")
-            nc.scalar.activation(own[e][:], dealt(ow), COPY, scale=wg_own[:, e : e + 1])
+            ms_dealt = ms[:].rearrange("p (m t) -> p t m", t=PACK)
+            if e < ON_VECTOR:
+                gated[e] = ring.tile([P, PACK, P], F32, name="gated")[:]
+                nc.vector.scalar_tensor_tensor(gated[e], ms_dealt, wg_col[:, e : e + 1], eta, MULT, MULT)
+            else:
+                if e == EDGE_TILES - 1:
+                    message = by_tile(picked(2, 0, HALF))
+                else:
+                    message = ring.tile([P, PACK, P], F32, name="message")[:]
+                nc.scalar.activation(message, ms_dealt, COPY, scale=wg_col[:, e : e + 1])
+                gated[e] = by_tile(late["all"][:, N * (e - ON_VECTOR) : N * (e - ON_VECTOR + 1)])
+                nc.gpsimd.tensor_tensor(gated[e], message, eta, MULT)
+            own[e] = ring.tile([P, PACK, P], F32, name="own")[:]
+            weight = wg_own if e < ON_VECTOR else wg_col
+            nc.scalar.activation(own[e], dealt(ow), COPY, scale=weight[:, e : e + 1])
 
         def turn_and_add(e):
             turned = psum.tile([P, PACK, P], F32, name="turned")
@@ -187,34 +208,34 @@ def tile_list_rgg_ownLP_kernel(
                 nc.tensor.matmul(turned[:, t, :], gated[e][:, t, :], ident[:], start=False, stop=True, is_transpose=True)
             nc.scalar.copy(summed[:, :, P * e : P * (e + 1)], turned[:])
 
+        def listed(tile, lo, hi):
+            return tile[:].indirect(dst[:, lo // 16 : hi // 16])
+
         def gather_state(s, lo, hi):
-            nc.vector.tensor_tensor(
-                picked[:, J * s + lo : J * s + hi], state[ORDER[s]][:].indirect(dst[:, lo // 16 : hi // 16]), wg_row[:, lo:hi], MULT
-            )
+            nc.vector.tensor_tensor(picked(s, lo, hi), listed(state[ORDER[s]], lo, hi), wg_row[:, lo:hi], MULT)
 
         def scatter(s, lo, hi):
-            nc.vector.tensor_tensor(
-                windows[s % 3][:].indirect(dst[:, lo // 16 : hi // 16]), picked[:, J * s + lo : J * s + hi], summed[:, ORDER[s], lo:hi], ADD
-            )
+            nc.vector.tensor_tensor(listed(windows[s % 3], lo, hi), picked(s, lo, hi), summed[:, ORDER[s], lo:hi], ADD)
 
-        windows = {}
+        def add_and_scatter(s, lo, hi):
+            start = N * (EDGE_TILES - ON_VECTOR) + (J - PAIR) * s
+            total = late["all"][:, start + lo : start + hi]
+            nc.gpsimd.tensor_tensor(total, picked(s, lo, hi), summed[:, ORDER[s], lo:hi], ADD)
+            nc.vector.tensor_copy(listed(windows[s % 3], lo, hi), total)
 
-        def clear_window(i, tag):
-            windows[i] = held("window%d" % i, [P, T], F32, tag)
-            nc.gpsimd.memset(windows[i][:], 0.0)
-
-        clear_window(0, "grouped_wo")
         for e in range(EDGE_TILES + 1):
             if e < EDGE_TILES:
                 edge_products(e)
             if e > 0:
                 turn_and_add(e - 1)
-            if e < EDGE_TILES:
+            if e < ON_VECTOR:
                 gather_state(e // 2, HALF * (e % 2), HALF * (e % 2 + 1))
-            if e in (1, 3):
-                clear_window(1 + e // 2, "state%d" % ORDER[e // 2])
-            if e in PIECES[1:]:
-                scatter(0, P * PIECES[PIECES.index(e) - 1], P * e)
+            if e == ON_VECTOR - 1:
+                late["all"] = held("late", [P, N * (EDGE_TILES - ON_VECTOR) + 2 * (J - PAIR)], F32, "state%d" % ORDER[1])
+            if e in (3, 5, 6):
+                for s in range(2):
+                    add_and_scatter(s, PAIR * ((e - 2) // 2), PAIR * (e // 2 if e % 2 == 0 else (e - 2) // 2 + 1))
+        gather_state(2, 0, J)
 
         y_rows = out_0.rearrange("(p t) c -> t p c", t=PACK)
         rounded = [held("rounded%d" % h, [P, T // 2, PACK], BF16) for h in range(2)]
@@ -229,25 +250,30 @@ def tile_list_rgg_ownLP_kernel(
         def round_columns(move, s, lo, hi):
             move(woven(lo, hi)[:, :, ORDER[s]], windows[s % 3][:, lo:hi])
 
-        pairs = held("pairs", [P, 2, CHUNK, 2], BF16)
+        pairs = held("pairs", [P, 2, T // 2, 2], BF16)
 
-        def round_pairs(move, s):
-            move(pairs[:, ORDER[s] // 2, :, ORDER[s] % 2], windows[s % 3][:, 0:CHUNK])
+        def round_pairs(move, s, lo, hi):
+            move(pairs[:, ORDER[s] // 2, lo:hi, ORDER[s] % 2], windows[s % 3][:, lo:hi])
+
+        def weave(lo, hi):
+            nc.vector.tensor_copy(
+                woven(lo, hi).rearrange("p c i -> p (c i)").bitcast(F32).rearrange("p (c u) -> p c u", u=2),
+                pairs[:].rearrange("p u c e -> p u (c e)").bitcast(F32).rearrange("p u c -> p c u")[:, lo:hi],
+            )
 
         for s in range(PACK):
-            scatter(s, P * PIECES[-1] if s == 0 else 0, J)
+            scatter(s, J - PAIR if s < 2 else 0, J)
+            if s == 1:
+                gather_state(3, 0, J)
             nc.sync.dma_start(out=y_rows[ORDER[s]], in_=windows[s % 3][:])
             if s < PACK - 1:
-                round_pairs(nc.scalar.copy, s)
-                round_columns(nc.scalar.copy, s, CHUNK, T // 2)
+                round_pairs(nc.scalar.copy, s, 0, T // 2)
                 round_columns(nc.scalar.copy, s, T // 2, T)
         last = PACK - 1
-        round_pairs(nc.vector.tensor_copy, last)
-        round_columns(nc.vector.tensor_copy, last, CHUNK, 2 * CHUNK)
-        nc.vector.tensor_copy(
-            woven(0, CHUNK).rearrange("p c i -> p (c i)").bitcast(F32).rearrange("p (c u) -> p c u", u=2),
-            pairs[:].rearrange("p u c e -> p u (c e)").bitcast(F32).rearrange("p u c -> p c u"),
-        )
+        round_pairs(nc.vector.tensor_copy, last, 0, CHUNK)
+        round_pairs(nc.vector.tensor_copy, last, CHUNK, 2 * CHUNK)
+        weave(0, CHUNK)
+        weave(CHUNK, 2 * CHUNK)
         cuts = (2 * CHUNK, 3 * CHUNK, T - CHUNK // 2, T)
         for lo, hi in zip(cuts, cuts[1:]):
             round_columns(nc.scalar.copy, last, lo, hi)

@@ -27,6 +27,8 @@ CHUNK = 512
 ORDER = (0, 2, 3, 1)
 ON_VECTOR = 4
 PAIR = 2 * P
+PAIRED = 768
+PARK_STEP = 704
 
 
 def tile_list_rgg_ownLP_kernel(
@@ -113,12 +115,13 @@ def tile_list_rgg_ownLP_kernel(
         wg_turned = psum.tile([P, PACK, P], F32, name="turned")
         nc.tensor.transpose(wg_turned[:, 0, :], wg_cut[:], ident[:])
         nc.scalar.copy(wg_col[:], wg_turned[:, 0, 0:EDGE_TILES])
-        picked_all = held("picked", [P, 3, J], F32)
-        wg_own = picked_all[:].rearrange("p s (h c) -> p (s h) c", h=2)[:, 0:ON_VECTOR, 0]
+        picked_all = held("picked", [P, 3 * J + PAIR], F32)
+        wg_own = picked_all[:, 0 : ON_VECTOR * PARK_STEP : PARK_STEP]
         nc.scalar.copy(wg_own, wg_turned[:, 0, 0:ON_VECTOR])
 
         def picked(s, lo, hi):
-            return picked_all[:, s % 3, lo:hi]
+            start = (0, J, 2 * J + PAIR, 0)[s]
+            return picked_all[:, start + lo : start + hi]
 
         wg_row = held("wg_row", [P, J], F32)
         for h in range(2):
@@ -171,6 +174,7 @@ def tile_list_rgg_ownLP_kernel(
         gated = {}
         own = {}
         late = {}
+        messages = held("messages", [P, 3, N], F32)
 
         def by_tile(part):
             return part.rearrange("p (t m) -> p t m", t=PACK)
@@ -193,7 +197,7 @@ def tile_list_rgg_ownLP_kernel(
                 if e == EDGE_TILES - 1:
                     message = by_tile(picked(2, 0, HALF))
                 else:
-                    message = ring.tile([P, PACK, P], F32, name="message")[:]
+                    message = by_tile(messages[:, e - ON_VECTOR, :])
                 nc.scalar.activation(message, ms_dealt, COPY, scale=wg_col[:, e : e + 1])
                 gated[e] = by_tile(late["all"][:, N * (e - ON_VECTOR) : N * (e - ON_VECTOR + 1)])
                 nc.gpsimd.tensor_tensor(gated[e], message, eta, MULT)
@@ -218,8 +222,13 @@ def tile_list_rgg_ownLP_kernel(
             nc.vector.tensor_tensor(listed(windows[s % 3], lo, hi), picked(s, lo, hi), summed[:, ORDER[s], lo:hi], ADD)
 
         def add_and_scatter(s, lo, hi):
-            start = N * (EDGE_TILES - ON_VECTOR) + (J - PAIR) * s
-            total = late["all"][:, start + lo : start + hi]
+            if s == 0:
+                start = N * (EDGE_TILES - ON_VECTOR)
+                total = late["all"][:, start + lo : start + hi]
+            elif lo == 0:
+                total = picked_all[:, 2 * J : 2 * J + PAIR]
+            else:
+                total = messages[:, lo // PAIR, 0:PAIR]
             nc.gpsimd.tensor_tensor(total, picked(s, lo, hi), summed[:, ORDER[s], lo:hi], ADD)
             nc.vector.tensor_copy(listed(windows[s % 3], lo, hi), total)
 
@@ -228,13 +237,18 @@ def tile_list_rgg_ownLP_kernel(
                 edge_products(e)
             if e > 0:
                 turn_and_add(e - 1)
-            if e < ON_VECTOR:
-                gather_state(e // 2, HALF * (e % 2), HALF * (e % 2 + 1))
-            if e == ON_VECTOR - 1:
-                late["all"] = held("late", [P, N * (EDGE_TILES - ON_VECTOR) + 2 * (J - PAIR)], F32, "state%d" % ORDER[1])
-            if e in (3, 5, 6):
-                for s in range(2):
-                    add_and_scatter(s, PAIR * ((e - 2) // 2), PAIR * (e // 2 if e % 2 == 0 else (e - 2) // 2 + 1))
+            if e < 2:
+                gather_state(0, HALF * e, HALF * (e + 1))
+            if e == 2:
+                gather_state(1, 0, J)
+                late["all"] = held("late", [P, N * (EDGE_TILES - ON_VECTOR) + J - PAIR], F32, "state%d" % ORDER[1])
+            if e == 3:
+                add_and_scatter(0, 0, PAIR)
+                add_and_scatter(1, 0, PAIR)
+            if e in (4, 6):
+                add_and_scatter(0, P * e - PAIR, P * e)
+            if e in (5, 6):
+                add_and_scatter(1, PAIR * (e - 4), PAIR * (e - 3))
         gather_state(2, 0, J)
 
         y_rows = out_0.rearrange("(p t) c -> t p c", t=PACK)
@@ -250,7 +264,7 @@ def tile_list_rgg_ownLP_kernel(
         def round_columns(move, s, lo, hi):
             move(woven(lo, hi)[:, :, ORDER[s]], windows[s % 3][:, lo:hi])
 
-        pairs = held("pairs", [P, 2, T // 2, 2], BF16)
+        pairs = held("pairs", [P, 2, PAIRED, 2], BF16)
 
         def round_pairs(move, s, lo, hi):
             move(pairs[:, ORDER[s] // 2, lo:hi, ORDER[s] % 2], windows[s % 3][:, lo:hi])
@@ -267,13 +281,14 @@ def tile_list_rgg_ownLP_kernel(
                 gather_state(3, 0, J)
             nc.sync.dma_start(out=y_rows[ORDER[s]], in_=windows[s % 3][:])
             if s < PACK - 1:
-                round_pairs(nc.scalar.copy, s, 0, T // 2)
+                round_pairs(nc.scalar.copy, s, 0, PAIRED)
+                round_columns(nc.scalar.copy, s, PAIRED, T // 2)
                 round_columns(nc.scalar.copy, s, T // 2, T)
         last = PACK - 1
-        round_pairs(nc.vector.tensor_copy, last, 0, CHUNK)
-        round_pairs(nc.vector.tensor_copy, last, CHUNK, 2 * CHUNK)
+        round_pairs(nc.vector.tensor_copy, last, 0, PAIRED)
+        round_columns(nc.vector.tensor_copy, last, PAIRED, T // 2)
         weave(0, CHUNK)
-        weave(CHUNK, 2 * CHUNK)
+        weave(CHUNK, PAIRED)
         cuts = (2 * CHUNK, 3 * CHUNK, T - CHUNK // 2, T)
         for lo, hi in zip(cuts, cuts[1:]):
             round_columns(nc.scalar.copy, last, lo, hi)

@@ -51,12 +51,12 @@ def tile_list_rgg_ownLP_kernel(
         dst = held("dst", [P, J // 16], U16)
         tab_plane = held("tab_plane", [P, T], U8)
         tab_codes = held("tab_codes", [P, T], I32)
-        wc_plane = held("wc_plane", [P, N], U8)
-        wc_codes = held("wc_codes", [P, 2 * N], U8)
+        wc_rows = held("wc_rows", [P, N], U8)
+        wc_raw = held("wc_raw", [P, 2 * N], U8)
         wg_cut = held("wg_cut", [P, P], F32)
         nc.gpsimd.memset(tab_plane[:].bitcast(I32), 0)
         nc.gpsimd.memset(wg_cut[:], 0.0)
-        nc.gpsimd.memset(wc_plane[:].bitcast(I32), 0)
+        nc.gpsimd.memset(wc_rows[:].bitcast(I32), 0)
         nc.sync.dma_start(src[:], offs)
         load_scale_rows(nc.sync, tab_plane, tab_scales[0])
         nc.sync.dma_start(dst[:], offs2)
@@ -86,8 +86,8 @@ def tile_list_rgg_ownLP_kernel(
             nc.gpsimd.memset(window[:], 0.0)
 
         load_weight("wa", wa, 2)
-        nc.sync.dma_start(out=wc_codes[:].bitcast(I32), in_=wc_words[0].bitcast(I32))
-        load_scale_rows(nc.sync, wc_plane, wc_scales[0])
+        nc.sync.dma_start(out=wc_raw[:].bitcast(I32), in_=wc_words[0].bitcast(I32))
+        load_scale_rows(nc.sync, wc_rows, wc_scales[0])
         load_weight("wo", wo, 2)
         r_rows = rT.rearrange("(p t) c -> t p c", t=PACK)
         state = {}
@@ -151,6 +151,15 @@ def tile_list_rgg_ownLP_kernel(
         quantise_weight("wb")
         quantise_weight("wa")
         gather_codes("dst", dst, 1, "raw_wa1")
+        wc_plane = held("wc_plane", [P, N], U8)
+        wc_codes = held("wc_codes", [P, 2 * N], U8)
+        nc.vector.tensor_copy(
+            wc_codes[:].bitcast(U16).rearrange("p (t m) -> p t m", t=PACK),
+            wc_raw[:].bitcast(U16).rearrange("p (m t) -> p t m", t=PACK),
+        )
+        nc.vector.tensor_copy(
+            wc_plane[:].rearrange("p (t m) -> p t m", t=PACK), wc_rows[:].rearrange("p (m t) -> p t m", t=PACK)
+        )
         quantise_weight("wo")
 
         summed = held("summed", [P, PACK, J], F32)
@@ -189,7 +198,7 @@ def tile_list_rgg_ownLP_kernel(
             product(ow, "dst", e, w_codes["wo"][:].bitcast(FP8X4), w_plane["wo"][:], True, True)
             eta = gates[:, e]
             nc.scalar.activation(eta, dealt(za), SIGMOID)
-            ms_dealt = ms[:].rearrange("p (m t) -> p t m", t=PACK)
+            ms_dealt = dealt(ms)
             if e < ON_VECTOR:
                 gated[e] = ring.tile([P, PACK, P], F32, name="gated")[:]
                 nc.vector.scalar_tensor_tensor(gated[e], ms_dealt, wg_col[:, e : e + 1], eta, MULT, MULT)

@@ -25,10 +25,8 @@ EDGE_TILES = J // P
 HALF = J // 2
 CHUNK = 512
 ORDER = (0, 2, 3, 1)
-ON_VECTOR = 4
-PAIR = 2 * P
-PAIRED = 768
-PARK_STEP = 704
+SPARE = 2 * P
+PAIRED = 1280
 
 
 def tile_list_rgg_ownLP_kernel(
@@ -37,7 +35,6 @@ def tile_list_rgg_ownLP_kernel(
     nc = tc.nc
     with ExitStack() as ctx:
         keep = ctx.enter_context(tc.tile_pool(name="keep", bufs=1))
-        ring = ctx.enter_context(tc.tile_pool(name="ring", bufs=3))
         psum = ctx.enter_context(tc.psum_pool(name="psum", bufs=2))
 
         def held(name, shape, dtype, tag=None):
@@ -101,28 +98,20 @@ def tile_list_rgg_ownLP_kernel(
             picked_plane[name] = held("plane_" + name, [P, J], U8)
             nc.vector.tensor_copy(picked_plane[name][:], tab_plane[:].indirect(lst[:]))
 
-        def gather_codes(name, lst, h, tag):
+        def gather_codes(name, lst, h, tag=None):
             picked_codes[name, h] = held("codes_%s%d" % (name, h), [P, HALF], U32, tag)
             nc.vector.tensor_copy(
                 picked_codes[name, h][:], tab_codes[:].bitcast(U32).indirect(lst[:, 32 * h : 32 * (h + 1)])
             )
 
-        gather_codes("src", src, 0, None)
-        gather_codes("dst", dst, 0, None)
-        gather_codes("src", src, 1, None)
+        gather_codes("src", src, 0)
+        gather_codes("dst", dst, 0)
+        gather_codes("src", src, 1)
 
         wg_col = held("wg_col", [P, EDGE_TILES], F32)
         wg_turned = psum.tile([P, PACK, P], F32, name="turned")
         nc.tensor.transpose(wg_turned[:, 0, :], wg_cut[:], ident[:])
         nc.scalar.copy(wg_col[:], wg_turned[:, 0, 0:EDGE_TILES])
-        picked_all = held("picked", [P, 3 * J + PAIR], F32)
-        wg_own = picked_all[:, 0 : ON_VECTOR * PARK_STEP : PARK_STEP]
-        nc.scalar.copy(wg_own, wg_turned[:, 0, 0:ON_VECTOR])
-
-        def picked(s, lo, hi):
-            start = (0, J, 2 * J + PAIR, 0)[s]
-            return picked_all[:, start + lo : start + hi]
-
         wg_row = held("wg_row", [P, J], F32)
         for h in range(2):
             spread = psum.tile([P, PACK, P], F32, name="turned")
@@ -151,154 +140,222 @@ def tile_list_rgg_ownLP_kernel(
         quantise_weight("wb")
         quantise_weight("wa")
         gather_codes("dst", dst, 1, "raw_wa1")
-        wc_plane = held("wc_plane", [P, N], U8)
+        w_plane["wc"] = held("wc_plane", [P, N], U8)
         wc_codes = held("wc_codes", [P, 2 * N], U8)
         nc.vector.tensor_copy(
             wc_codes[:].bitcast(U16).rearrange("p (t m) -> p t m", t=PACK),
             wc_raw[:].bitcast(U16).rearrange("p (m t) -> p t m", t=PACK),
         )
         nc.vector.tensor_copy(
-            wc_plane[:].rearrange("p (t m) -> p t m", t=PACK), wc_rows[:].rearrange("p (m t) -> p t m", t=PACK)
+            w_plane["wc"][:].rearrange("p (t m) -> p t m", t=PACK), wc_rows[:].rearrange("p (m t) -> p t m", t=PACK)
         )
         quantise_weight("wo")
 
-        summed = held("summed", [P, PACK, J], F32)
-        gates = held("gates", [P, EDGE_TILES, PACK, P], F32, "raw_wo1")
-
-        def dealt(bank):
-            return bank[:].rearrange("p (t m) -> p t m", t=PACK)
-
-        def product(bank, side, e, codes, plane, start, stop):
-            h, c = divmod(P * e, HALF)
+        def product(out, side, e, name, t, start, stop):
+            if name == "wc":
+                codes = wc_codes[:, 2 * P * t : 2 * P * (t + 1)].bitcast(FP4X4)
+            else:
+                codes = w_codes[name][:, P * t : P * (t + 1)].bitcast(FP8X4)
             nc.tensor.matmul_mx(
-                out=bank[:],
-                lhsT=picked_codes[side, h][:, c : c + P].bitcast(FP8X4),
+                out=out,
+                lhsT=picked_codes[side, e // PACK][:, tile_cols(e % PACK)].bitcast(FP8X4),
                 lhsT_scale=picked_plane[side][:, P * e : P * (e + 1)],
                 rhs=codes,
-                rhs_scale=plane,
+                rhs_scale=w_plane[name][:, P * t : P * (t + 1)],
                 start=start,
                 stop=stop,
             )
 
-        gated = {}
-        own = {}
-        late = {}
-        messages = held("messages", [P, 3, N], F32)
+        eta, message, own, gated, sums, totals, picked = {}, {}, {}, {}, {}, {}, {}
 
-        def by_tile(part):
-            return part.rearrange("p (t m) -> p t m", t=PACK)
+        def tile_cols(i):
+            return slice(P * i, P * (i + 1))
 
-        def edge_products(e):
-            ms = psum.tile([P, N], F32, name="ms")
-            za = psum.tile([P, N], F32, name="za")
-            ow = psum.tile([P, N], F32, name="ow")
-            product(ms, "src", e, wc_codes[:].bitcast(FP4X4), wc_plane[:], True, True)
-            product(za, "src", e, w_codes["wb"][:].bitcast(FP8X4), w_plane["wb"][:], True, False)
-            product(za, "dst", e, w_codes["wa"][:].bitcast(FP8X4), w_plane["wa"][:], False, True)
-            product(ow, "dst", e, w_codes["wo"][:].bitcast(FP8X4), w_plane["wo"][:], True, True)
-            eta = gates[:, e]
-            nc.scalar.activation(eta, dealt(za), SIGMOID)
-            ms_dealt = dealt(ms)
-            if e < ON_VECTOR:
-                gated[e] = ring.tile([P, PACK, P], F32, name="gated")[:]
-                nc.vector.scalar_tensor_tensor(gated[e], ms_dealt, wg_col[:, e : e + 1], eta, MULT, MULT)
-            else:
-                if e == EDGE_TILES - 1:
-                    message = by_tile(picked(2, 0, HALF))
-                else:
-                    message = by_tile(messages[:, e - ON_VECTOR, :])
-                nc.scalar.activation(message, ms_dealt, COPY, scale=wg_col[:, e : e + 1])
-                gated[e] = by_tile(late["all"][:, N * (e - ON_VECTOR) : N * (e - ON_VECTOR + 1)])
-                nc.gpsimd.tensor_tensor(gated[e], message, eta, MULT)
-            own[e] = ring.tile([P, PACK, P], F32, name="own")[:]
-            weight = wg_own if e < ON_VECTOR else wg_col
-            nc.scalar.activation(own[e], dealt(ow), COPY, scale=weight[:, e : e + 1])
+        def half_cols(h):
+            return slice(HALF * h, HALF * (h + 1))
 
-        def turn_and_add(e):
-            turned = psum.tile([P, PACK, P], F32, name="turned")
-            for t in range(PACK):
-                nc.tensor.matmul(turned[:, t, :], own[e][:, t, :], ident[:], start=True, stop=False, is_transpose=True)
-                nc.tensor.matmul(turned[:, t, :], gated[e][:, t, :], ident[:], start=False, stop=True, is_transpose=True)
-            nc.scalar.copy(summed[:, :, P * e : P * (e + 1)], turned[:])
+        def gate_of(s, h):
+            za = psum.tile([P, HALF], F32, name="za")
+            for i in range(PACK):
+                product(za[:, tile_cols(i)], "src", PACK * h + i, "wb", ORDER[s], True, False)
+                product(za[:, tile_cols(i)], "dst", PACK * h + i, "wa", ORDER[s], False, True)
+            nc.scalar.activation(eta[s, h], za[:], SIGMOID)
+
+        def weighted(name, side, s, h):
+            bank = psum.tile([P, HALF], F32, name="bank_" + name)
+            for i in range(PACK):
+                product(bank[:, tile_cols(i)], side, PACK * h + i, name, ORDER[s], True, True)
+            return bank
+
+        def copy_weighted(out, bank, h):
+            for i in range(PACK):
+                e = PACK * h + i
+                nc.scalar.activation(out[:, tile_cols(i)], bank[:, tile_cols(i)], COPY, scale=wg_col[:, e : e + 1])
+
+        def message_of(s, h):
+            copy_weighted(message[s, h], weighted("wc", "src", s, h), h)
+
+        def own_of(s, h):
+            copy_weighted(own[s, h], weighted("wo", "dst", s, h), h)
+
+        def let_through_from(bank, s, h):
+            for i in range(PACK):
+                e = PACK * h + i
+                cols = tile_cols(i)
+                nc.vector.scalar_tensor_tensor(
+                    gated[s, h][:, cols], bank[:, cols], wg_col[:, e : e + 1], eta[s, h][:, cols], MULT, MULT
+                )
+
+        def let_through(s, h):
+            nc.gpsimd.tensor_tensor(gated[s, h], message[s, h], eta[s, h], MULT)
+
+        def turn_and_add(s, h):
+            turned = psum.tile([P, HALF], F32, name="turned")
+            for n, part in enumerate((own[s, h], gated[s, h])):
+                for i in range(PACK):
+                    cols = tile_cols(i)
+                    first, final = n == 0 and i == 0, n == 1 and i == PACK - 1
+                    nc.tensor.matmul(turned[:, cols], part[:, cols], ident[:], start=first, stop=final, is_transpose=True)
+            nc.scalar.copy(sums[s, h], turned[:])
 
         def listed(tile, lo, hi):
             return tile[:].indirect(dst[:, lo // 16 : hi // 16])
 
-        def gather_state(s, lo, hi):
-            nc.vector.tensor_tensor(picked(s, lo, hi), listed(state[ORDER[s]], lo, hi), wg_row[:, lo:hi], MULT)
+        def gather_state(s, out):
+            picked[s] = out
+            nc.vector.tensor_tensor(out, listed(state[ORDER[s]], 0, J), wg_row[:], MULT)
 
-        def scatter(s, lo, hi):
-            nc.vector.tensor_tensor(listed(windows[s % 3], lo, hi), picked(s, lo, hi), summed[:, ORDER[s], lo:hi], ADD)
+        def add_state(s, h):
+            nc.gpsimd.tensor_tensor(totals[s, h], picked[s][:, half_cols(h)], sums[s, h], ADD)
 
-        def add_and_scatter(s, lo, hi):
-            if s == 0:
-                start = N * (EDGE_TILES - ON_VECTOR)
-                total = late["all"][:, start + lo : start + hi]
-            elif lo == 0:
-                total = picked_all[:, 2 * J : 2 * J + PAIR]
-            else:
-                total = messages[:, lo // PAIR, 0:PAIR]
-            nc.gpsimd.tensor_tensor(total, picked(s, lo, hi), summed[:, ORDER[s], lo:hi], ADD)
-            nc.vector.tensor_copy(listed(windows[s % 3], lo, hi), total)
+        def scatter_total(s, h):
+            nc.vector.tensor_copy(listed(windows[s], HALF * h, HALF * (h + 1)), totals[s, h])
 
-        for e in range(EDGE_TILES + 1):
-            if e < EDGE_TILES:
-                edge_products(e)
-            if e > 0:
-                turn_and_add(e - 1)
-            if e < 2:
-                gather_state(0, HALF * e, HALF * (e + 1))
-            if e == 2:
-                gather_state(1, 0, J)
-                late["all"] = held("late", [P, N * (EDGE_TILES - ON_VECTOR) + J - PAIR], F32, "state%d" % ORDER[1])
-            if e == 3:
-                add_and_scatter(0, 0, PAIR)
-                add_and_scatter(1, 0, PAIR)
-            if e in (4, 6):
-                add_and_scatter(0, P * e - PAIR, P * e)
-            if e in (5, 6):
-                add_and_scatter(1, PAIR * (e - 4), PAIR * (e - 3))
-        gather_state(2, 0, J)
+        first_gates = held("first_gates", [P, J], F32, "raw_wo1")
+        own_ring = held("own_ring", [P, J], F32)
+        last_sums = held("last_sums", [P, J], F32)
+        for s in range(PACK):
+            for h in range(2):
+                own[s, h] = own_ring[:, half_cols(h)]
+                if s == PACK - 1:
+                    sums[s, h] = last_sums[:, half_cols(h)]
+                else:
+                    sums[s, h] = held("sums%d%d" % (s, h), [P, HALF], F32)[:]
+        room = [held("room%d" % h, [P, 2 * SPARE + J], F32) for h in range(2)]
+        for step, tile in (((1, 0), room[0]), ((2, 0), room[0]), ((1, 1), room[1]), ((2, 1), room[1]), ((3, 0), room[1])):
+            message[step] = tile[:, SPARE : SPARE + HALF]
+            eta[step] = tile[:, SPARE + HALF : SPARE + J]
+        for h in range(2):
+            eta[0, h] = first_gates[:, half_cols(h)]
+        gated[0, 0] = held("gated00", [P, HALF], F32)[:]
+
+        banks = [weighted("wc", "src", 0, h) for h in range(2)]
+        gate_of(0, 0)
+        let_through_from(banks[0], 0, 0)
+        gate_of(0, 1)
+        own_of(0, 0)
+        turn_and_add(0, 0)
+        own_of(0, 1)
+        gate_of(1, 0)
+        message_of(1, 0)
+        gather_state(0, held("picked0", [P, J], F32)[:])
+        early = held("early", [P, 2, HALF], F32, "state%d" % ORDER[0])
+        gated[0, 1], totals[0, 0] = early[:, 0, :], early[:, 1, :]
+        let_through_from(banks[1], 0, 1)
+        add_state(0, 0)
+        gather_state(1, held("picked1", [P, J], F32)[:])
+        late = held("late", [P, PACK, HALF], F32, "state%d" % ORDER[1])
+        totals[0, 1], gated[1, 0], totals[1, 0], totals[2, 0] = (late[:, n, :] for n in range(PACK))
+        totals[1, 1], totals[2, 1] = room[0][:, 0:HALF], room[1][:, 0:HALF]
+        gated[1, 1] = picked[0][:, half_cols(1)]
+        for h in range(2):
+            gated[2, h] = picked[1][:, half_cols(h)]
+        scatter_total(0, 0)
+        turn_and_add(0, 1)
+        let_through(1, 0)
+        gate_of(1, 1)
+        message_of(1, 1)
+        own_of(1, 0)
+        add_state(0, 1)
+        scatter_total(0, 1)
+        turn_and_add(1, 0)
+        let_through(1, 1)
+        own_of(1, 1)
+        gate_of(2, 0)
+        message_of(2, 0)
+        add_state(1, 0)
+        scatter_total(1, 0)
+        turn_and_add(1, 1)
+        let_through(2, 0)
+        gate_of(2, 1)
+        message_of(2, 1)
+        own_of(2, 0)
+        gather_state(2, room[0][:, 2 * SPARE :])
+        add_state(1, 1)
+        scatter_total(1, 1)
+        turn_and_add(2, 0)
+        let_through(2, 1)
 
         y_rows = out_0.rearrange("(p t) c -> t p c", t=PACK)
-        rounded = [held("rounded%d" % h, [P, T // 2, PACK], BF16) for h in range(2)]
-        y_codes = held("y_codes", [P, T], I32)
-        y_plane = held("y_plane", [P, T // 2], U8)
-        code_rows = out_1[0].rearrange("p t i -> p (t i)").bitcast(I32)
-
-        def woven(lo, hi):
-            h = lo // (T // 2)
-            return rounded[h][:, lo - T // 2 * h : hi - T // 2 * h, :]
-
-        def round_columns(move, s, lo, hi):
-            move(woven(lo, hi)[:, :, ORDER[s]], windows[s % 3][:, lo:hi])
-
-        pairs = held("pairs", [P, 2, PAIRED, 2], BF16)
+        pair_room = held("pairs", [P, 2, PAIRED], F32, "sums10")
+        pairs = pair_room[:].bitcast(BF16).rearrange("p u (c e) -> p u c e", e=2)
 
         def round_pairs(move, s, lo, hi):
             move(pairs[:, ORDER[s] // 2, lo:hi, ORDER[s] % 2], windows[s % 3][:, lo:hi])
 
-        def weave(lo, hi):
-            nc.vector.tensor_copy(
-                woven(lo, hi).rearrange("p c i -> p (c i)").bitcast(F32).rearrange("p (c u) -> p c u", u=2),
-                pairs[:].rearrange("p u c e -> p u (c e)").bitcast(F32).rearrange("p u c -> p c u")[:, lo:hi],
+        nc.sync.dma_start(out=y_rows[ORDER[0]], in_=windows[0][:])
+        own_of(2, 1)
+        gate_of(3, 0)
+        message_of(3, 0)
+        turn_and_add(2, 1)
+        round_pairs(nc.scalar.copy, 0, 0, PAIRED)
+        message[3, 1], eta[3, 1] = picked[1][:, half_cols(0)], picked[1][:, half_cols(1)]
+        gated[3, 0], gated[3, 1] = picked[2][:, half_cols(0)], sums[2, 0]
+        own[3, 0] = held("own30", [P, HALF], F32)[:]
+        own[3, 1] = pair_room[:, 1, 0:HALF]
+        gate_of(3, 1)
+        message_of(3, 1)
+        own_of(3, 0)
+        own_of(3, 1)
+        add_state(2, 0)
+        scatter_total(2, 0)
+        let_through(3, 0)
+        gather_state(3, room[1][:, 2 * SPARE :])
+        add_state(2, 1)
+        let_through(3, 1)
+        scatter_total(2, 1)
+        turn_and_add(3, 0)
+        turn_and_add(3, 1)
+
+        rounded = held("rounded", [P, T, PACK], BF16, "own30")
+        y_codes = held("y_codes", [P, T], I32)
+        y_plane = held("y_plane", [P, T // 2], U8)
+        code_rows = out_1[0].rearrange("p t i -> p (t i)").bitcast(I32)
+
+        def round_columns(move, s, lo, hi):
+            move(rounded[:, lo:hi, ORDER[s]], windows[s % 3][:, lo:hi])
+
+        def weave(move, lo, hi):
+            move(
+                rounded[:, lo:hi, :].rearrange("p c i -> p (c i)").bitcast(F32).rearrange("p (c u) -> p c u", u=2),
+                pair_room[:].rearrange("p u c -> p c u")[:, lo:hi],
             )
 
-        for s in range(PACK):
-            scatter(s, J - PAIR if s < 2 else 0, J)
-            if s == 1:
-                gather_state(3, 0, J)
-            nc.sync.dma_start(out=y_rows[ORDER[s]], in_=windows[s % 3][:])
-            if s < PACK - 1:
-                round_pairs(nc.scalar.copy, s, 0, PAIRED)
-                round_columns(nc.scalar.copy, s, PAIRED, T // 2)
-                round_columns(nc.scalar.copy, s, T // 2, T)
+        round_columns(nc.scalar.copy, 0, PAIRED, T)
+        for s in (1, 2):
+            nc.sync.dma_start(out=y_rows[ORDER[s]], in_=windows[s][:])
+            round_pairs(nc.scalar.copy, s, 0, PAIRED)
+            round_columns(nc.scalar.copy, s, PAIRED, T)
         last = PACK - 1
-        round_pairs(nc.vector.tensor_copy, last, 0, PAIRED)
-        round_columns(nc.vector.tensor_copy, last, PAIRED, T // 2)
-        weave(0, CHUNK)
-        weave(CHUNK, PAIRED)
-        cuts = (2 * CHUNK, 3 * CHUNK, T - CHUNK // 2, T)
+        nc.vector.tensor_tensor(listed(windows[0], 0, J), picked[last], last_sums[:], ADD)
+        nc.sync.dma_start(out=y_rows[ORDER[last]], in_=windows[0][:])
+        round_pairs(nc.vector.tensor_copy, last, 0, CHUNK)
+        round_pairs(nc.vector.tensor_copy, last, CHUNK, PAIRED - CHUNK)
+        round_pairs(nc.scalar.copy, last, PAIRED - CHUNK, PAIRED)
+        weave(nc.vector.tensor_copy, 0, CHUNK)
+        weave(nc.vector.tensor_copy, CHUNK, 2 * CHUNK)
+        weave(nc.scalar.copy, 2 * CHUNK, PAIRED)
+        cuts = (PAIRED, 3 * CHUNK, T - CHUNK // 2, T)
         for lo, hi in zip(cuts, cuts[1:]):
             round_columns(nc.scalar.copy, last, lo, hi)
 
@@ -307,7 +364,7 @@ def tile_list_rgg_ownLP_kernel(
             nc.vector.quantize_mx(
                 out=y_codes[:, lo:hi].bitcast(FP8X4),
                 scales=y_plane[4 * h : P, lo - T // 2 * h : hi - T // 2 * h],
-                in_=woven(lo, hi).rearrange("p c i -> p (c i)"),
+                in_=rounded[:, lo:hi, :].rearrange("p c i -> p (c i)"),
             )
 
         def store_codes(lo, hi):

@@ -25,8 +25,7 @@ EDGE_TILES = J // P
 HALF = J // 2
 CHUNK = 512
 ORDER = (0, 2, 3, 1)
-SPARE = 2 * P
-PAIRED = 1280
+PAIRED = 768
 
 
 def tile_list_rgg_ownLP_kernel(
@@ -36,6 +35,7 @@ def tile_list_rgg_ownLP_kernel(
     with ExitStack() as ctx:
         keep = ctx.enter_context(tc.tile_pool(name="keep", bufs=1))
         psum = ctx.enter_context(tc.psum_pool(name="psum", bufs=2))
+        single = ctx.enter_context(tc.psum_pool(name="single", bufs=1))
 
         def held(name, shape, dtype, tag=None):
             return keep.tile(shape, dtype, name=name, tag=tag or name, align_bytes=64)
@@ -78,9 +78,9 @@ def tile_list_rgg_ownLP_kernel(
 
         ident = held("ident", [P, P], F32)
         make_identity(nc, ident[:])
-        windows = [held("window%d" % i, [P, T], F32) for i in range(3)]
-        for window in windows:
-            nc.gpsimd.memset(window[:], 0.0)
+        windows = {i: held("window%d" % i, [P, T], F32) for i in (1, 2)}
+        for i in (1, 2):
+            nc.gpsimd.memset(windows[i][:], 0.0)
 
         load_weight("wa", wa, 2)
         nc.sync.dma_start(out=wc_raw[:].bitcast(I32), in_=wc_words[0].bitcast(I32))
@@ -182,7 +182,10 @@ def tile_list_rgg_ownLP_kernel(
             nc.scalar.activation(eta[s, h], za[:], SIGMOID)
 
         def weighted(name, side, s, h):
-            bank = psum.tile([P, HALF], F32, name="bank_" + name)
+            if name == "wo":
+                bank = psum.tile([P, HALF], F32, name="ow")
+            else:
+                bank = single.tile([P, HALF], F32, name="ms_kept" if (s, h) == (0, 1) else "ms")
             for i in range(PACK):
                 product(bank[:, tile_cols(i)], side, PACK * h + i, name, ORDER[s], True, True)
             return bank
@@ -241,10 +244,10 @@ def tile_list_rgg_ownLP_kernel(
                     sums[s, h] = last_sums[:, half_cols(h)]
                 else:
                     sums[s, h] = held("sums%d%d" % (s, h), [P, HALF], F32)[:]
-        room = [held("room%d" % h, [P, 2 * SPARE + J], F32) for h in range(2)]
-        for step, tile in (((1, 0), room[0]), ((2, 0), room[0]), ((1, 1), room[1]), ((2, 1), room[1]), ((3, 0), room[1])):
-            message[step] = tile[:, SPARE : SPARE + HALF]
-            eta[step] = tile[:, SPARE + HALF : SPARE + J]
+        room = held("room", [P, 2, 2, HALF], F32)
+        for s in range(1, PACK):
+            for h in range(2):
+                message[s, h], eta[s, h] = room[:, h, 0, :], room[:, h, 1, :]
         for h in range(2):
             eta[0, h] = first_gates[:, half_cols(h)]
         gated[0, 0] = held("gated00", [P, HALF], F32)[:]
@@ -258,76 +261,54 @@ def tile_list_rgg_ownLP_kernel(
         own_of(0, 1)
         gate_of(1, 0)
         message_of(1, 0)
-        gather_state(0, held("picked0", [P, J], F32)[:])
-        early = held("early", [P, 2, HALF], F32, "state%d" % ORDER[0])
-        gated[0, 1], totals[0, 0] = early[:, 0, :], early[:, 1, :]
-        let_through_from(banks[1], 0, 1)
-        add_state(0, 0)
-        gather_state(1, held("picked1", [P, J], F32)[:])
-        late = held("late", [P, PACK, HALF], F32, "state%d" % ORDER[1])
-        totals[0, 1], gated[1, 0], totals[1, 0], totals[2, 0] = (late[:, n, :] for n in range(PACK))
-        totals[1, 1], totals[2, 1] = room[0][:, 0:HALF], room[1][:, 0:HALF]
-        gated[1, 1] = picked[0][:, half_cols(1)]
-        for h in range(2):
-            gated[2, h] = picked[1][:, half_cols(h)]
-        scatter_total(0, 0)
-        turn_and_add(0, 1)
-        let_through(1, 0)
         gate_of(1, 1)
         message_of(1, 1)
         own_of(1, 0)
-        add_state(0, 1)
-        scatter_total(0, 1)
-        turn_and_add(1, 0)
-        let_through(1, 1)
+        for s in range(2):
+            gather_state(s, held("picked%d" % s, [P, J], F32)[:])
+        early = held("early", [P, 2, HALF], F32, "state%d" % ORDER[1])
+        gated[0, 1], totals[0, 0] = early[:, 0, :], early[:, 1, :]
+        let_through_from(banks[1], 0, 1)
+        add_state(0, 0)
+        gather_state(2, held("picked2", [P, J], F32)[:])
+        windows[0] = held("window0", [P, T], F32, "state%d" % ORDER[2])
+        nc.gpsimd.memset(windows[0][:], 0.0)
+        turn_and_add(0, 1)
         own_of(1, 1)
-        gate_of(2, 0)
-        message_of(2, 0)
-        add_state(1, 0)
-        scatter_total(1, 0)
-        turn_and_add(1, 1)
-        let_through(2, 0)
-        gate_of(2, 1)
-        message_of(2, 1)
-        own_of(2, 0)
-        gather_state(2, room[0][:, 2 * SPARE :])
-        add_state(1, 1)
-        scatter_total(1, 1)
-        turn_and_add(2, 0)
-        let_through(2, 1)
+        gather_state(PACK - 1, held("picked_last", [P, J], F32)[:])
+        late = held("late", [P, 6, HALF], F32, "state%d" % ORDER[PACK - 1])
+        steps = [(s, h) for s in range(PACK) for h in range(2)]
+        for n, (s, h) in enumerate(steps[:6]):
+            if n > 0:
+                totals[s, h] = late[:, n, :]
+            gated[s + 1, h] = picked[s][:, half_cols(h)] if n > 0 else late[:, 0, :]
 
         y_rows = out_0.rearrange("(p t) c -> t p c", t=PACK)
-        pair_room = held("pairs", [P, 2, PAIRED], F32, "sums10")
-        pairs = pair_room[:].bitcast(BF16).rearrange("p u (c e) -> p u c e", e=2)
+        pair_room = {}
 
         def round_pairs(move, s, lo, hi):
+            pairs = pair_room[0][:].bitcast(BF16).rearrange("p u (c e) -> p u c e", e=2)
             move(pairs[:, ORDER[s] // 2, lo:hi, ORDER[s] % 2], windows[s % 3][:, lo:hi])
 
-        nc.sync.dma_start(out=y_rows[ORDER[0]], in_=windows[0][:])
-        own_of(2, 1)
-        gate_of(3, 0)
-        message_of(3, 0)
-        turn_and_add(2, 1)
-        round_pairs(nc.scalar.copy, 0, 0, PAIRED)
-        message[3, 1], eta[3, 1] = picked[1][:, half_cols(0)], picked[1][:, half_cols(1)]
-        gated[3, 0], gated[3, 1] = picked[2][:, half_cols(0)], sums[2, 0]
-        own[3, 0] = held("own30", [P, HALF], F32)[:]
-        own[3, 1] = pair_room[:, 1, 0:HALF]
-        gate_of(3, 1)
-        message_of(3, 1)
-        own_of(3, 0)
-        own_of(3, 1)
-        add_state(2, 0)
-        scatter_total(2, 0)
-        let_through(3, 0)
-        gather_state(3, room[1][:, 2 * SPARE :])
-        add_state(2, 1)
-        let_through(3, 1)
-        scatter_total(2, 1)
-        turn_and_add(3, 0)
-        turn_and_add(3, 1)
+        for n, (s, h) in enumerate(steps[:6]):
+            if n > 0:
+                add_state(s, h)
+            scatter_total(s, h)
+            let_through(s + 1, h)
+            turn_and_add(s + 1, h)
+            if (s, h) == (1, 0):
+                pair_room[0] = held("pairs", [P, 2, PAIRED], F32, "sums10")
+                own[3, 0] = pair_room[0][:, 1, 0:HALF]
+            if s + 2 < PACK:
+                gate_of(s + 2, h)
+                message_of(s + 2, h)
+                own_of(s + 2, h)
+            if (s, h) == (0, 1):
+                nc.sync.dma_start(out=y_rows[ORDER[0]], in_=windows[0][:])
+            if (s, h) == (1, 0):
+                round_pairs(nc.scalar.copy, 0, 0, PAIRED)
 
-        rounded = held("rounded", [P, T, PACK], BF16, "own30")
+        rounded = held("rounded", [P, T, PACK], BF16, "room")
         y_codes = held("y_codes", [P, T], I32)
         y_plane = held("y_plane", [P, T // 2], U8)
         code_rows = out_1[0].rearrange("p t i -> p (t i)").bitcast(I32)
@@ -338,10 +319,10 @@ def tile_list_rgg_ownLP_kernel(
         def weave(move, lo, hi):
             move(
                 rounded[:, lo:hi, :].rearrange("p c i -> p (c i)").bitcast(F32).rearrange("p (c u) -> p c u", u=2),
-                pair_room[:].rearrange("p u c -> p c u")[:, lo:hi],
+                pair_room[0][:].rearrange("p u c -> p c u")[:, lo:hi],
             )
 
-        round_columns(nc.scalar.copy, 0, PAIRED, T)
+        round_columns(nc.gpsimd.tensor_copy, 0, PAIRED, T)
         for s in (1, 2):
             nc.sync.dma_start(out=y_rows[ORDER[s]], in_=windows[s][:])
             round_pairs(nc.scalar.copy, s, 0, PAIRED)
@@ -349,13 +330,11 @@ def tile_list_rgg_ownLP_kernel(
         last = PACK - 1
         nc.vector.tensor_tensor(listed(windows[0], 0, J), picked[last], last_sums[:], ADD)
         nc.sync.dma_start(out=y_rows[ORDER[last]], in_=windows[0][:])
-        round_pairs(nc.vector.tensor_copy, last, 0, CHUNK)
-        round_pairs(nc.vector.tensor_copy, last, CHUNK, PAIRED - CHUNK)
-        round_pairs(nc.scalar.copy, last, PAIRED - CHUNK, PAIRED)
+        round_pairs(nc.vector.tensor_copy, last, 0, PAIRED)
+        round_columns(nc.vector.tensor_copy, last, PAIRED, T // 2)
         weave(nc.vector.tensor_copy, 0, CHUNK)
-        weave(nc.vector.tensor_copy, CHUNK, 2 * CHUNK)
-        weave(nc.scalar.copy, 2 * CHUNK, PAIRED)
-        cuts = (PAIRED, 3 * CHUNK, T - CHUNK // 2, T)
+        weave(nc.vector.tensor_copy, CHUNK, PAIRED)
+        cuts = (2 * CHUNK, 3 * CHUNK, T - CHUNK // 2, T)
         for lo, hi in zip(cuts, cuts[1:]):
             round_columns(nc.scalar.copy, last, lo, hi)
 
@@ -374,10 +353,10 @@ def tile_list_rgg_ownLP_kernel(
         quantise_columns(CHUNK, 2 * CHUNK)
         store_codes(0, 2 * CHUNK)
         quantise_columns(2 * CHUNK, 3 * CHUNK)
+        store_codes(2 * CHUNK, 3 * CHUNK)
         quantise_columns(3 * CHUNK, T - CHUNK // 2)
-        store_codes(2 * CHUNK, T - CHUNK // 2)
         quantise_columns(T - CHUNK // 2, T)
-        store_codes(T - CHUNK // 2, T)
+        store_codes(3 * CHUNK, T)
         scale_rows = out_2[0].bitcast(I32)
         for q in range(4):
             queue = nc.scalar if q % 2 else nc.sync

@@ -25,7 +25,8 @@ EDGE_TILES = J // P
 HALF = J // 2
 CHUNK = 512
 ORDER = (0, 2, 3, 1)
-PAIRED = 768
+PAIRED = 1024
+FIRST = 3 * P
 
 
 def tile_list_rgg_ownLP_kernel(
@@ -228,20 +229,27 @@ def tile_list_rgg_ownLP_kernel(
             picked[s] = out
             nc.vector.tensor_tensor(out, listed(state[ORDER[s]], 0, J), wg_row[:], MULT)
 
+        def piece(s, h):
+            cut = FIRST if s == 0 else HALF
+            return (0, cut) if h == 0 else (cut, J)
+
         def add_state(s, h):
-            nc.gpsimd.tensor_tensor(totals[s, h], picked[s][:, half_cols(h)], sums[s, h], ADD)
+            lo, hi = piece(s, h)
+            products = first_sums[:, lo:hi] if s == 0 else sums[s, h]
+            nc.gpsimd.tensor_tensor(totals[s, h], picked[s][:, lo:hi], products, ADD)
 
         def scatter_total(s, h):
-            nc.vector.tensor_copy(listed(windows[s], HALF * h, HALF * (h + 1)), totals[s, h])
+            nc.vector.tensor_copy(listed(windows[s], *piece(s, h)), totals[s, h])
 
         first_gates = held("first_gates", [P, J], F32, "raw_wo1")
         own_ring = held("own_ring", [P, J], F32)
+        first_sums = held("first_sums", [P, J], F32)
         last_sums = held("last_sums", [P, J], F32)
         for s in range(PACK):
             for h in range(2):
                 own[s, h] = own_ring[:, half_cols(h)]
-                if s == PACK - 1:
-                    sums[s, h] = last_sums[:, half_cols(h)]
+                if s in (0, PACK - 1):
+                    sums[s, h] = (first_sums if s == 0 else last_sums)[:, half_cols(h)]
                 else:
                     sums[s, h] = held("sums%d%d" % (s, h), [P, HALF], F32)[:]
         room = held("room", [P, 2, 2, HALF], F32)
@@ -267,7 +275,7 @@ def tile_list_rgg_ownLP_kernel(
         for s in range(2):
             gather_state(s, held("picked%d" % s, [P, J], F32)[:])
         early = held("early", [P, 2, HALF], F32, "state%d" % ORDER[1])
-        gated[0, 1], totals[0, 0] = early[:, 0, :], early[:, 1, :]
+        gated[0, 1], totals[0, 0] = early[:, 0, :], early[:, 1, 0:FIRST]
         let_through_from(banks[1], 0, 1)
         add_state(0, 0)
         gather_state(2, held("picked2", [P, J], F32)[:])
@@ -276,12 +284,13 @@ def tile_list_rgg_ownLP_kernel(
         turn_and_add(0, 1)
         own_of(1, 1)
         gather_state(PACK - 1, held("picked_last", [P, J], F32)[:])
-        late = held("late", [P, 6, HALF], F32, "state%d" % ORDER[PACK - 1])
+        late = held("late", [P, J - FIRST + 4 * HALF], F32, "state%d" % ORDER[PACK - 1])
         steps = [(s, h) for s in range(PACK) for h in range(2)]
+        totals[0, 1] = late[:, 0 : J - FIRST]
         for n, (s, h) in enumerate(steps[:6]):
-            if n > 0:
-                totals[s, h] = late[:, n, :]
-            gated[s + 1, h] = picked[s][:, half_cols(h)] if n > 0 else late[:, 0, :]
+            if s > 0:
+                totals[s, h] = late[:, J - FIRST + HALF * (n - 2) : J - FIRST + HALF * (n - 1)]
+            gated[s + 1, h] = picked[s][:, half_cols(h)]
 
         y_rows = out_0.rearrange("(p t) c -> t p c", t=PACK)
         pair_room = {}
@@ -290,10 +299,13 @@ def tile_list_rgg_ownLP_kernel(
             pairs = pair_room[0][:].bitcast(BF16).rearrange("p u (c e) -> p u c e", e=2)
             move(pairs[:, ORDER[s] // 2, lo:hi, ORDER[s] % 2], windows[s % 3][:, lo:hi])
 
+        scatter_total(0, 0)
+        add_state(0, 1)
         for n, (s, h) in enumerate(steps[:6]):
-            if n > 0:
+            if s > 0:
                 add_state(s, h)
-            scatter_total(s, h)
+            if n > 0:
+                scatter_total(s, h)
             let_through(s + 1, h)
             turn_and_add(s + 1, h)
             if (s, h) == (1, 0):
@@ -322,7 +334,7 @@ def tile_list_rgg_ownLP_kernel(
                 pair_room[0][:].rearrange("p u c -> p c u")[:, lo:hi],
             )
 
-        round_columns(nc.gpsimd.tensor_copy, 0, PAIRED, T)
+        nc.gpsimd.tensor_scalar(rounded[:, PAIRED:T, ORDER[0]], windows[0][:, PAIRED:T], 1.0, 0.0, MULT, ADD)
         for s in (1, 2):
             nc.sync.dma_start(out=y_rows[ORDER[s]], in_=windows[s][:])
             round_pairs(nc.scalar.copy, s, 0, PAIRED)
@@ -330,8 +342,8 @@ def tile_list_rgg_ownLP_kernel(
         last = PACK - 1
         nc.vector.tensor_tensor(listed(windows[0], 0, J), picked[last], last_sums[:], ADD)
         nc.sync.dma_start(out=y_rows[ORDER[last]], in_=windows[0][:])
-        round_pairs(nc.vector.tensor_copy, last, 0, PAIRED)
-        round_columns(nc.vector.tensor_copy, last, PAIRED, T // 2)
+        round_pairs(nc.vector.tensor_copy, last, 0, CHUNK)
+        round_pairs(nc.vector.tensor_copy, last, CHUNK, PAIRED)
         weave(nc.vector.tensor_copy, 0, CHUNK)
         weave(nc.vector.tensor_copy, CHUNK, PAIRED)
         cuts = (2 * CHUNK, 3 * CHUNK, T - CHUNK // 2, T)

@@ -26,7 +26,7 @@ HALF = J // 2
 CHUNK = 512
 ORDER = (0, 2, 3, 1)
 PAIRED = 1024
-FIRST = 3 * P
+FIRST = 448
 
 
 def tile_list_rgg_ownLP_kernel(
@@ -258,7 +258,8 @@ def tile_list_rgg_ownLP_kernel(
                 message[s, h], eta[s, h] = room[:, h, 0, :], room[:, h, 1, :]
         for h in range(2):
             eta[0, h] = first_gates[:, half_cols(h)]
-        gated[0, 0] = held("gated00", [P, HALF], F32)[:]
+        gather_state(0, held("picked0", [P, J], F32)[:])
+        gated[0, 0] = held("gated00", [P, HALF], F32, "state%d" % ORDER[0])[:]
 
         banks = [weighted("wc", "src", 0, h) for h in range(2)]
         gate_of(0, 0)
@@ -272,8 +273,7 @@ def tile_list_rgg_ownLP_kernel(
         gate_of(1, 1)
         message_of(1, 1)
         own_of(1, 0)
-        for s in range(2):
-            gather_state(s, held("picked%d" % s, [P, J], F32)[:])
+        gather_state(1, held("picked1", [P, J], F32)[:])
         early = held("early", [P, 2, HALF], F32, "state%d" % ORDER[1])
         gated[0, 1], totals[0, 0] = early[:, 0, :], early[:, 1, 0:FIRST]
         let_through_from(banks[1], 0, 1)
@@ -284,13 +284,13 @@ def tile_list_rgg_ownLP_kernel(
         turn_and_add(0, 1)
         own_of(1, 1)
         gather_state(PACK - 1, held("picked_last", [P, J], F32)[:])
-        late = held("late", [P, J - FIRST + 4 * HALF], F32, "state%d" % ORDER[PACK - 1])
+        late = held("late", [P, J - FIRST + 5 * HALF], F32, "state%d" % ORDER[PACK - 1])
         steps = [(s, h) for s in range(PACK) for h in range(2)]
         totals[0, 1] = late[:, 0 : J - FIRST]
         for n, (s, h) in enumerate(steps[:6]):
             if s > 0:
                 totals[s, h] = late[:, J - FIRST + HALF * (n - 2) : J - FIRST + HALF * (n - 1)]
-            gated[s + 1, h] = picked[s][:, half_cols(h)]
+            gated[s + 1, h] = picked[s][:, half_cols(h)] if n > 0 else late[:, J - FIRST + 4 * HALF :]
 
         y_rows = out_0.rearrange("(p t) c -> t p c", t=PACK)
         pair_room = {}
@@ -300,11 +300,9 @@ def tile_list_rgg_ownLP_kernel(
             move(pairs[:, ORDER[s] // 2, lo:hi, ORDER[s] % 2], windows[s % 3][:, lo:hi])
 
         scatter_total(0, 0)
-        add_state(0, 1)
         for n, (s, h) in enumerate(steps[:6]):
-            if s > 0:
-                add_state(s, h)
             if n > 0:
+                add_state(s, h)
                 scatter_total(s, h)
             let_through(s + 1, h)
             turn_and_add(s + 1, h)

@@ -300,25 +300,32 @@ def tile_list_rgg_ownLP_kernel(
             move(pairs[:, ORDER[s] // 2, lo:hi, ORDER[s] % 2], windows[s % 3][:, lo:hi])
 
         scatter_total(0, 0)
-        for n, (s, h) in enumerate(steps[:6]):
+        gated[3, 1], totals[2, 1] = sums[2, 0], message[3, 1]
+        for n, (s, h) in enumerate(steps[:5]):
             if n > 0:
                 add_state(s, h)
                 scatter_total(s, h)
             let_through(s + 1, h)
             turn_and_add(s + 1, h)
-            if (s, h) == (1, 0):
-                pair_room[0] = held("pairs", [P, 2, PAIRED], F32, "sums10")
-                own[3, 0] = pair_room[0][:, 1, 0:HALF]
             if s + 2 < PACK:
                 gate_of(s + 2, h)
                 message_of(s + 2, h)
+            if (s, h) == (1, 1):
+                pair_room[0] = held("pairs", [P, 2, PAIRED], F32, "sums11")
+                own[3, 0] = pair_room[0][:, 1, 0:HALF]
+                own_of(3, 0)
+            if s + 2 < PACK and (s, h) != (1, 0):
                 own_of(s + 2, h)
             if (s, h) == (0, 1):
                 nc.sync.dma_start(out=y_rows[ORDER[0]], in_=windows[0][:])
-            if (s, h) == (1, 0):
+            if (s, h) == (1, 1):
                 round_pairs(nc.scalar.copy, 0, 0, PAIRED)
+        let_through(3, 1)
+        turn_and_add(3, 1)
+        add_state(2, 1)
+        scatter_total(2, 1)
 
-        rounded = held("rounded", [P, T, PACK], BF16, "room")
+        rounded = held("rounded", [P, T, PACK], BF16, "sums21")
         y_codes = held("y_codes", [P, T], I32)
         y_plane = held("y_plane", [P, T // 2], U8)
         code_rows = out_1[0].rearrange("p t i -> p (t i)").bitcast(I32)

@@ -252,10 +252,10 @@ def tile_list_rgg_ownLP_kernel(
                     sums[s, h] = (first_sums if s == 0 else last_sums)[:, half_cols(h)]
                 else:
                     sums[s, h] = held("sums%d%d" % (s, h), [P, HALF], F32)[:]
-        room = held("room", [P, 2, 2, HALF], F32)
-        for s in range(1, PACK):
-            for h in range(2):
-                message[s, h], eta[s, h] = room[:, h, 0, :], room[:, h, 1, :]
+        own[0, 1] = own[0, 0]
+        room = held("room", [P, 3, 2, HALF], F32)
+        for n, step in enumerate(((1, 0), (2, 0), (1, 1), (2, 1), (3, 0), (3, 1))):
+            message[step], eta[step] = room[:, n % 3, 0, :], room[:, n % 3, 1, :]
         for h in range(2):
             eta[0, h] = first_gates[:, half_cols(h)]
         gather_state(0, held("picked0", [P, J], F32)[:])
@@ -270,9 +270,9 @@ def tile_list_rgg_ownLP_kernel(
         own_of(0, 1)
         gate_of(1, 0)
         message_of(1, 0)
-        gate_of(1, 1)
-        message_of(1, 1)
-        own_of(1, 0)
+        for step in ((2, 0), (1, 1)):
+            gate_of(*step)
+            message_of(*step)
         gather_state(1, held("picked1", [P, J], F32)[:])
         early = held("early", [P, 2, HALF], F32, "state%d" % ORDER[1])
         gated[0, 1], totals[0, 0] = early[:, 0, :], early[:, 1, 0:FIRST]
@@ -282,7 +282,10 @@ def tile_list_rgg_ownLP_kernel(
         windows[0] = held("window0", [P, T], F32, "state%d" % ORDER[2])
         nc.gpsimd.memset(windows[0][:], 0.0)
         turn_and_add(0, 1)
-        own_of(1, 1)
+        own[2, 0] = own[2, 1] = gated[0, 1]
+        own[1, 1] = own[3, 1] = own[1, 0]
+        own_of(1, 0)
+        own_of(2, 0)
         gather_state(PACK - 1, held("picked_last", [P, J], F32)[:])
         late = held("late", [P, J - FIRST + 5 * HALF], F32, "state%d" % ORDER[PACK - 1])
         steps = [(s, h) for s in range(PACK) for h in range(2)]
@@ -290,7 +293,6 @@ def tile_list_rgg_ownLP_kernel(
         for n, (s, h) in enumerate(steps[:6]):
             if s > 0:
                 totals[s, h] = late[:, J - FIRST + HALF * (n - 2) : J - FIRST + HALF * (n - 1)]
-            gated[s + 1, h] = picked[s][:, half_cols(h)] if n > 0 else late[:, J - FIRST + 4 * HALF :]
 
         y_rows = out_0.rearrange("(p t) c -> t p c", t=PACK)
         pair_room = {}
@@ -300,30 +302,35 @@ def tile_list_rgg_ownLP_kernel(
             move(pairs[:, ORDER[s] // 2, lo:hi, ORDER[s] % 2], windows[s % 3][:, lo:hi])
 
         scatter_total(0, 0)
-        gated[3, 1], totals[2, 1] = sums[2, 0], message[3, 1]
-        for n, (s, h) in enumerate(steps[:5]):
-            if n > 0:
-                add_state(s, h)
-                scatter_total(s, h)
-            let_through(s + 1, h)
-            turn_and_add(s + 1, h)
-            if s + 2 < PACK:
-                gate_of(s + 2, h)
-                message_of(s + 2, h)
-            if (s, h) == (1, 1):
-                pair_room[0] = held("pairs", [P, 2, PAIRED], F32, "sums11")
-                own[3, 0] = pair_room[0][:, 1, 0:HALF]
-                own_of(3, 0)
-            if s + 2 < PACK and (s, h) != (1, 0):
-                own_of(s + 2, h)
-            if (s, h) == (0, 1):
-                nc.sync.dma_start(out=y_rows[ORDER[0]], in_=windows[0][:])
-            if (s, h) == (1, 1):
-                round_pairs(nc.scalar.copy, 0, 0, PAIRED)
-        let_through(3, 1)
-        turn_and_add(3, 1)
-        add_state(2, 1)
-        scatter_total(2, 1)
+        gated[1, 0] = late[:, J - FIRST + 4 * HALF :]
+        gated[2, 0], gated[1, 1] = picked[0][:, half_cols(1)], picked[1][:, half_cols(0)]
+        gated[2, 1], gated[3, 0] = picked[2][:, half_cols(0)], picked[1][:, half_cols(1)]
+        gated[3, 1], totals[2, 1] = sums[1, 1], message[3, 1]
+
+        def step_of(product, after, total):
+            let_through(*product)
+            turn_and_add(*product)
+            if after is not None:
+                gate_of(*after)
+                message_of(*after)
+            if total is not None:
+                add_state(*total)
+                scatter_total(*total)
+
+        step_of((1, 0), (2, 1), (0, 1))
+        nc.sync.dma_start(out=y_rows[ORDER[0]], in_=windows[0][:])
+        own_of(1, 1)
+        step_of((2, 0), (3, 0), (1, 0))
+        own_of(2, 1)
+        step_of((1, 1), (3, 1), (2, 0))
+        own_of(3, 1)
+        pair_room[0] = held("pairs", [P, 2, PAIRED], F32, "sums20")
+        own[3, 0] = pair_room[0][:, 1, 0:HALF]
+        own_of(3, 0)
+        step_of((2, 1), None, (1, 1))
+        round_pairs(nc.scalar.copy, 0, 0, PAIRED)
+        step_of((3, 0), None, None)
+        step_of((3, 1), None, (2, 1))
 
         rounded = held("rounded", [P, T, PACK], BF16, "sums21")
         y_codes = held("y_codes", [P, T], I32)

@@ -25,8 +25,8 @@ EDGE_TILES = J // P
 HALF = J // 2
 CHUNK = 512
 ORDER = (0, 2, 3, 1)
-PAIRED = 1024
-FIRST = 448
+SHARE = 1024
+FRONT = 384
 
 
 def tile_list_rgg_ownLP_kernel(
@@ -35,15 +35,23 @@ def tile_list_rgg_ownLP_kernel(
     nc = tc.nc
     with ExitStack() as ctx:
         keep = ctx.enter_context(tc.tile_pool(name="keep", bufs=1))
-        psum = ctx.enter_context(tc.psum_pool(name="psum", bufs=2))
-        single = ctx.enter_context(tc.psum_pool(name="single", bufs=1))
+        psum = ctx.enter_context(tc.psum_pool(name="psum", bufs=1))
 
         def held(name, shape, dtype, tag=None):
             return keep.tile(shape, dtype, name=name, tag=tag or name, align_bytes=64)
 
-        def load_scale_rows(queue, plane, rows):
+        def bank(tag):
+            return psum.tile([P, HALF], F32, name=tag, tag=tag)
+
+        def load_scale_rows(plane, rows):
             for q in range(4):
-                queue.dma_start(out=plane[32 * q : 32 * q + 4, :].bitcast(I32), in_=rows.bitcast(I32)[4 * q : 4 * q + 4, :])
+                nc.sync.dma_start(out=plane[32 * q : 32 * q + 4, :].bitcast(I32), in_=rows.bitcast(I32)[4 * q : 4 * q + 4, :])
+
+        def tile_cols(i):
+            return slice(P * i, P * (i + 1))
+
+        def half_cols(h):
+            return slice(HALF * h, HALF * (h + 1))
 
         src = held("src", [P, J // 16], U16)
         dst = held("dst", [P, J // 16], U16)
@@ -56,7 +64,7 @@ def tile_list_rgg_ownLP_kernel(
         nc.gpsimd.memset(wg_cut[:], 0.0)
         nc.gpsimd.memset(wc_rows[:].bitcast(I32), 0)
         nc.sync.dma_start(src[:], offs)
-        load_scale_rows(nc.sync, tab_plane, tab_scales[0])
+        load_scale_rows(tab_plane, tab_scales[0])
         nc.sync.dma_start(dst[:], offs2)
         nc.sync.dma_start(out=wg_cut[0:EDGE_TILES, :], in_=wgo[0].rearrange("(e j) -> e j", j=P))
         raw = {}
@@ -69,8 +77,17 @@ def tile_list_rgg_ownLP_kernel(
                 raw[name].append(held("raw_%s%d" % (name, h), [P, PACK, width], F32))
                 nc.sync.dma_start(out=raw[name][h][:], in_=rows[:, :, width * h : width * (h + 1)])
 
+        r_rows = rT.rearrange("(p t) c -> t p c", t=PACK)
+        state = {}
+
+        def load_state(s):
+            state[s] = held("state%d" % s, [P, T], F32)
+            nc.sync.dma_start(out=state[s][:], in_=r_rows[ORDER[s]])
+
         load_weight("wb", wb, 1)
         nc.sync.dma_start(out=tab_codes[:], in_=tab_words[0].rearrange("p t i -> p (t i)").bitcast(I32))
+        nc.sync.dma_start(out=wc_raw[:].bitcast(I32), in_=wc_words[0].bitcast(I32))
+        load_scale_rows(wc_rows, wc_scales[0])
 
         warm_in = held("warm_in", [P, 1], F32)
         warm_out = held("warm_out", [P, 1], F32)
@@ -79,19 +96,15 @@ def tile_list_rgg_ownLP_kernel(
 
         ident = held("ident", [P, P], F32)
         make_identity(nc, ident[:])
-        windows = {i: held("window%d" % i, [P, T], F32) for i in (1, 2)}
-        for i in (1, 2):
-            nc.gpsimd.memset(windows[i][:], 0.0)
+        windows = [held("window%d" % i, [P, T], F32) for i in range(3)]
+        for window in windows:
+            nc.gpsimd.memset(window[:], 0.0)
 
         load_weight("wa", wa, 2)
-        nc.sync.dma_start(out=wc_raw[:].bitcast(I32), in_=wc_words[0].bitcast(I32))
-        load_scale_rows(nc.sync, wc_rows, wc_scales[0])
+        load_state(0)
         load_weight("wo", wo, 2)
-        r_rows = rT.rearrange("(p t) c -> t p c", t=PACK)
-        state = {}
-        for t in ORDER:
-            state[t] = held("state%d" % t, [P, T], F32)
-            nc.sync.dma_start(out=state[t][:], in_=r_rows[t])
+        for s in range(1, PACK):
+            load_state(s)
 
         picked_plane = {}
         picked_codes = {}
@@ -99,58 +112,64 @@ def tile_list_rgg_ownLP_kernel(
             picked_plane[name] = held("plane_" + name, [P, J], U8)
             nc.vector.tensor_copy(picked_plane[name][:], tab_plane[:].indirect(lst[:]))
 
-        def gather_codes(name, lst, h, tag=None):
-            picked_codes[name, h] = held("codes_%s%d" % (name, h), [P, HALF], U32, tag)
+        def gather_codes(name, lst, h):
+            picked_codes[name, h] = held("codes_%s%d" % (name, h), [P, HALF], U32)
             nc.vector.tensor_copy(
                 picked_codes[name, h][:], tab_codes[:].bitcast(U32).indirect(lst[:, 32 * h : 32 * (h + 1)])
             )
 
-        gather_codes("src", src, 0)
-        gather_codes("dst", dst, 0)
-        gather_codes("src", src, 1)
-
+        first = held("first", [P, 2 * J - FRONT], F32)
+        wg_row = first[:, J - FRONT :]
         wg_col = held("wg_col", [P, EDGE_TILES], F32)
-        wg_turned = psum.tile([P, PACK, P], F32, name="turned")
-        nc.tensor.transpose(wg_turned[:, 0, :], wg_cut[:], ident[:])
-        nc.scalar.copy(wg_col[:], wg_turned[:, 0, 0:EDGE_TILES])
-        wg_row = held("wg_row", [P, J], F32)
+        wg_turned = bank("turn0")
+        nc.tensor.transpose(wg_turned[:, 0:P], wg_cut[:], ident[:])
+        nc.scalar.copy(wg_col[:], wg_turned[:, 0:EDGE_TILES])
         for h in range(2):
-            spread = psum.tile([P, PACK, P], F32, name="turned")
+            spread = bank("turn%d" % (1 - h))
             for i in range(PACK):
                 e = PACK * h + i
-                nc.tensor.transpose(spread[:, i, :], wg_col[:, e : e + 1].to_broadcast([P, P]), ident[:])
-            nc.scalar.copy(wg_row[:, HALF * h : HALF * (h + 1)], spread[:].rearrange("p i j -> p (i j)"))
+                nc.tensor.transpose(spread[:, tile_cols(i)], wg_col[:, e : e + 1].to_broadcast([P, P]), ident[:])
+            nc.scalar.copy(wg_row[:, half_cols(h)], spread[:])
 
+        grouped = {}
         w_codes = {}
         w_plane = {}
 
-        def quantise_weight(name):
-            grouped = held("grouped_" + name, [P, N, PACK], BF16)
+        def round_weight(name):
+            grouped[name] = held("grouped_" + name, [P, N, PACK], BF16)
             share = P // len(raw[name])
             for h, part in enumerate(raw[name]):
                 nc.scalar.copy(
-                    grouped[:].rearrange("p (t m) i -> p m i t", t=PACK)[:, share * h : share * (h + 1)],
+                    grouped[name][:].rearrange("p (t m) i -> p m i t", t=PACK)[:, share * h : share * (h + 1)],
                     part[:].rearrange("p i (m t) -> p m i t", t=PACK),
                 )
+
+        def quantise_weight(name):
             w_codes[name] = held("wcodes_" + name, [P, N], U32)
             w_plane[name] = held("wplane_" + name, [P, N], U8)
             nc.vector.quantize_mx(
-                out=w_codes[name][:].bitcast(FP8X4), scales=w_plane[name][:], in_=grouped[:].rearrange("p n i -> p (n i)")
+                out=w_codes[name][:].bitcast(FP8X4),
+                scales=w_plane[name][:],
+                in_=grouped[name][:].rearrange("p n i -> p (n i)"),
             )
 
+        round_weight("wb")
+        gather_codes("src", src, 0)
+        gather_codes("dst", dst, 0)
+        gather_codes("src", src, 1)
         quantise_weight("wb")
-        quantise_weight("wa")
-        gather_codes("dst", dst, 1, "raw_wa1")
+        gather_codes("dst", dst, 1)
         w_plane["wc"] = held("wc_plane", [P, N], U8)
         wc_codes = held("wc_codes", [P, 2 * N], U8)
-        nc.vector.tensor_copy(
+        nc.scalar.copy(
             wc_codes[:].bitcast(U16).rearrange("p (t m) -> p t m", t=PACK),
             wc_raw[:].bitcast(U16).rearrange("p (m t) -> p t m", t=PACK),
         )
-        nc.vector.tensor_copy(
+        nc.gpsimd.tensor_copy(
             w_plane["wc"][:].rearrange("p (t m) -> p t m", t=PACK), wc_rows[:].rearrange("p (m t) -> p t m", t=PACK)
         )
-        quantise_weight("wo")
+        round_weight("wa")
+        quantise_weight("wa")
 
         def product(out, side, e, name, t, start, stop):
             if name == "wc":
@@ -167,172 +186,137 @@ def tile_list_rgg_ownLP_kernel(
                 stop=stop,
             )
 
-        eta, message, own, gated, sums, totals, picked = {}, {}, {}, {}, {}, {}, {}
+        eta, message, own, gated, residual, sums, totals, picked = {}, {}, {}, {}, {}, {}, {}, {}
 
-        def tile_cols(i):
-            return slice(P * i, P * (i + 1))
-
-        def half_cols(h):
-            return slice(HALF * h, HALF * (h + 1))
+        def copy_weighted(out, source, h):
+            for i in range(PACK):
+                e = PACK * h + i
+                nc.scalar.activation(out[:, tile_cols(i)], source[:, tile_cols(i)], COPY, scale=wg_col[:, e : e + 1])
 
         def gate_of(s, h):
-            za = psum.tile([P, HALF], F32, name="za")
+            za = bank("gate%d" % h)
             for i in range(PACK):
                 product(za[:, tile_cols(i)], "src", PACK * h + i, "wb", ORDER[s], True, False)
                 product(za[:, tile_cols(i)], "dst", PACK * h + i, "wa", ORDER[s], False, True)
             nc.scalar.activation(eta[s, h], za[:], SIGMOID)
 
-        def weighted(name, side, s, h):
-            if name == "wo":
-                bank = psum.tile([P, HALF], F32, name="ow")
-            else:
-                bank = single.tile([P, HALF], F32, name="ms_kept" if (s, h) == (0, 1) else "ms")
-            for i in range(PACK):
-                product(bank[:, tile_cols(i)], side, PACK * h + i, name, ORDER[s], True, True)
-            return bank
-
-        def copy_weighted(out, bank, h):
-            for i in range(PACK):
-                e = PACK * h + i
-                nc.scalar.activation(out[:, tile_cols(i)], bank[:, tile_cols(i)], COPY, scale=wg_col[:, e : e + 1])
-
         def message_of(s, h):
-            copy_weighted(message[s, h], weighted("wc", "src", s, h), h)
+            ms = bank("message%d" % h)
+            for i in range(PACK):
+                product(ms[:, tile_cols(i)], "src", PACK * h + i, "wc", ORDER[s], True, True)
+            copy_weighted(message[s, h], ms, h)
 
         def own_of(s, h):
-            copy_weighted(own[s, h], weighted("wo", "dst", s, h), h)
-
-        def let_through_from(bank, s, h):
+            ow = bank("own%d" % h)
             for i in range(PACK):
-                e = PACK * h + i
-                cols = tile_cols(i)
-                nc.vector.scalar_tensor_tensor(
-                    gated[s, h][:, cols], bank[:, cols], wg_col[:, e : e + 1], eta[s, h][:, cols], MULT, MULT
-                )
+                product(ow[:, tile_cols(i)], "dst", PACK * h + i, "wo", ORDER[s], True, True)
+            copy_weighted(own[s, h], ow, h)
+
+        def residual_of(s, h):
+            back = bank("gate%d" % h)
+            for i in range(PACK):
+                nc.tensor.transpose(back[:, tile_cols(i)], picked[s][:, tile_cols(PACK * h + i)], ident[:])
+            copy_weighted(residual[s, h], back, h)
 
         def let_through(s, h):
             nc.gpsimd.tensor_tensor(gated[s, h], message[s, h], eta[s, h], MULT)
 
-        def turn_and_add(s, h):
-            turned = psum.tile([P, HALF], F32, name="turned")
-            for n, part in enumerate((own[s, h], gated[s, h])):
+        def turn_and_add(out, parts, h):
+            turned = bank("turn%d" % h)
+            for n, part in enumerate(parts):
                 for i in range(PACK):
                     cols = tile_cols(i)
-                    first, final = n == 0 and i == 0, n == 1 and i == PACK - 1
-                    nc.tensor.matmul(turned[:, cols], part[:, cols], ident[:], start=first, stop=final, is_transpose=True)
-            nc.scalar.copy(sums[s, h], turned[:])
+                    begin, final = n == 0 and i == 0, n == len(parts) - 1 and i == PACK - 1
+                    nc.tensor.matmul(turned[:, cols], part[:, cols], ident[:], start=begin, stop=final, is_transpose=True)
+            nc.scalar.copy(out, turned[:])
 
         def listed(tile, lo, hi):
             return tile[:].indirect(dst[:, lo // 16 : hi // 16])
 
-        def gather_state(s, out):
-            picked[s] = out
-            nc.vector.tensor_tensor(out, listed(state[ORDER[s]], 0, J), wg_row[:], MULT)
-
-        def piece(s, h):
-            cut = FIRST if s == 0 else HALF
-            return (0, cut) if h == 0 else (cut, J)
-
         def add_state(s, h):
-            lo, hi = piece(s, h)
-            products = first_sums[:, lo:hi] if s == 0 else sums[s, h]
-            nc.gpsimd.tensor_tensor(totals[s, h], picked[s][:, lo:hi], products, ADD)
+            nc.gpsimd.tensor_tensor(totals[s][:, half_cols(h)], picked[s][:, half_cols(h)], sums[s, h], ADD)
 
-        def scatter_total(s, h):
-            nc.vector.tensor_copy(listed(windows[s], *piece(s, h)), totals[s, h])
+        def scatter_total(s):
+            nc.vector.tensor_copy(listed(windows[s % 3], 0, J), totals[s])
 
-        first_gates = held("first_gates", [P, J], F32, "raw_wo1")
-        own_ring = held("own_ring", [P, J], F32)
-        first_sums = held("first_sums", [P, J], F32)
-        last_sums = held("last_sums", [P, J], F32)
-        for s in range(PACK):
-            for h in range(2):
-                own[s, h] = own_ring[:, half_cols(h)]
-                if s in (0, PACK - 1):
-                    sums[s, h] = (first_sums if s == 0 else last_sums)[:, half_cols(h)]
-                else:
-                    sums[s, h] = held("sums%d%d" % (s, h), [P, HALF], F32)[:]
-        own[0, 1] = own[0, 0]
-        room = held("room", [P, 3, 2, HALF], F32)
-        for n, step in enumerate(((1, 0), (2, 0), (1, 1), (2, 1), (3, 0), (3, 1))):
-            message[step], eta[step] = room[:, n % 3, 0, :], room[:, n % 3, 1, :]
+        def two_halves(name, tag=None):
+            tile = held(name, [P, J], F32, tag)
+            return [tile[:, half_cols(h)] for h in range(2)]
+
+        room_m = two_halves("room_m", "raw_wa1")
         for h in range(2):
-            eta[0, h] = first_gates[:, half_cols(h)]
-        gather_state(0, held("picked0", [P, J], F32)[:])
-        gated[0, 0] = held("gated00", [P, HALF], F32, "state%d" % ORDER[0])[:]
+            message[0, h] = room_m[h]
+            message_of(0, h)
+        picked[0] = held("picked0", [P, J], F32)[:]
+        nc.vector.tensor_copy(picked[0], listed(state[0], 0, J))
+        round_weight("wo")
+        quantise_weight("wo")
+        picked[1] = held("picked1", [P, J], F32, "grouped_wo")[:]
+        nc.vector.tensor_copy(picked[1], listed(state[1], 0, J))
 
-        banks = [weighted("wc", "src", 0, h) for h in range(2)]
-        gate_of(0, 0)
-        let_through_from(banks[0], 0, 0)
-        gate_of(0, 1)
-        own_of(0, 0)
-        turn_and_add(0, 0)
-        own_of(0, 1)
-        gate_of(1, 0)
-        message_of(1, 0)
-        for step in ((2, 0), (1, 1)):
-            gate_of(*step)
-            message_of(*step)
-        gather_state(1, held("picked1", [P, J], F32)[:])
-        early = held("early", [P, 2, HALF], F32, "state%d" % ORDER[1])
-        gated[0, 1], totals[0, 0] = early[:, 0, :], early[:, 1, 0:FIRST]
-        let_through_from(banks[1], 0, 1)
-        add_state(0, 0)
-        gather_state(2, held("picked2", [P, J], F32)[:])
-        windows[0] = held("window0", [P, T], F32, "state%d" % ORDER[2])
-        nc.gpsimd.memset(windows[0][:], 0.0)
-        turn_and_add(0, 1)
-        own[2, 0] = own[2, 1] = gated[0, 1]
-        own[1, 1] = own[3, 1] = own[1, 0]
-        own_of(1, 0)
-        own_of(2, 0)
-        gather_state(PACK - 1, held("picked_last", [P, J], F32)[:])
-        late = held("late", [P, J - FIRST + 5 * HALF], F32, "state%d" % ORDER[PACK - 1])
-        steps = [(s, h) for s in range(PACK) for h in range(2)]
-        totals[0, 1] = late[:, 0 : J - FIRST]
-        for n, (s, h) in enumerate(steps[:6]):
-            if s > 0:
-                totals[s, h] = late[:, J - FIRST + HALF * (n - 2) : J - FIRST + HALF * (n - 1)]
+        room_e, room_g, room_b, room_o = two_halves("room_e", "raw_wo1"), two_halves("room_g"), two_halves("room_b"), two_halves("room_o")
+        room_n = two_halves("room_n")
+        for h in range(2):
+            eta[0, h], gated[0, h], residual[0, h], own[0, h] = room_e[h], room_g[h], room_b[h], room_o[h]
+            eta[1, h], message[1, h], residual[1, h], own[1, h] = room_b[h], room_g[h], room_o[h], room_e[h]
+            eta[2, h], message[2, h], own[2, h] = room_m[h], room_n[h], room_b[h]
+            sums[3, h] = room_n[h]
+        for h in range(2):
+            gate_of(0, h)
+            let_through(0, h)
+        for h in range(2):
+            residual_of(0, h)
+        for h in range(2):
+            own_of(0, h)
 
+        picked[2] = held("picked2", [P, J], F32)[:]
+        nc.vector.tensor_tensor(picked[2], listed(state[2], 0, J), wg_row, MULT)
+        picked[3] = held("picked3", [P, J], F32)[:]
+        nc.vector.tensor_tensor(picked[3][:, 0:FRONT], listed(state[3], 0, FRONT), wg_row[:, 0:FRONT], MULT)
+        totals[0] = first[:, 0:J]
+        for h in range(2):
+            turn_and_add(totals[0][:, half_cols(h)], (residual[0, h], gated[0, h], own[0, h]), h)
+        nc.vector.tensor_tensor(picked[3][:, FRONT:J], listed(state[3], FRONT, J), wg_row[:, FRONT:J], MULT)
+        scatter_total(0)
         y_rows = out_0.rearrange("(p t) c -> t p c", t=PACK)
-        pair_room = {}
-
-        def round_pairs(move, s, lo, hi):
-            pairs = pair_room[0][:].bitcast(BF16).rearrange("p u (c e) -> p u c e", e=2)
-            move(pairs[:, ORDER[s] // 2, lo:hi, ORDER[s] % 2], windows[s % 3][:, lo:hi])
-
-        scatter_total(0, 0)
-        gated[1, 0] = late[:, J - FIRST + 4 * HALF :]
-        gated[2, 0], gated[1, 1] = picked[0][:, half_cols(1)], picked[1][:, half_cols(0)]
-        gated[2, 1], gated[3, 0] = picked[2][:, half_cols(0)], picked[1][:, half_cols(1)]
-        gated[3, 1], totals[2, 1] = sums[1, 1], message[3, 1]
-
-        def step_of(product, after, total):
-            let_through(*product)
-            turn_and_add(*product)
-            if after is not None:
-                gate_of(*after)
-                message_of(*after)
-            if total is not None:
-                add_state(*total)
-                scatter_total(*total)
-
-        step_of((1, 0), (2, 1), (0, 1))
         nc.sync.dma_start(out=y_rows[ORDER[0]], in_=windows[0][:])
-        own_of(1, 1)
-        step_of((2, 0), (3, 0), (1, 0))
-        own_of(2, 1)
-        step_of((1, 1), (3, 1), (2, 0))
-        own_of(3, 1)
-        pair_room[0] = held("pairs", [P, 2, PAIRED], F32, "sums20")
-        own[3, 0] = pair_room[0][:, 1, 0:HALF]
-        own_of(3, 0)
-        step_of((2, 1), None, (1, 1))
-        round_pairs(nc.scalar.copy, 0, 0, PAIRED)
-        step_of((3, 0), None, None)
-        step_of((3, 1), None, (2, 1))
 
-        rounded = held("rounded", [P, T, PACK], BF16, "sums21")
+        late = held("late", [P, 2, J], F32, "state3")
+        second = held("second", [P, 2, J], F32, "state0")
+        third = held("third", [P, 2, J], F32, "state1")
+        totals[1], totals[2], totals[3] = second[:, 0, :], third[:, 0, :], third[:, 1, :]
+        for h in range(2):
+            gated[1, h], gated[2, h] = late[:, 0, half_cols(h)], late[:, 1, half_cols(h)]
+            sums[2, h] = second[:, 1, half_cols(h)]
+
+        for h in range(2):
+            gate_of(1, h)
+            message_of(1, h)
+            let_through(1, h)
+        for h in range(2):
+            own_of(1, h)
+            residual_of(1, h)
+        for h in range(2):
+            turn_and_add(totals[1][:, half_cols(h)], (residual[1, h], own[1, h], gated[1, h]), h)
+        scatter_total(1)
+        nc.sync.dma_start(out=y_rows[ORDER[1]], in_=windows[1][:])
+        rounded = held("rounded", [P, T, PACK], BF16, "grouped_wo")
+        before = rounded[:].rearrange("p c i -> p (c i)").bitcast(F32)
+        for h in range(2):
+            own[3, h], gated[3, h], message[3, h], eta[3, h] = [before[:, J * n + HALF * h : J * n + HALF * (h + 1)] for n in range(4)]
+        for s in (2, 3):
+            for h in range(2):
+                gate_of(s, h)
+                message_of(s, h)
+                let_through(s, h)
+                own_of(s, h)
+            for h in range(2):
+                turn_and_add(sums[s, h], (own[s, h], gated[s, h]), h)
+                add_state(s, h)
+            if s == 2:
+                scatter_total(s)
+                nc.sync.dma_start(out=y_rows[ORDER[s]], in_=windows[s][:])
+
         y_codes = held("y_codes", [P, T], I32)
         y_plane = held("y_plane", [P, T // 2], U8)
         code_rows = out_1[0].rearrange("p t i -> p (t i)").bitcast(I32)
@@ -340,24 +324,18 @@ def tile_list_rgg_ownLP_kernel(
         def round_columns(move, s, lo, hi):
             move(rounded[:, lo:hi, ORDER[s]], windows[s % 3][:, lo:hi])
 
-        def weave(move, lo, hi):
-            move(
-                rounded[:, lo:hi, :].rearrange("p c i -> p (c i)").bitcast(F32).rearrange("p (c u) -> p c u", u=2),
-                pair_room[0][:].rearrange("p u c -> p c u")[:, lo:hi],
-            )
+        def gpsimd_round(out, in_):
+            nc.gpsimd.tensor_scalar(out, in_, 1.0, 0.0, MULT, ADD)
 
-        nc.gpsimd.tensor_scalar(rounded[:, PAIRED:T, ORDER[0]], windows[0][:, PAIRED:T], 1.0, 0.0, MULT, ADD)
-        for s in (1, 2):
-            nc.sync.dma_start(out=y_rows[ORDER[s]], in_=windows[s][:])
-            round_pairs(nc.scalar.copy, s, 0, PAIRED)
-            round_columns(nc.scalar.copy, s, PAIRED, T)
+        for s in range(PACK - 1):
+            round_columns(nc.scalar.copy, s, 0, SHARE)
+            round_columns(gpsimd_round, s, SHARE, SHARE + CHUNK)
+            round_columns(gpsimd_round, s, SHARE + CHUNK, T)
         last = PACK - 1
-        nc.vector.tensor_tensor(listed(windows[0], 0, J), picked[last], last_sums[:], ADD)
+        scatter_total(last)
         nc.sync.dma_start(out=y_rows[ORDER[last]], in_=windows[0][:])
-        round_pairs(nc.vector.tensor_copy, last, 0, CHUNK)
-        round_pairs(nc.vector.tensor_copy, last, CHUNK, PAIRED)
-        weave(nc.vector.tensor_copy, 0, CHUNK)
-        weave(nc.vector.tensor_copy, CHUNK, PAIRED)
+        round_columns(nc.vector.tensor_copy, last, 0, CHUNK)
+        round_columns(nc.vector.tensor_copy, last, CHUNK, SHARE)
         cuts = (2 * CHUNK, 3 * CHUNK, T - CHUNK // 2, T)
         for lo, hi in zip(cuts, cuts[1:]):
             round_columns(nc.scalar.copy, last, lo, hi)

@@ -24,7 +24,7 @@ PACK = 4
 EDGE_TILES = J // P
 HALF = J // 2
 CHUNK = 512
-ORDER = (0, 2, 3, 1)
+ORDER = (2, 0, 1, 3)
 SHARE = 1024
 FRONT = 384
 
@@ -85,9 +85,9 @@ def tile_list_rgg_ownLP_kernel(
             nc.sync.dma_start(out=state[s][:], in_=r_rows[ORDER[s]])
 
         load_weight("wb", wb, 1)
-        nc.sync.dma_start(out=tab_codes[:], in_=tab_words[0].rearrange("p t i -> p (t i)").bitcast(I32))
         nc.sync.dma_start(out=wc_raw[:].bitcast(I32), in_=wc_words[0].bitcast(I32))
         load_scale_rows(wc_rows, wc_scales[0])
+        nc.sync.dma_start(out=tab_codes[:], in_=tab_words[0].rearrange("p t i -> p (t i)").bitcast(I32))
 
         warm_in = held("warm_in", [P, 1], F32)
         warm_out = held("warm_out", [P, 1], F32)
@@ -118,8 +118,9 @@ def tile_list_rgg_ownLP_kernel(
                 picked_codes[name, h][:], tab_codes[:].bitcast(U32).indirect(lst[:, 32 * h : 32 * (h + 1)])
             )
 
-        first = held("first", [P, 2 * J - FRONT], F32)
-        wg_row = first[:, J - FRONT :]
+        first = held("first", [P, J], F32)
+        wg_front = first[:, J - FRONT :]
+        wg_row = held("wg_row", [P, J], F32)[:]
         wg_col = held("wg_col", [P, EDGE_TILES], F32)
         wg_turned = bank("turn0")
         nc.tensor.transpose(wg_turned[:, 0:P], wg_cut[:], ident[:])
@@ -130,6 +131,8 @@ def tile_list_rgg_ownLP_kernel(
                 e = PACK * h + i
                 nc.tensor.transpose(spread[:, tile_cols(i)], wg_col[:, e : e + 1].to_broadcast([P, P]), ident[:])
             nc.scalar.copy(wg_row[:, half_cols(h)], spread[:])
+            if h == 0:
+                nc.scalar.copy(wg_front, spread[:, 0:FRONT])
 
         grouped = {}
         w_codes = {}
@@ -165,7 +168,7 @@ def tile_list_rgg_ownLP_kernel(
             wc_codes[:].bitcast(U16).rearrange("p (t m) -> p t m", t=PACK),
             wc_raw[:].bitcast(U16).rearrange("p (m t) -> p t m", t=PACK),
         )
-        nc.gpsimd.tensor_copy(
+        nc.vector.tensor_copy(
             w_plane["wc"][:].rearrange("p (t m) -> p t m", t=PACK), wc_rows[:].rearrange("p (m t) -> p t m", t=PACK)
         )
         round_weight("wa")
@@ -270,10 +273,10 @@ def tile_list_rgg_ownLP_kernel(
             own_of(0, h)
 
         picked[2] = held("picked2", [P, J], F32)[:]
-        nc.vector.tensor_tensor(picked[2], listed(state[2], 0, J), wg_row, MULT)
+        nc.vector.tensor_copy(picked[2], listed(state[2], 0, J))
         picked[3] = held("picked3", [P, J], F32)[:]
-        nc.vector.tensor_tensor(picked[3][:, 0:FRONT], listed(state[3], 0, FRONT), wg_row[:, 0:FRONT], MULT)
-        totals[0] = first[:, 0:J]
+        nc.vector.tensor_tensor(picked[3][:, 0:FRONT], listed(state[3], 0, FRONT), wg_front, MULT)
+        totals[0] = first[:]
         for h in range(2):
             turn_and_add(totals[0][:, half_cols(h)], (residual[0, h], gated[0, h], own[0, h]), h)
         nc.vector.tensor_tensor(picked[3][:, FRONT:J], listed(state[3], FRONT, J), wg_row[:, FRONT:J], MULT)
@@ -281,7 +284,7 @@ def tile_list_rgg_ownLP_kernel(
         y_rows = out_0.rearrange("(p t) c -> t p c", t=PACK)
         nc.sync.dma_start(out=y_rows[ORDER[0]], in_=windows[0][:])
 
-        late = held("late", [P, 2, J], F32, "state3")
+        late = held("late", [P, 3, J], F32, "state3")
         second = held("second", [P, 2, J], F32, "state0")
         third = held("third", [P, 2, J], F32, "state1")
         totals[1], totals[2], totals[3] = second[:, 0, :], third[:, 0, :], third[:, 1, :]
@@ -300,16 +303,23 @@ def tile_list_rgg_ownLP_kernel(
             turn_and_add(totals[1][:, half_cols(h)], (residual[1, h], own[1, h], gated[1, h]), h)
         scatter_total(1)
         nc.sync.dma_start(out=y_rows[ORDER[1]], in_=windows[1][:])
-        rounded = held("rounded", [P, T, PACK], BF16, "grouped_wo")
-        before = rounded[:].rearrange("p c i -> p (c i)").bitcast(F32)
+        pairs = held("pairs", [P, 2, SHARE], F32)
+        rows = held("rows", [P, PACK - 1, (T - SHARE) // 2], F32, "grouped_wo")
         for h in range(2):
-            own[3, h], gated[3, h], message[3, h], eta[3, h] = [before[:, J * n + HALF * h : J * n + HALF * (h + 1)] for n in range(4)]
+            gated[3, h], own[3, h] = pairs[:, 0, half_cols(h)], pairs[:, 1, half_cols(h)]
+        eta[3, 0], message[3, 0] = room_g[0], room_o[0]
+        message[3, 1], eta[3, 1], sums[3, 1] = [rows[:, ORDER[s], :] for s in range(PACK - 1)]
         for s in (2, 3):
             for h in range(2):
                 gate_of(s, h)
                 message_of(s, h)
                 let_through(s, h)
                 own_of(s, h)
+            if s == 2:
+                weighted = late[:, 2, :]
+                for h in range(2):
+                    nc.gpsimd.tensor_tensor(weighted[:, half_cols(h)], picked[s][:, half_cols(h)], wg_row[:, half_cols(h)], MULT)
+                picked[s] = weighted
             for h in range(2):
                 turn_and_add(sums[s, h], (own[s, h], gated[s, h]), h)
                 add_state(s, h)
@@ -317,6 +327,7 @@ def tile_list_rgg_ownLP_kernel(
                 scatter_total(s)
                 nc.sync.dma_start(out=y_rows[ORDER[s]], in_=windows[s][:])
 
+        rounded = held("rounded", [P, T, PACK], BF16)
         y_codes = held("y_codes", [P, T], I32)
         y_plane = held("y_plane", [P, T // 2], U8)
         code_rows = out_1[0].rearrange("p t i -> p (t i)").bitcast(I32)
@@ -324,18 +335,39 @@ def tile_list_rgg_ownLP_kernel(
         def round_columns(move, s, lo, hi):
             move(rounded[:, lo:hi, ORDER[s]], windows[s % 3][:, lo:hi])
 
-        def gpsimd_round(out, in_):
-            nc.gpsimd.tensor_scalar(out, in_, 1.0, 0.0, MULT, ADD)
+        def round_pairs(move, s, lo, hi):
+            halves = pairs[:].bitcast(BF16).rearrange("p u (c e) -> p u c e", e=2)
+            move(halves[:, ORDER[s] // 2, lo:hi, ORDER[s] % 2], windows[s % 3][:, lo:hi])
+
+        def weave(lo, hi):
+            nc.vector.tensor_copy(
+                rounded[:, lo:hi, :].rearrange("p c i -> p (c i)").bitcast(F32).rearrange("p (c u) -> p c u", u=2),
+                pairs[:].rearrange("p u c -> p c u")[:, lo:hi],
+            )
 
         for s in range(PACK - 1):
-            round_columns(nc.scalar.copy, s, 0, SHARE)
-            round_columns(gpsimd_round, s, SHARE, SHARE + CHUNK)
-            round_columns(gpsimd_round, s, SHARE + CHUNK, T)
+            round_pairs(nc.scalar.copy, s, 0, SHARE)
+            for lo in (0, CHUNK):
+                nc.gpsimd.tensor_scalar(
+                    rows[:, ORDER[s], :].bitcast(BF16)[:, lo : lo + CHUNK],
+                    windows[s][:, SHARE + lo : SHARE + lo + CHUNK],
+                    1.0,
+                    0.0,
+                    MULT,
+                    ADD,
+                )
+        for lo in (0, CHUNK):
+            nc.scalar.copy(
+                rounded[:, SHARE + lo : SHARE + lo + CHUNK, 0 : PACK - 1],
+                rows[:].bitcast(BF16).rearrange("p t c -> p c t")[:, lo : lo + CHUNK],
+            )
         last = PACK - 1
         scatter_total(last)
         nc.sync.dma_start(out=y_rows[ORDER[last]], in_=windows[0][:])
-        round_columns(nc.vector.tensor_copy, last, 0, CHUNK)
-        round_columns(nc.vector.tensor_copy, last, CHUNK, SHARE)
+        round_pairs(nc.vector.tensor_copy, last, 0, CHUNK)
+        round_pairs(nc.vector.tensor_copy, last, CHUNK, SHARE)
+        weave(0, CHUNK)
+        weave(CHUNK, SHARE)
         cuts = (2 * CHUNK, 3 * CHUNK, T - CHUNK // 2, T)
         for lo, hi in zip(cuts, cuts[1:]):
             round_columns(nc.scalar.copy, last, lo, hi)

@@ -101,9 +101,9 @@ def tile_list_rgg_ownLP_kernel(
             nc.gpsimd.memset(window[:], 0.0)
 
         load_weight("wa", wa, 2)
-        load_state(0)
+        load_state(1)
         load_weight("wo", wo, 2)
-        for s in range(1, PACK):
+        for s in (0, 2, 3):
             load_state(s)
 
         picked_plane = {}
@@ -118,9 +118,8 @@ def tile_list_rgg_ownLP_kernel(
                 picked_codes[name, h][:], tab_codes[:].bitcast(U32).indirect(lst[:, 32 * h : 32 * (h + 1)])
             )
 
-        first = held("first", [P, J], F32)
-        wg_front = first[:, J - FRONT :]
-        wg_row = held("wg_row", [P, J], F32)[:]
+        first = held("first", [P, 2 * J - FRONT], F32)
+        wg_row = first[:, J - FRONT :]
         wg_col = held("wg_col", [P, EDGE_TILES], F32)
         wg_turned = bank("turn0")
         nc.tensor.transpose(wg_turned[:, 0:P], wg_cut[:], ident[:])
@@ -131,8 +130,6 @@ def tile_list_rgg_ownLP_kernel(
                 e = PACK * h + i
                 nc.tensor.transpose(spread[:, tile_cols(i)], wg_col[:, e : e + 1].to_broadcast([P, P]), ident[:])
             nc.scalar.copy(wg_row[:, half_cols(h)], spread[:])
-            if h == 0:
-                nc.scalar.copy(wg_front, spread[:, 0:FRONT])
 
         grouped = {}
         w_codes = {}
@@ -250,47 +247,46 @@ def tile_list_rgg_ownLP_kernel(
         for h in range(2):
             message[0, h] = room_m[h]
             message_of(0, h)
-        picked[0] = held("picked0", [P, J], F32)[:]
-        nc.vector.tensor_copy(picked[0], listed(state[0], 0, J))
+        picked[1] = held("picked1", [P, J], F32)[:]
+        nc.vector.tensor_tensor(picked[1], listed(state[1], 0, J), wg_row, MULT)
         round_weight("wo")
         quantise_weight("wo")
-        picked[1] = held("picked1", [P, J], F32, "grouped_wo")[:]
-        nc.vector.tensor_copy(picked[1], listed(state[1], 0, J))
+        picked[0] = held("picked0", [P, J], F32, "grouped_wo")[:]
+        nc.vector.tensor_copy(picked[0], listed(state[0], 0, J))
 
         room_e, room_g, room_b, room_o = two_halves("room_e", "raw_wo1"), two_halves("room_g"), two_halves("room_b"), two_halves("room_o")
         room_n = two_halves("room_n")
         for h in range(2):
             eta[0, h], gated[0, h], residual[0, h], own[0, h] = room_e[h], room_g[h], room_b[h], room_o[h]
-            eta[1, h], message[1, h], residual[1, h], own[1, h] = room_b[h], room_g[h], room_o[h], room_e[h]
+            eta[1, h], message[1, h], sums[1, h], own[1, h] = room_b[h], room_g[h], room_o[h], room_e[h]
             eta[2, h], message[2, h], own[2, h] = room_m[h], room_n[h], room_b[h]
-            sums[3, h] = room_n[h]
         for h in range(2):
             gate_of(0, h)
             let_through(0, h)
         for h in range(2):
-            residual_of(0, h)
-        for h in range(2):
             own_of(0, h)
+        for h in range(2):
+            residual_of(0, h)
 
         picked[2] = held("picked2", [P, J], F32)[:]
-        nc.vector.tensor_copy(picked[2], listed(state[2], 0, J))
+        nc.vector.tensor_tensor(picked[2], listed(state[2], 0, J), wg_row, MULT)
         picked[3] = held("picked3", [P, J], F32)[:]
-        nc.vector.tensor_tensor(picked[3][:, 0:FRONT], listed(state[3], 0, FRONT), wg_front, MULT)
-        totals[0] = first[:]
+        nc.vector.tensor_tensor(picked[3][:, 0:FRONT], listed(state[3], 0, FRONT), wg_row[:, 0:FRONT], MULT)
+        totals[0] = first[:, 0:J]
         for h in range(2):
-            turn_and_add(totals[0][:, half_cols(h)], (residual[0, h], gated[0, h], own[0, h]), h)
+            turn_and_add(totals[0][:, half_cols(h)], (own[0, h], gated[0, h], residual[0, h]), h)
         nc.vector.tensor_tensor(picked[3][:, FRONT:J], listed(state[3], FRONT, J), wg_row[:, FRONT:J], MULT)
         scatter_total(0)
         y_rows = out_0.rearrange("(p t) c -> t p c", t=PACK)
         nc.sync.dma_start(out=y_rows[ORDER[0]], in_=windows[0][:])
 
-        late = held("late", [P, 3, J], F32, "state3")
+        late = held("late", [P, 2, J], F32, "state3")
         second = held("second", [P, 2, J], F32, "state0")
         third = held("third", [P, 2, J], F32, "state1")
-        totals[1], totals[2], totals[3] = second[:, 0, :], third[:, 0, :], third[:, 1, :]
+        totals[1], totals[2], last_sums = second[:, 0, :], third[:, 0, :], third[:, 1, :]
         for h in range(2):
             gated[1, h], gated[2, h] = late[:, 0, half_cols(h)], late[:, 1, half_cols(h)]
-            sums[2, h] = second[:, 1, half_cols(h)]
+            sums[2, h], sums[3, h] = second[:, 1, half_cols(h)], last_sums[:, half_cols(h)]
 
         for h in range(2):
             gate_of(1, h)
@@ -298,31 +294,28 @@ def tile_list_rgg_ownLP_kernel(
             let_through(1, h)
         for h in range(2):
             own_of(1, h)
-            residual_of(1, h)
         for h in range(2):
-            turn_and_add(totals[1][:, half_cols(h)], (residual[1, h], own[1, h], gated[1, h]), h)
+            turn_and_add(sums[1, h], (own[1, h], gated[1, h]), h)
+            add_state(1, h)
         scatter_total(1)
         nc.sync.dma_start(out=y_rows[ORDER[1]], in_=windows[1][:])
         pairs = held("pairs", [P, 2, SHARE], F32)
-        rows = held("rows", [P, PACK - 1, (T - SHARE) // 2], F32, "grouped_wo")
-        for h in range(2):
-            gated[3, h], own[3, h] = pairs[:, 0, half_cols(h)], pairs[:, 1, half_cols(h)]
+        rows = held("rows", [P, PACK - 1, (T - SHARE) // 2], F32, "picked1")
+        flat = pairs[:].rearrange("p u c -> p (u c)")
+        own[3, 0], gated[3, 0] = flat[:, 0:HALF], flat[:, 3 * HALF :]
+        own[3, 1] = flat[:, SHARE - HALF // 2 : SHARE + HALF // 2]
         eta[3, 0], message[3, 0] = room_g[0], room_o[0]
-        message[3, 1], eta[3, 1], sums[3, 1] = [rows[:, ORDER[s], :] for s in range(PACK - 1)]
+        message[3, 1], eta[3, 1], gated[3, 1] = [rows[:, ORDER[s], :] for s in range(PACK - 1)]
         for s in (2, 3):
             for h in range(2):
                 gate_of(s, h)
                 message_of(s, h)
                 let_through(s, h)
                 own_of(s, h)
-            if s == 2:
-                weighted = late[:, 2, :]
-                for h in range(2):
-                    nc.gpsimd.tensor_tensor(weighted[:, half_cols(h)], picked[s][:, half_cols(h)], wg_row[:, half_cols(h)], MULT)
-                picked[s] = weighted
             for h in range(2):
                 turn_and_add(sums[s, h], (own[s, h], gated[s, h]), h)
-                add_state(s, h)
+                if s == 2:
+                    add_state(s, h)
             if s == 2:
                 scatter_total(s)
                 nc.sync.dma_start(out=y_rows[ORDER[s]], in_=windows[s][:])
@@ -345,24 +338,18 @@ def tile_list_rgg_ownLP_kernel(
                 pairs[:].rearrange("p u c -> p c u")[:, lo:hi],
             )
 
-        for s in range(PACK - 1):
+        for s in range(2):
             round_pairs(nc.scalar.copy, s, 0, SHARE)
-            for lo in (0, CHUNK):
-                nc.gpsimd.tensor_scalar(
-                    rows[:, ORDER[s], :].bitcast(BF16)[:, lo : lo + CHUNK],
-                    windows[s][:, SHARE + lo : SHARE + lo + CHUNK],
-                    1.0,
-                    0.0,
-                    MULT,
-                    ADD,
-                )
+            nc.gpsimd.tensor_scalar(rows[:, ORDER[s], :].bitcast(BF16), windows[s][:, SHARE:T], 1.0, 0.0, MULT, ADD)
+        nc.scalar.copy(rows[:, ORDER[2], :].bitcast(BF16), windows[2][:, SHARE:T])
+        round_pairs(nc.scalar.copy, 2, 0, SHARE)
         for lo in (0, CHUNK):
             nc.scalar.copy(
                 rounded[:, SHARE + lo : SHARE + lo + CHUNK, 0 : PACK - 1],
                 rows[:].bitcast(BF16).rearrange("p t c -> p c t")[:, lo : lo + CHUNK],
             )
         last = PACK - 1
-        scatter_total(last)
+        nc.vector.tensor_tensor(listed(windows[0], 0, J), picked[last], last_sums, ADD)
         nc.sync.dma_start(out=y_rows[ORDER[last]], in_=windows[0][:])
         round_pairs(nc.vector.tensor_copy, last, 0, CHUNK)
         round_pairs(nc.vector.tensor_copy, last, CHUNK, SHARE)

@@ -60,11 +60,14 @@ def tile_list_rgg_ownLP_kernel(
         wc_rows = held("wc_rows", [P, N], U8)
         wc_raw = held("wc_raw", [P, 2 * N], U8)
         wg_cut = held("wg_cut", [P, P], F32)
-        nc.gpsimd.memset(tab_plane[:].bitcast(I32), 0)
         nc.gpsimd.memset(wg_cut[:], 0.0)
         nc.gpsimd.memset(wc_rows[:].bitcast(I32), 0)
         nc.sync.dma_start(src[:], offs)
-        load_scale_rows(tab_plane, tab_scales[0])
+        for q in range(4):
+            nc.sync.dma_start(
+                out=tab_plane[32 * q : 32 * (q + 1), :].bitcast(I32),
+                in_=tab_scales[0].bitcast(I32)[4 * q : 4 * q + 4, :].unsqueeze(0).to_broadcast([8, 4, T // 4]),
+            )
         nc.sync.dma_start(dst[:], offs2)
         nc.sync.dma_start(out=wg_cut[0:EDGE_TILES, :], in_=wgo[0].rearrange("(e j) -> e j", j=P))
         raw = {}
@@ -254,8 +257,10 @@ def tile_list_rgg_ownLP_kernel(
         picked[0] = held("picked0", [P, J], F32, "grouped_wo")[:]
         nc.vector.tensor_copy(picked[0], listed(state[0], 0, J))
 
-        room_e, room_g, room_b, room_o = two_halves("room_e", "raw_wo1"), two_halves("room_g"), two_halves("room_b"), two_halves("room_o")
+        room_e, room_g, room_b = two_halves("room_e", "raw_wo1"), two_halves("room_g"), two_halves("room_b")
         room_n = two_halves("room_n")
+        across = held("across", [P, 3 * HALF], F32)
+        room_o = [across[:, J:], across[:, HALF // 2 : 3 * HALF // 2]]
         for h in range(2):
             eta[0, h], gated[0, h], residual[0, h], own[0, h] = room_e[h], room_g[h], room_b[h], room_o[h]
             eta[1, h], message[1, h], sums[1, h], own[1, h] = room_b[h], room_g[h], room_o[h], room_e[h]
@@ -280,13 +285,13 @@ def tile_list_rgg_ownLP_kernel(
         y_rows = out_0.rearrange("(p t) c -> t p c", t=PACK)
         nc.sync.dma_start(out=y_rows[ORDER[0]], in_=windows[0][:])
 
-        late = held("late", [P, 2, J], F32, "state3")
+        late = held("late", [P, J], F32, "state3")
         second = held("second", [P, 2, J], F32, "state0")
         third = held("third", [P, 2, J], F32, "state1")
         totals[1], totals[2], last_sums = second[:, 0, :], third[:, 0, :], third[:, 1, :]
         for h in range(2):
-            gated[1, h], gated[2, h] = late[:, 0, half_cols(h)], late[:, 1, half_cols(h)]
-            sums[2, h], sums[3, h] = second[:, 1, half_cols(h)], last_sums[:, half_cols(h)]
+            gated[1, h], gated[2, h] = late[:, half_cols(h)], across[:, half_cols(h)]
+            sums[3, h] = last_sums[:, half_cols(h)]
 
         for h in range(2):
             gate_of(1, h)
@@ -301,9 +306,9 @@ def tile_list_rgg_ownLP_kernel(
         nc.sync.dma_start(out=y_rows[ORDER[1]], in_=windows[1][:])
         pairs = held("pairs", [P, 2, SHARE], F32)
         rows = held("rows", [P, PACK - 1, (T - SHARE) // 2], F32, "picked1")
-        flat = pairs[:].rearrange("p u c -> p (u c)")
-        own[3, 0], gated[3, 0] = flat[:, 0:HALF], flat[:, 3 * HALF :]
-        own[3, 1] = flat[:, SHARE - HALF // 2 : SHARE + HALF // 2]
+        for h in range(2):
+            own[3, h], sums[2, h] = pairs[:, 0, half_cols(h)], pairs[:, 1, half_cols(h)]
+        gated[3, 0] = second[:, 1, 0:HALF]
         eta[3, 0], message[3, 0] = room_g[0], room_o[0]
         message[3, 1], eta[3, 1], gated[3, 1] = [rows[:, ORDER[s], :] for s in range(PACK - 1)]
         for s in (2, 3):

@@ -99,7 +99,7 @@ def tile_list_rgg_ownLP_kernel(
 
         ident = held("ident", [P, P], F32)
         make_identity(nc, ident[:])
-        windows = [held("window%d" % i, [P, T], F32) for i in range(3)]
+        windows = [held("window%d" % i, [P, T], F32) for i in range(2)]
         for window in windows:
             nc.gpsimd.memset(window[:], 0.0)
 
@@ -273,6 +273,8 @@ def tile_list_rgg_ownLP_kernel(
         for h in range(2):
             residual_of(0, h)
 
+        windows.append(held("window2", [P, T], F32, "state0"))
+        nc.gpsimd.memset(windows[2][:], 0.0)
         picked[2] = held("picked2", [P, J], F32)[:]
         nc.vector.tensor_tensor(picked[2], listed(state[2], 0, J), wg_row, MULT)
         picked[3] = held("picked3", [P, J], F32)[:]
@@ -286,7 +288,7 @@ def tile_list_rgg_ownLP_kernel(
         nc.sync.dma_start(out=y_rows[ORDER[0]], in_=windows[0][:])
 
         late = held("late", [P, J], F32, "state3")
-        second = held("second", [P, 2, J], F32, "state0")
+        second = held("second", [P, 2, J], F32)
         third = held("third", [P, 2, J], F32, "state1")
         totals[1], totals[2], last_sums = second[:, 0, :], third[:, 0, :], third[:, 1, :]
         for h in range(2):

@@ -239,8 +239,8 @@ def tile_list_rgg_ownLP_kernel(
         def add_state(s, h):
             nc.gpsimd.tensor_tensor(totals[s][:, half_cols(h)], picked[s][:, half_cols(h)], sums[s, h], ADD)
 
-        def scatter_total(s):
-            nc.vector.tensor_copy(listed(windows[s % 3], 0, J), totals[s])
+        def scatter_total(s, lo, hi):
+            nc.vector.tensor_copy(listed(windows[s], lo, hi), totals[s][:, lo:hi])
 
         def two_halves(name, tag=None):
             tile = held(name, [P, J], F32, tag)
@@ -258,13 +258,11 @@ def tile_list_rgg_ownLP_kernel(
         nc.vector.tensor_copy(picked[0], listed(state[0], 0, J))
 
         room_e, room_g, room_b = two_halves("room_e", "raw_wo1"), two_halves("room_g"), two_halves("room_b")
-        room_n = two_halves("room_n")
-        across = held("across", [P, 3 * HALF], F32)
-        room_o = [across[:, J:], across[:, HALF // 2 : 3 * HALF // 2]]
+        room_n, room_o = two_halves("room_n"), two_halves("room_o")
         for h in range(2):
             eta[0, h], gated[0, h], residual[0, h], own[0, h] = room_e[h], room_g[h], room_b[h], room_o[h]
-            eta[1, h], message[1, h], sums[1, h], own[1, h] = room_b[h], room_g[h], room_o[h], room_e[h]
-            eta[2, h], message[2, h], own[2, h] = room_m[h], room_n[h], room_b[h]
+            eta[1, h], message[1, h], own[1, h] = room_b[h], room_g[h], room_e[h]
+            eta[2, h], message[2, h], own[2, h] = room_m[h], room_n[h], room_o[h]
         for h in range(2):
             gate_of(0, h)
             let_through(0, h)
@@ -283,49 +281,44 @@ def tile_list_rgg_ownLP_kernel(
         for h in range(2):
             turn_and_add(totals[0][:, half_cols(h)], (own[0, h], gated[0, h], residual[0, h]), h)
         nc.vector.tensor_tensor(picked[3][:, FRONT:J], listed(state[3], FRONT, J), wg_row[:, FRONT:J], MULT)
-        scatter_total(0)
+        scatter_total(0, 0, J)
         y_rows = out_0.rearrange("(p t) c -> t p c", t=PACK)
         nc.sync.dma_start(out=y_rows[ORDER[0]], in_=windows[0][:])
 
-        late = held("late", [P, J], F32, "state3")
+        late = held("late", [P, 2, J], F32, "state3")
         second = held("second", [P, 2, J], F32)
         third = held("third", [P, 2, J], F32, "state1")
+        pairs = held("pairs", [P, 2, SHARE], F32)
+        under_rows = held("under_rows", [P, PACK - 1, J], F32)
+        rows = under_rows[:, :, HALF // 2 : 3 * HALF // 2]
         totals[1], totals[2], last_sums = second[:, 0, :], third[:, 0, :], third[:, 1, :]
         for h in range(2):
-            gated[1, h], gated[2, h] = late[:, half_cols(h)], across[:, half_cols(h)]
-            sums[3, h] = last_sums[:, half_cols(h)]
+            gated[1, h], gated[2, h] = late[:, 0, half_cols(h)], late[:, 1, half_cols(h)]
+            own[3, h], sums[3, h] = pairs[:, 0, half_cols(h)], last_sums[:, half_cols(h)]
+        sums[2, 0], eta[3, 0] = pairs[:, 1, half_cols(0)], pairs[:, 1, half_cols(1)]
+        gated[3, 0], message[3, 0] = second[:, 1, half_cols(0)], second[:, 1, half_cols(1)]
+        sums[1, 0], sums[1, 1] = [under_rows[:, ORDER[0], half_cols(h)] for h in range(2)]
+        eta[3, 1], sums[2, 1] = [under_rows[:, ORDER[1], half_cols(h)] for h in range(2)]
+        gated[3, 1], message[3, 1] = [under_rows[:, ORDER[2], half_cols(h)] for h in range(2)]
 
-        for h in range(2):
-            gate_of(1, h)
-            message_of(1, h)
-            let_through(1, h)
-        for h in range(2):
-            own_of(1, h)
-        for h in range(2):
-            turn_and_add(sums[1, h], (own[1, h], gated[1, h]), h)
-            add_state(1, h)
-        scatter_total(1)
-        nc.sync.dma_start(out=y_rows[ORDER[1]], in_=windows[1][:])
-        pairs = held("pairs", [P, 2, SHARE], F32)
-        rows = held("rows", [P, PACK - 1, (T - SHARE) // 2], F32, "picked1")
-        for h in range(2):
-            own[3, h], sums[2, h] = pairs[:, 0, half_cols(h)], pairs[:, 1, half_cols(h)]
-        gated[3, 0] = second[:, 1, 0:HALF]
-        eta[3, 0], message[3, 0] = room_g[0], room_o[0]
-        message[3, 1], eta[3, 1], gated[3, 1] = [rows[:, ORDER[s], :] for s in range(PACK - 1)]
-        for s in (2, 3):
-            for h in range(2):
-                gate_of(s, h)
-                message_of(s, h)
-                let_through(s, h)
-                own_of(s, h)
-            for h in range(2):
-                turn_and_add(sums[s, h], (own[s, h], gated[s, h]), h)
-                if s == 2:
-                    add_state(s, h)
-            if s == 2:
-                scatter_total(s)
-                nc.sync.dma_start(out=y_rows[ORDER[s]], in_=windows[s][:])
+        steps = [(1, 0), (2, 0), (1, 1), (2, 1), (3, 0), (3, 1)]
+
+        def open_step(s, h):
+            gate_of(s, h)
+            message_of(s, h)
+            let_through(s, h)
+            own_of(s, h)
+
+        open_step(*steps[0])
+        for n, (s, h) in enumerate(steps):
+            if n + 1 < len(steps):
+                open_step(*steps[n + 1])
+            turn_and_add(sums[s, h], (own[s, h], gated[s, h]), h)
+            if s < PACK - 1:
+                add_state(s, h)
+                scatter_total(s, HALF * h, HALF * (h + 1))
+                if h == 1:
+                    nc.sync.dma_start(out=y_rows[ORDER[s]], in_=windows[s][:])
 
         rounded = held("rounded", [P, T, PACK], BF16)
         y_codes = held("y_codes", [P, T], I32)
@@ -353,7 +346,7 @@ def tile_list_rgg_ownLP_kernel(
         for lo in (0, CHUNK):
             nc.scalar.copy(
                 rounded[:, SHARE + lo : SHARE + lo + CHUNK, 0 : PACK - 1],
-                rows[:].bitcast(BF16).rearrange("p t c -> p c t")[:, lo : lo + CHUNK],
+                rows.bitcast(BF16).rearrange("p t c -> p c t")[:, lo : lo + CHUNK],
             )
         last = PACK - 1
         nc.vector.tensor_tensor(listed(windows[0], 0, J), picked[last], last_sums, ADD)

@@ -197,7 +197,7 @@ def tile_list_rgg_ownLP_kernel(
                 nc.scalar.activation(out[:, tile_cols(i)], source[:, tile_cols(i)], COPY, scale=wg_col[:, e : e + 1])
 
         def gate_of(s, h):
-            za = bank("gate%d" % h)
+            za = bank("%s%d" % ("turn" if s else "gate", h))
             for i in range(PACK):
                 product(za[:, tile_cols(i)], "src", PACK * h + i, "wb", ORDER[s], True, False)
                 product(za[:, tile_cols(i)], "dst", PACK * h + i, "wa", ORDER[s], False, True)
@@ -210,7 +210,7 @@ def tile_list_rgg_ownLP_kernel(
             copy_weighted(message[s, h], ms, h)
 
         def own_of(s, h):
-            ow = bank("own%d" % h)
+            ow = bank("%s%d" % ("own" if s < 2 else "message", h))
             for i in range(PACK):
                 product(ow[:, tile_cols(i)], "dst", PACK * h + i, "wo", ORDER[s], True, True)
             copy_weighted(own[s, h], ow, h)
@@ -224,8 +224,8 @@ def tile_list_rgg_ownLP_kernel(
         def let_through(s, h):
             nc.gpsimd.tensor_tensor(gated[s, h], message[s, h], eta[s, h], MULT)
 
-        def turn_and_add(out, parts, h):
-            turned = bank("turn%d" % h)
+        def turn_and_add(out, parts, h, tag):
+            turned = bank("%s%d" % (tag, h))
             for n, part in enumerate(parts):
                 for i in range(PACK):
                     cols = tile_cols(i)
@@ -255,7 +255,8 @@ def tile_list_rgg_ownLP_kernel(
         round_weight("wo")
         quantise_weight("wo")
         picked[0] = held("picked0", [P, J], F32, "grouped_wo")[:]
-        nc.vector.tensor_copy(picked[0], listed(state[0], 0, J))
+        for h in range(2):
+            nc.vector.tensor_copy(picked[0][:, half_cols(h)], listed(state[0], HALF * h, HALF * (h + 1)))
 
         room_e, room_g, room_b = two_halves("room_e", "raw_wo1"), two_halves("room_g"), two_halves("room_b")
         room_n, room_o = two_halves("room_n"), two_halves("room_o")
@@ -279,7 +280,7 @@ def tile_list_rgg_ownLP_kernel(
         nc.vector.tensor_tensor(picked[3][:, 0:FRONT], listed(state[3], 0, FRONT), wg_row[:, 0:FRONT], MULT)
         totals[0] = first[:, 0:J]
         for h in range(2):
-            turn_and_add(totals[0][:, half_cols(h)], (own[0, h], gated[0, h], residual[0, h]), h)
+            turn_and_add(totals[0][:, half_cols(h)], (own[0, h], gated[0, h], residual[0, h]), h, "turn")
         nc.vector.tensor_tensor(picked[3][:, FRONT:J], listed(state[3], FRONT, J), wg_row[:, FRONT:J], MULT)
         scatter_total(0, 0, J)
         y_rows = out_0.rearrange("(p t) c -> t p c", t=PACK)
@@ -313,7 +314,8 @@ def tile_list_rgg_ownLP_kernel(
         for n, (s, h) in enumerate(steps):
             if n + 1 < len(steps):
                 open_step(*steps[n + 1])
-            turn_and_add(sums[s, h], (own[s, h], gated[s, h]), h)
+            parts = (gated[s, h], own[s, h]) if s < PACK - 1 else (own[s, h], gated[s, h])
+            turn_and_add(sums[s, h], parts, h, "gate" if s % 2 else "own")
             if s < PACK - 1:
                 add_state(s, h)
                 scatter_total(s, HALF * h, HALF * (h + 1))
@@ -345,8 +347,8 @@ def tile_list_rgg_ownLP_kernel(
         round_pairs(nc.scalar.copy, 2, 0, SHARE)
         for lo in (0, CHUNK):
             nc.scalar.copy(
-                rounded[:, SHARE + lo : SHARE + lo + CHUNK, 0 : PACK - 1],
-                rows.bitcast(BF16).rearrange("p t c -> p c t")[:, lo : lo + CHUNK],
+                rounded[:, SHARE + lo : SHARE + lo + CHUNK, 0 : PACK - 1].rearrange("p (c i) t -> p c t i", i=PACK),
+                rows.bitcast(BF16)[:, :, lo : lo + CHUNK].rearrange("p t (c i) -> p c t i", i=PACK),
             )
         last = PACK - 1
         nc.vector.tensor_tensor(listed(windows[0], 0, J), picked[last], last_sums, ADD)

@@ -68,17 +68,12 @@ def tile_list_rgg_ownLP_kernel(
                 out=tab_plane[32 * q : 32 * (q + 1), :].bitcast(I32),
                 in_=tab_scales[0].bitcast(I32)[4 * q : 4 * q + 4, :].unsqueeze(0).to_broadcast([8, 4, T // 4]),
             )
-        nc.sync.dma_start(dst[:], offs2)
-        nc.sync.dma_start(out=wg_cut[0:EDGE_TILES, :], in_=wgo[0].rearrange("(e j) -> e j", j=P))
         raw = {}
 
-        def load_weight(name, w, parts):
-            rows = w.rearrange("(p i) n -> p i n", i=PACK)
-            width = N // parts
-            raw[name] = []
-            for h in range(parts):
-                raw[name].append(held("raw_%s%d" % (name, h), [P, PACK, width], F32))
-                nc.sync.dma_start(out=raw[name][h][:], in_=rows[:, :, width * h : width * (h + 1)])
+        def load_part(name, w, lo, hi):
+            part = held("raw_%s%d" % (name, lo), [P, PACK, hi - lo], F32)
+            nc.sync.dma_start(out=part[:], in_=w.rearrange("(p i) n -> p i n", i=PACK)[:, :, lo:hi])
+            raw.setdefault(name, []).append((lo, hi, part))
 
         r_rows = rT.rearrange("(p t) c -> t p c", t=PACK)
         state = {}
@@ -87,10 +82,12 @@ def tile_list_rgg_ownLP_kernel(
             state[s] = held("state%d" % s, [P, T], F32)
             nc.sync.dma_start(out=state[s][:], in_=r_rows[ORDER[s]])
 
-        load_weight("wb", wb, 1)
+        nc.sync.dma_start(dst[:], offs2)
+        load_part("wb", wb, 0, N)
+        nc.sync.dma_start(out=tab_codes[:], in_=tab_words[0].rearrange("p t i -> p (t i)").bitcast(I32))
+        nc.sync.dma_start(out=wg_cut[0:EDGE_TILES, :], in_=wgo[0].rearrange("(e j) -> e j", j=P))
         nc.sync.dma_start(out=wc_raw[:].bitcast(I32), in_=wc_words[0].bitcast(I32))
         load_scale_rows(wc_rows, wc_scales[0])
-        nc.sync.dma_start(out=tab_codes[:], in_=tab_words[0].rearrange("p t i -> p (t i)").bitcast(I32))
 
         warm_in = held("warm_in", [P, 1], F32)
         warm_out = held("warm_out", [P, 1], F32)
@@ -103,9 +100,12 @@ def tile_list_rgg_ownLP_kernel(
         for window in windows:
             nc.gpsimd.memset(window[:], 0.0)
 
-        load_weight("wa", wa, 2)
+        load_part("wa", wa, 0, N // 2)
+        load_part("wa", wa, N // 2, N)
+        load_part("wo", wo, 0, N // 2)
         load_state(1)
-        load_weight("wo", wo, 2)
+        load_part("wo", wo, N // 2, 3 * N // 4)
+        load_part("wo", wo, 3 * N // 4, N)
         for s in (0, 2, 3):
             load_state(s)
 
@@ -140,15 +140,14 @@ def tile_list_rgg_ownLP_kernel(
 
         def round_weight(name):
             grouped[name] = held("grouped_" + name, [P, N, PACK], BF16)
-            share = P // len(raw[name])
-            for h, part in enumerate(raw[name]):
+            for lo, hi, part in raw[name]:
                 nc.scalar.copy(
-                    grouped[name][:].rearrange("p (t m) i -> p m i t", t=PACK)[:, share * h : share * (h + 1)],
+                    grouped[name][:].rearrange("p (t m) i -> p m i t", t=PACK)[:, lo // PACK : hi // PACK],
                     part[:].rearrange("p i (m t) -> p m i t", t=PACK),
                 )
 
-        def quantise_weight(name):
-            w_codes[name] = held("wcodes_" + name, [P, N], U32)
+        def quantise_weight(name, tag=None):
+            w_codes[name] = held("wcodes_" + name, [P, N], U32, tag)
             w_plane[name] = held("wplane_" + name, [P, N], U8)
             nc.vector.quantize_mx(
                 out=w_codes[name][:].bitcast(FP8X4),
@@ -157,21 +156,20 @@ def tile_list_rgg_ownLP_kernel(
             )
 
         round_weight("wb")
-        gather_codes("src", src, 0)
-        gather_codes("dst", dst, 0)
-        gather_codes("src", src, 1)
-        quantise_weight("wb")
-        gather_codes("dst", dst, 1)
+        for name, lst in (("src", src), ("dst", dst)):
+            for h in range(2):
+                gather_codes(name, lst, h)
         w_plane["wc"] = held("wc_plane", [P, N], U8)
         wc_codes = held("wc_codes", [P, 2 * N], U8)
         nc.scalar.copy(
             wc_codes[:].bitcast(U16).rearrange("p (t m) -> p t m", t=PACK),
             wc_raw[:].bitcast(U16).rearrange("p (m t) -> p t m", t=PACK),
         )
-        nc.vector.tensor_copy(
+        nc.gpsimd.tensor_copy(
             w_plane["wc"][:].rearrange("p (t m) -> p t m", t=PACK), wc_rows[:].rearrange("p (m t) -> p t m", t=PACK)
         )
         round_weight("wa")
+        quantise_weight("wb", "raw_wa0")
         quantise_weight("wa")
 
         def product(out, side, e, name, t, start, stop):
@@ -246,10 +244,8 @@ def tile_list_rgg_ownLP_kernel(
             tile = held(name, [P, J], F32, tag)
             return [tile[:, half_cols(h)] for h in range(2)]
 
-        room_m = two_halves("room_m", "raw_wa1")
-        for h in range(2):
-            message[0, h] = room_m[h]
-            message_of(0, h)
+        message[0, 0] = held("first_message", [P, HALF], F32, "raw_wa256")[:]
+        message_of(0, 0)
         picked[1] = held("picked1", [P, J], F32)[:]
         nc.vector.tensor_tensor(picked[1], listed(state[1], 0, J), wg_row, MULT)
         round_weight("wo")
@@ -258,15 +254,21 @@ def tile_list_rgg_ownLP_kernel(
         for h in range(2):
             nc.vector.tensor_copy(picked[0][:, half_cols(h)], listed(state[0], HALF * h, HALF * (h + 1)))
 
-        room_e, room_g, room_b = two_halves("room_e", "raw_wo1"), two_halves("room_g"), two_halves("room_b")
+        behind_wo = held("behind_wo", [P, 3, HALF], F32, "raw_wo384")
+        room_e = [behind_wo[:, h, :] for h in range(2)]
+        message[0, 1] = behind_wo[:, 2, :]
+        room_m = [message[0, h] for h in range(2)]
+        room_g, room_b = two_halves("room_g"), two_halves("room_b")
         room_n, room_o = two_halves("room_n"), two_halves("room_o")
         for h in range(2):
             eta[0, h], gated[0, h], residual[0, h], own[0, h] = room_e[h], room_g[h], room_b[h], room_o[h]
             eta[1, h], message[1, h], own[1, h] = room_b[h], room_g[h], room_e[h]
             eta[2, h], message[2, h], own[2, h] = room_m[h], room_n[h], room_o[h]
-        for h in range(2):
-            gate_of(0, h)
-            let_through(0, h)
+        gate_of(0, 0)
+        let_through(0, 0)
+        message_of(0, 1)
+        gate_of(0, 1)
+        let_through(0, 1)
         for h in range(2):
             own_of(0, h)
         for h in range(2):

@@ -83,9 +83,9 @@ def tile_list_rgg_ownLP_kernel(
             nc.sync.dma_start(out=state[s][:], in_=r_rows[ORDER[s]])
 
         nc.sync.dma_start(dst[:], offs2)
+        nc.sync.dma_start(out=wg_cut[0:EDGE_TILES, :], in_=wgo[0].rearrange("(e j) -> e j", j=P))
         load_part("wb", wb, 0, N)
         nc.sync.dma_start(out=tab_codes[:], in_=tab_words[0].rearrange("p t i -> p (t i)").bitcast(I32))
-        nc.sync.dma_start(out=wg_cut[0:EDGE_TILES, :], in_=wgo[0].rearrange("(e j) -> e j", j=P))
         nc.sync.dma_start(out=wc_raw[:].bitcast(I32), in_=wc_words[0].bitcast(I32))
         load_scale_rows(wc_rows, wc_scales[0])
 

@@ -24,7 +24,7 @@ PACK = 4
 EDGE_TILES = J // P
 HALF = J // 2
 CHUNK = 512
-ORDER = (2, 0, 1, 3)
+ORDER = (2, 1, 0, 3)
 SHARE = 1024
 FRONT = 384
 
@@ -222,13 +222,14 @@ def tile_list_rgg_ownLP_kernel(
         def let_through(s, h):
             nc.gpsimd.tensor_tensor(gated[s, h], message[s, h], eta[s, h], MULT)
 
-        def turn_and_add(out, parts, h, tag):
+        def turn_and_add(out, parts, h, tag, first_last=False):
             turned = bank("%s%d" % (tag, h))
-            for n, part in enumerate(parts):
-                for i in range(PACK):
-                    cols = tile_cols(i)
-                    begin, final = n == 0 and i == 0, n == len(parts) - 1 and i == PACK - 1
-                    nc.tensor.matmul(turned[:, cols], part[:, cols], ident[:], start=begin, stop=final, is_transpose=True)
+            terms = [(part, tile_cols(i)) for part in parts for i in range(PACK)]
+            if first_last:
+                terms.append(terms.pop(PACK - 1))
+            for n, (part, cols) in enumerate(terms):
+                begin, final = n == 0, n == len(terms) - 1
+                nc.tensor.matmul(turned[:, cols], part[:, cols], ident[:], start=begin, stop=final, is_transpose=True)
             nc.scalar.copy(out, turned[:])
 
         def listed(tile, lo, hi):
@@ -292,17 +293,19 @@ def tile_list_rgg_ownLP_kernel(
         second = held("second", [P, 2, J], F32)
         third = held("third", [P, 2, J], F32, "state1")
         pairs = held("pairs", [P, 2, SHARE], F32)
-        under_rows = held("under_rows", [P, PACK - 1, J], F32)
-        rows = under_rows[:, :, HALF // 2 : 3 * HALF // 2]
+        ahead = HALF - P
+        under_rows = held("under_rows", [P, ahead + (PACK - 1) * HALF], F32)
+        rows = under_rows[:, ahead:].rearrange("p (t c) -> p t c", c=HALF)
+        spare = held("spare", [P, 5, HALF], F32)
         totals[1], totals[2], last_sums = second[:, 0, :], third[:, 0, :], third[:, 1, :]
         for h in range(2):
             gated[1, h], gated[2, h] = late[:, 0, half_cols(h)], late[:, 1, half_cols(h)]
-            own[3, h], sums[3, h] = pairs[:, 0, half_cols(h)], last_sums[:, half_cols(h)]
-        sums[2, 0], eta[3, 0] = pairs[:, 1, half_cols(0)], pairs[:, 1, half_cols(1)]
+            sums[3, h] = last_sums[:, half_cols(h)]
+        own[3, 0], gated[3, 1] = pairs[:, 0, half_cols(0)], pairs[:, 1, half_cols(1)]
         gated[3, 0], message[3, 0] = second[:, 1, half_cols(0)], second[:, 1, half_cols(1)]
-        sums[1, 0], sums[1, 1] = [under_rows[:, ORDER[0], half_cols(h)] for h in range(2)]
-        eta[3, 1], sums[2, 1] = [under_rows[:, ORDER[1], half_cols(h)] for h in range(2)]
-        gated[3, 1], message[3, 1] = [under_rows[:, ORDER[2], half_cols(h)] for h in range(2)]
+        sums[1, 0], sums[1, 1], sums[2, 0], sums[2, 1], eta[3, 0] = [spare[:, n, :] for n in range(5)]
+        eta[3, 1] = pairs[:].rearrange("p u c -> p (u c)")[:, 3 * HALF // 2 : 5 * HALF // 2]
+        own[3, 1], message[3, 1] = under_rows[:, 0:HALF], under_rows[:, 2 * HALF - P // 2 : 3 * HALF - P // 2]
 
         steps = [(1, 0), (2, 0), (1, 1), (2, 1), (3, 0), (3, 1)]
 
@@ -317,7 +320,7 @@ def tile_list_rgg_ownLP_kernel(
             if n + 1 < len(steps):
                 open_step(*steps[n + 1])
             parts = (gated[s, h], own[s, h]) if s < PACK - 1 else (own[s, h], gated[s, h])
-            turn_and_add(sums[s, h], parts, h, "gate" if s % 2 else "own")
+            turn_and_add(sums[s, h], parts, h, "gate" if s % 2 else "own", n + 1 == len(steps))
             if s < PACK - 1:
                 add_state(s, h)
                 scatter_total(s, HALF * h, HALF * (h + 1))
@@ -336,15 +339,20 @@ def tile_list_rgg_ownLP_kernel(
             halves = pairs[:].bitcast(BF16).rearrange("p u (c e) -> p u c e", e=2)
             move(halves[:, ORDER[s] // 2, lo:hi, ORDER[s] % 2], windows[s % 3][:, lo:hi])
 
+        def round_on_gpsimd(out, source):
+            nc.gpsimd.tensor_scalar(out, source, 1.0, 0.0, MULT, ADD)
+
         def weave(lo, hi):
             nc.vector.tensor_copy(
                 rounded[:, lo:hi, :].rearrange("p c i -> p (c i)").bitcast(F32).rearrange("p (c u) -> p c u", u=2),
                 pairs[:].rearrange("p u c -> p c u")[:, lo:hi],
             )
 
+        round_pairs(nc.scalar.copy, 0, 0, CHUNK)
+        round_pairs(nc.scalar.copy, 1, 0, SHARE)
         for s in range(2):
-            round_pairs(nc.scalar.copy, s, 0, SHARE)
             nc.gpsimd.tensor_scalar(rows[:, ORDER[s], :].bitcast(BF16), windows[s][:, SHARE:T], 1.0, 0.0, MULT, ADD)
+        round_pairs(round_on_gpsimd, 0, CHUNK, SHARE)
         nc.scalar.copy(rows[:, ORDER[2], :].bitcast(BF16), windows[2][:, SHARE:T])
         round_pairs(nc.scalar.copy, 2, 0, SHARE)
         for lo in (0, CHUNK):

@@ -383,8 +383,9 @@ def tile_list_rgg_ownLP_kernel(
             nc.sync.dma_start(out=code_rows[:, lo:hi], in_=y_codes[:, lo:hi])
 
         quantise_columns(0, CHUNK)
+        store_codes(0, CHUNK)
         quantise_columns(CHUNK, 2 * CHUNK)
-        store_codes(0, 2 * CHUNK)
+        store_codes(CHUNK, 2 * CHUNK)
         quantise_columns(2 * CHUNK, 3 * CHUNK)
         store_codes(2 * CHUNK, 3 * CHUNK)
         quantise_columns(3 * CHUNK, T - CHUNK // 2)

@@ -38,7 +38,7 @@ def tile_list_rgg_ownLP_kernel(
         psum = ctx.enter_context(tc.psum_pool(name="psum", bufs=1))
 
         def held(name, shape, dtype, tag=None):
-            return keep.tile(shape, dtype, name=name, tag=tag or name, align_bytes=64)
+            return keep.tile(shape, dtype, name=name, tag=tag or name, align_bytes=256)
 
         def bank(tag):
             return psum.tile([P, HALF], F32, name=tag, tag=tag)

@@ -251,11 +251,11 @@ def tile_list_rgg_ownLP_kernel(
         nc.vector.tensor_tensor(picked[1], listed(state[1], 0, J), wg_row, MULT)
         round_weight("wo")
         quantise_weight("wo")
-        picked[0] = held("picked0", [P, J], F32, "grouped_wo")[:]
+        behind_wo = held("behind_wo", [P, 5, HALF], F32, "raw_wo384")
+        picked[0] = behind_wo[:, 3:5, :].rearrange("p h c -> p (h c)")
         for h in range(2):
             nc.vector.tensor_copy(picked[0][:, half_cols(h)], listed(state[0], HALF * h, HALF * (h + 1)))
 
-        behind_wo = held("behind_wo", [P, 3, HALF], F32, "raw_wo384")
         room_e = [behind_wo[:, h, :] for h in range(2)]
         message[0, 1] = behind_wo[:, 2, :]
         room_m = [message[0, h] for h in range(2)]
@@ -389,8 +389,9 @@ def tile_list_rgg_ownLP_kernel(
         quantise_columns(2 * CHUNK, 3 * CHUNK)
         store_codes(2 * CHUNK, 3 * CHUNK)
         quantise_columns(3 * CHUNK, T - CHUNK // 2)
+        store_codes(3 * CHUNK, T - CHUNK // 2)
         quantise_columns(T - CHUNK // 2, T)
-        store_codes(3 * CHUNK, T)
+        store_codes(T - CHUNK // 2, T)
         scale_rows = out_2[0].bitcast(I32)
         for q in range(4):
             queue = nc.scalar if q % 2 else nc.sync

@@ -100,12 +100,10 @@ def tile_list_rgg_ownLP_kernel(
         for window in windows:
             nc.gpsimd.memset(window[:], 0.0)
 
-        load_part("wa", wa, 0, N // 2)
-        load_part("wa", wa, N // 2, N)
+        load_part("wa", wa, 0, N)
         load_part("wo", wo, 0, N // 2)
         load_state(1)
-        load_part("wo", wo, N // 2, 3 * N // 4)
-        load_part("wo", wo, 3 * N // 4, N)
+        load_part("wo", wo, N // 2, N)
         for s in (0, 2, 3):
             load_state(s)
 
@@ -245,13 +243,13 @@ def tile_list_rgg_ownLP_kernel(
             tile = held(name, [P, J], F32, tag)
             return [tile[:, half_cols(h)] for h in range(2)]
 
-        message[0, 0] = held("first_message", [P, HALF], F32, "raw_wa256")[:]
+        message[0, 0] = held("first_message", [P, HALF], F32, "grouped_wb")[:]
         message_of(0, 0)
         picked[1] = held("picked1", [P, J], F32)[:]
         nc.vector.tensor_tensor(picked[1], listed(state[1], 0, J), wg_row, MULT)
         round_weight("wo")
         quantise_weight("wo")
-        behind_wo = held("behind_wo", [P, 5, HALF], F32, "raw_wo384")
+        behind_wo = held("behind_wo", [P, 5, HALF], F32, "raw_wo256")
         picked[0] = behind_wo[:, 3:5, :].rearrange("p h c -> p (h c)")
         for h in range(2):
             nc.vector.tensor_copy(picked[0][:, half_cols(h)], listed(state[0], HALF * h, HALF * (h + 1)))

@@ -100,11 +100,13 @@ def tile_list_rgg_ownLP_kernel(
         for window in windows:
             nc.gpsimd.memset(window[:], 0.0)
 
-        load_part("wa", wa, 0, N)
+        load_part("wa", wa, 0, N // 2)
+        load_part("wa", wa, N // 2, N)
         load_part("wo", wo, 0, N // 2)
         load_state(1)
+        load_state(0)
         load_part("wo", wo, N // 2, N)
-        for s in (0, 2, 3):
+        for s in (2, 3):
             load_state(s)
 
         picked_plane = {}
@@ -243,26 +245,27 @@ def tile_list_rgg_ownLP_kernel(
             tile = held(name, [P, J], F32, tag)
             return [tile[:, half_cols(h)] for h in range(2)]
 
-        message[0, 0] = held("first_message", [P, HALF], F32, "grouped_wb")[:]
+        message[0, 0] = held("first_message", [P, HALF], F32, "raw_wa256")[:]
         message_of(0, 0)
         picked[1] = held("picked1", [P, J], F32)[:]
         nc.vector.tensor_tensor(picked[1], listed(state[1], 0, J), wg_row, MULT)
-        round_weight("wo")
-        quantise_weight("wo")
-        behind_wo = held("behind_wo", [P, 5, HALF], F32, "raw_wo256")
-        picked[0] = behind_wo[:, 3:5, :].rearrange("p h c -> p (h c)")
+        picked[0] = held("picked0", [P, J], F32)[:]
         for h in range(2):
             nc.vector.tensor_copy(picked[0][:, half_cols(h)], listed(state[0], HALF * h, HALF * (h + 1)))
+        round_weight("wo")
+        quantise_weight("wo")
 
-        room_e = [behind_wo[:, h, :] for h in range(2)]
-        message[0, 1] = behind_wo[:, 2, :]
+        room_e = two_halves("room_e")
+        message[0, 1] = held("second_message", [P, HALF], F32, "raw_wo0")[:]
         room_m = [message[0, h] for h in range(2)]
-        room_g, room_b = two_halves("room_g"), two_halves("room_b")
-        room_n, room_o = two_halves("room_n"), two_halves("room_o")
+        room_g, room_b = two_halves("room_g"), two_halves("room_b", "raw_wo256")
+        room_n = two_halves("room_n")
+        room_o = [held("room_o%d" % h, [P, HALF], F32)[:] for h in range(2)]
+        behind_o = [held("behind_o%d" % h, [P, 2, HALF], F32, "room_o%d" % h) for h in range(2)]
         for h in range(2):
             eta[0, h], gated[0, h], residual[0, h], own[0, h] = room_e[h], room_g[h], room_b[h], room_o[h]
-            eta[1, h], message[1, h], own[1, h] = room_b[h], room_g[h], room_e[h]
-            eta[2, h], message[2, h], own[2, h] = room_m[h], room_n[h], room_o[h]
+            eta[1, h], message[1, h], own[1, h] = room_b[h], behind_o[h][:, 0, :], behind_o[h][:, 1, :]
+            eta[2, h], message[2, h], own[2, h] = room_m[h], room_n[h], room_g[h]
         gate_of(0, 0)
         let_through(0, 0)
         message_of(0, 1)
@@ -273,7 +276,7 @@ def tile_list_rgg_ownLP_kernel(
         for h in range(2):
             residual_of(0, h)
 
-        windows.append(held("window2", [P, T], F32, "state0"))
+        windows.append(held("window2", [P, T], F32, "grouped_wo"))
         nc.gpsimd.memset(windows[2][:], 0.0)
         picked[2] = held("picked2", [P, J], F32)[:]
         nc.vector.tensor_tensor(picked[2], listed(state[2], 0, J), wg_row, MULT)
@@ -281,7 +284,7 @@ def tile_list_rgg_ownLP_kernel(
         nc.vector.tensor_tensor(picked[3][:, 0:FRONT], listed(state[3], 0, FRONT), wg_row[:, 0:FRONT], MULT)
         totals[0] = first[:, 0:J]
         for h in range(2):
-            turn_and_add(totals[0][:, half_cols(h)], (own[0, h], gated[0, h], residual[0, h]), h, "turn")
+            turn_and_add(totals[0][:, half_cols(h)], (residual[0, h], gated[0, h], own[0, h]), h, "turn")
         nc.vector.tensor_tensor(picked[3][:, FRONT:J], listed(state[3], FRONT, J), wg_row[:, FRONT:J], MULT)
         scatter_total(0, 0, J)
         y_rows = out_0.rearrange("(p t) c -> t p c", t=PACK)

from contextlib import ExitStack

import concourse.mybir as mybir
from concourse.masks import make_identity

K, N, T, J = 512, 512, 2048, 1024
FLOPS = 4 * 2 * K * N * J

F32 = mybir.dt.float32
BF16 = mybir.dt.bfloat16
I32 = mybir.dt.int32
U32 = mybir.dt.uint32
U16 = mybir.dt.uint16
U8 = mybir.dt.uint8
FP8X4 = mybir.dt.float8_e4m3fn_x4
FP4X4 = mybir.dt.float4_e2m1fn_x4
MULT = mybir.AluOpType.mult
ADD = mybir.AluOpType.add
COPY = mybir.ActivationFunctionType.Copy
SIGMOID = mybir.ActivationFunctionType.Sigmoid

P = 128
PACK = 4
EDGE_TILES = J // P
HALF = J // 2
CHUNK = 512
ORDER = (2, 1, 0, 3)
SHARE = 1024
FRONT = 384


def tile_list_rgg_ownLP_kernel(
    tc, tab_words, tab_scales, wa, wb, wc_words, wc_scales, wo, rT, wgo, offs, offs2, out_0, out_1, out_2
):
    nc = tc.nc
    with ExitStack() as ctx:
        keep = ctx.enter_context(tc.tile_pool(name="keep", bufs=1))
        psum = ctx.enter_context(tc.psum_pool(name="psum", bufs=1))

        def held(name, shape, dtype, tag=None):
            return keep.tile(shape, dtype, name=name, tag=tag or name, align_bytes=256)

        def bank(tag):
            return psum.tile([P, HALF], F32, name=tag, tag=tag)

        def load_scale_rows(plane, rows):
            for q in range(4):
                nc.sync.dma_start(out=plane[32 * q : 32 * q + 4, :].bitcast(I32), in_=rows.bitcast(I32)[4 * q : 4 * q + 4, :])

        def tile_cols(i):
            return slice(P * i, P * (i + 1))

        def half_cols(h):
            return slice(HALF * h, HALF * (h + 1))

        src = held("src", [P, J // 16], U16)
        dst = held("dst", [P, J // 16], U16)
        tab_plane = held("tab_plane", [P, T], U8)
        tab_codes = held("tab_codes", [P, T], I32)
        wc_rows = held("wc_rows", [P, N], U8)
        wc_raw = held("wc_raw", [P, 2 * N], U8)
        wg_cut = held("wg_cut", [P, P], F32)
        nc.gpsimd.memset(wg_cut[:], 0.0)
        nc.gpsimd.memset(wc_rows[:].bitcast(I32), 0)
        nc.sync.dma_start(src[:], offs)
        for q in range(4):
            nc.sync.dma_start(
                out=tab_plane[32 * q : 32 * (q + 1), :].bitcast(I32),
                in_=tab_scales[0].bitcast(I32)[4 * q : 4 * q + 4, :].unsqueeze(0).to_broadcast([8, 4, T // 4]),
            )
        raw = {}

        def load_part(name, w, lo, hi):
            part = held("raw_%s%d" % (name, lo), [P, PACK, hi - lo], F32)
            nc.sync.dma_start(out=part[:], in_=w.rearrange("(p i) n -> p i n", i=PACK)[:, :, lo:hi])
            raw.setdefault(name, []).append((lo, hi, part))

        r_rows = rT.rearrange("(p t) c -> t p c", t=PACK)
        state = {}

        def load_state(s):
            state[s] = held("state%d" % s, [P, T], F32)
            nc.sync.dma_start(out=state[s][:], in_=r_rows[ORDER[s]])

        nc.sync.dma_start(dst[:], offs2)
        nc.sync.dma_start(out=wg_cut[0:EDGE_TILES, :], in_=wgo[0].rearrange("(e j) -> e j", j=P))
        load_part("wb", wb, 0, N)
        nc.sync.dma_start(out=tab_codes[:], in_=tab_words[0].rearrange("p t i -> p (t i)").bitcast(I32))
        nc.sync.dma_start(out=wc_raw[:].bitcast(I32), in_=wc_words[0].bitcast(I32))
        load_scale_rows(wc_rows, wc_scales[0])

        warm_in = held("warm_in", [P, 1], F32)
        warm_out = held("warm_out", [P, 1], F32)
        nc.vector.memset(warm_in[:], 0.0)
        nc.scalar.activation(warm_out[:], warm_in[:], SIGMOID)

        ident = held("ident", [P, P], F32)
        make_identity(nc, ident[:])
        windows = [held("window%d" % i, [P, T], F32) for i in range(2)]
        for window in windows:
            nc.gpsimd.memset(window[:], 0.0)

        load_part("wa", wa, 0, N // 2)
        load_part("wa", wa, N // 2, N)
        load_part("wo", wo, 0, N // 2)
        load_state(1)
        load_state(0)
        load_part("wo", wo, N // 2, N)
        for s in (2, 3):
            load_state(s)

        picked_plane = {}
        picked_codes = {}
        for name, lst in (("src", src), ("dst", dst)):
            picked_plane[name] = held("plane_" + name, [P, J], U8)
            nc.vector.tensor_copy(picked_plane[name][:], tab_plane[:].indirect(lst[:]))

        def gather_codes(name, lst, h):
            picked_codes[name, h] = held("codes_%s%d" % (name, h), [P, HALF], U32)
            nc.vector.tensor_copy(
                picked_codes[name, h][:], tab_codes[:].bitcast(U32).indirect(lst[:, 32 * h : 32 * (h + 1)])
            )

        first = held("first", [P, 2 * J - FRONT], F32)
        wg_row = first[:, J - FRONT :]
        wg_col = held("wg_col", [P, EDGE_TILES], F32)
        wg_turned = bank("turn0")
        nc.tensor.transpose(wg_turned[:, 0:P], wg_cut[:], ident[:])
        nc.scalar.copy(wg_col[:], wg_turned[:, 0:EDGE_TILES])
        for h in range(2):
            spread = bank("turn%d" % (1 - h))
            for i in range(PACK):
                e = PACK * h + i
                nc.tensor.transpose(spread[:, tile_cols(i)], wg_col[:, e : e + 1].to_broadcast([P, P]), ident[:])
            nc.scalar.copy(wg_row[:, half_cols(h)], spread[:])

        grouped = {}
        w_codes = {}
        w_plane = {}

        def round_weight(name):
            grouped[name] = held("grouped_" + name, [P, N, PACK], BF16)
            for lo, hi, part in raw[name]:
                nc.scalar.copy(
                    grouped[name][:].rearrange("p (t m) i -> p m i t", t=PACK)[:, lo // PACK : hi // PACK],
                    part[:].rearrange("p i (m t) -> p m i t", t=PACK),
                )

        def quantise_weight(name, tag=None):
            w_codes[name] = held("wcodes_" + name, [P, N], U32, tag)
            w_plane[name] = held("wplane_" + name, [P, N], U8)
            nc.vector.quantize_mx(
                out=w_codes[name][:].bitcast(FP8X4),
                scales=w_plane[name][:],
                in_=grouped[name][:].rearrange("p n i -> p (n i)"),
            )

        round_weight("wb")
        for name, lst in (("src", src), ("dst", dst)):
            for h in range(2):
                gather_codes(name, lst, h)
        w_plane["wc"] = held("wc_plane", [P, N], U8)
        wc_codes = held("wc_codes", [P, 2 * N], U8)
        nc.scalar.copy(
            wc_codes[:].bitcast(U16).rearrange("p (t m) -> p t m", t=PACK),
            wc_raw[:].bitcast(U16).rearrange("p (m t) -> p t m", t=PACK),
        )
        nc.gpsimd.tensor_copy(
            w_plane["wc"][:].rearrange("p (t m) -> p t m", t=PACK), wc_rows[:].rearrange("p (m t) -> p t m", t=PACK)
        )
        round_weight("wa")
        quantise_weight("wb", "raw_wa0")
        quantise_weight("wa")

        def product(out, side, e, name, t, start, stop):
            if name == "wc":
                codes = wc_codes[:, 2 * P * t : 2 * P * (t + 1)].bitcast(FP4X4)
            else:
                codes = w_codes[name][:, P * t : P * (t + 1)].bitcast(FP8X4)
            nc.tensor.matmul_mx(
                out=out,
                lhsT=picked_codes[side, e // PACK][:, tile_cols(e % PACK)].bitcast(FP8X4),
                lhsT_scale=picked_plane[side][:, P * e : P * (e + 1)],
                rhs=codes,
                rhs_scale=w_plane[name][:, P * t : P * (t + 1)],
                start=start,
                stop=stop,
            )

        eta, message, own, gated, residual, sums, totals, picked = {}, {}, {}, {}, {}, {}, {}, {}

        def copy_weighted(out, source, h):
            for i in range(PACK):
                e = PACK * h + i
                nc.scalar.activation(out[:, tile_cols(i)], source[:, tile_cols(i)], COPY, scale=wg_col[:, e : e + 1])

        def gate_of(s, h):
            za = bank("%s%d" % ("turn" if s else "gate", h))
            for i in range(PACK):
                product(za[:, tile_cols(i)], "src", PACK * h + i, "wb", ORDER[s], True, False)
                product(za[:, tile_cols(i)], "dst", PACK * h + i, "wa", ORDER[s], False, True)
            nc.scalar.activation(eta[s, h], za[:], SIGMOID)

        def message_of(s, h):
            ms = bank("message%d" % h)
            for i in range(PACK):
                product(ms[:, tile_cols(i)], "src", PACK * h + i, "wc", ORDER[s], True, True)
            copy_weighted(message[s, h], ms, h)

        def own_of(s, h):
            ow = bank("%s%d" % ("own" if s < 2 else "message", h))
            for i in range(PACK):
                product(ow[:, tile_cols(i)], "dst", PACK * h + i, "wo", ORDER[s], True, True)
            copy_weighted(own[s, h], ow, h)

        def residual_of(s, h):
            back = bank("gate%d" % h)
            for i in range(PACK):
                nc.tensor.transpose(back[:, tile_cols(i)], picked[s][:, tile_cols(PACK * h + i)], ident[:])
            copy_weighted(residual[s, h], back, h)

        def let_through(s, h):
            nc.gpsimd.tensor_tensor(gated[s, h], message[s, h], eta[s, h], MULT)

        def turn_and_add(out, parts, h, tag, first_last=False):
            turned = bank("%s%d" % (tag, h))
            terms = [(part, tile_cols(i)) for part in parts for i in range(PACK)]
            if first_last:
                terms.append(terms.pop(PACK - 1))
            for n, (part, cols) in enumerate(terms):
                begin, final = n == 0, n == len(terms) - 1
                nc.tensor.matmul(turned[:, cols], part[:, cols], ident[:], start=begin, stop=final, is_transpose=True)
            nc.scalar.copy(out, turned[:])

        def listed(tile, lo, hi):
            return tile[:].indirect(dst[:, lo // 16 : hi // 16])

        def add_state(s, h):
            nc.gpsimd.tensor_tensor(totals[s][:, half_cols(h)], picked[s][:, half_cols(h)], sums[s, h], ADD)

        def scatter_total(s, lo, hi):
            nc.vector.tensor_copy(listed(windows[s], lo, hi), totals[s][:, lo:hi])

        def two_halves(name, tag=None):
            tile = held(name, [P, J], F32, tag)
            return [tile[:, half_cols(h)] for h in range(2)]

        message[0, 0] = held("first_message", [P, HALF], F32, "raw_wa256")[:]
        message_of(0, 0)
        picked[1] = held("picked1", [P, J], F32)[:]
        nc.vector.tensor_tensor(picked[1], listed(state[1], 0, J), wg_row, MULT)
        picked[0] = held("picked0", [P, J], F32)[:]
        for h in range(2):
            nc.vector.tensor_copy(picked[0][:, half_cols(h)], listed(state[0], HALF * h, HALF * (h + 1)))
        round_weight("wo")
        quantise_weight("wo")

        room_e = two_halves("room_e")
        message[0, 1] = held("second_message", [P, HALF], F32, "raw_wo0")[:]
        room_m = [message[0, h] for h in range(2)]
        room_g, room_b = two_halves("room_g"), two_halves("room_b", "raw_wo256")
        room_n = two_halves("room_n")
        room_o = [held("room_o%d" % h, [P, HALF], F32)[:] for h in range(2)]
        behind_o = [held("behind_o%d" % h, [P, 2, HALF], F32, "room_o%d" % h) for h in range(2)]
        for h in range(2):
            eta[0, h], gated[0, h], residual[0, h], own[0, h] = room_e[h], room_g[h], room_b[h], room_o[h]
            eta[1, h], message[1, h], own[1, h] = room_b[h], behind_o[h][:, 0, :], behind_o[h][:, 1, :]
            eta[2, h], message[2, h], own[2, h] = room_m[h], room_n[h], room_g[h]
        gate_of(0, 0)
        let_through(0, 0)
        message_of(0, 1)
        gate_of(0, 1)
        let_through(0, 1)
        for h in range(2):
            own_of(0, h)
        for h in range(2):
            residual_of(0, h)

        windows.append(held("window2", [P, T], F32, "grouped_wo"))
        nc.gpsimd.memset(windows[2][:], 0.0)
        picked[2] = held("picked2", [P, J], F32)[:]
        nc.vector.tensor_tensor(picked[2], listed(state[2], 0, J), wg_row, MULT)
        picked[3] = held("picked3", [P, J], F32)[:]
        nc.vector.tensor_tensor(picked[3][:, 0:FRONT], listed(state[3], 0, FRONT), wg_row[:, 0:FRONT], MULT)
        totals[0] = first[:, 0:J]
        for h in range(2):
            turn_and_add(totals[0][:, half_cols(h)], (residual[0, h], gated[0, h], own[0, h]), h, "turn")
        nc.vector.tensor_tensor(picked[3][:, FRONT:J], listed(state[3], FRONT, J), wg_row[:, FRONT:J], MULT)
        scatter_total(0, 0, J)
        y_rows = out_0.rearrange("(p t) c -> t p c", t=PACK)
        nc.sync.dma_start(out=y_rows[ORDER[0]], in_=windows[0][:])

        late = held("late", [P, 2, J], F32, "state3")
        second = held("second", [P, 2, J], F32)
        third = held("third", [P, 2, J], F32, "state1")
        pairs = held("pairs", [P, 2, SHARE], F32)
        ahead = HALF - P
        under_rows = held("under_rows", [P, ahead + (PACK - 1) * HALF], F32)
        rows = under_rows[:, ahead:].rearrange("p (t c) -> p t c", c=HALF)
        spare = held("spare", [P, 5, HALF], F32)
        totals[1], totals[2], last_sums = second[:, 0, :], third[:, 0, :], third[:, 1, :]
        for h in range(2):
            gated[1, h], gated[2, h] = late[:, 0, half_cols(h)], late[:, 1, half_cols(h)]
            sums[3, h] = last_sums[:, half_cols(h)]
        own[3, 0], gated[3, 1] = pairs[:, 0, half_cols(0)], pairs[:, 1, half_cols(1)]
        gated[3, 0], message[3, 0] = second[:, 1, half_cols(0)], second[:, 1, half_cols(1)]
        sums[1, 0], sums[1, 1], sums[2, 0], sums[2, 1], eta[3, 0] = [spare[:, n, :] for n in range(5)]
        eta[3, 1] = pairs[:].rearrange("p u c -> p (u c)")[:, 3 * HALF // 2 : 5 * HALF // 2]
        own[3, 1], message[3, 1] = under_rows[:, 0:HALF], under_rows[:, 2 * HALF - P // 2 : 3 * HALF - P // 2]

        steps = [(1, 0), (2, 0), (1, 1), (2, 1), (3, 0), (3, 1)]

        def open_step(s, h):
            gate_of(s, h)
            message_of(s, h)
            let_through(s, h)
            own_of(s, h)

        open_step(*steps[0])
        for n, (s, h) in enumerate(steps):
            if n + 1 < len(steps):
                open_step(*steps[n + 1])
            parts = (gated[s, h], own[s, h]) if s < PACK - 1 else (own[s, h], gated[s, h])
            turn_and_add(sums[s, h], parts, h, "gate" if s % 2 else "own", n + 1 == len(steps))
            if s < PACK - 1:
                add_state(s, h)
                scatter_total(s, HALF * h, HALF * (h + 1))
                if h == 1:
                    nc.sync.dma_start(out=y_rows[ORDER[s]], in_=windows[s][:])

        rounded = held("rounded", [P, T, PACK], BF16)
        y_codes = held("y_codes", [P, T], I32)
        y_plane = held("y_plane", [P, T // 2], U8)
        code_rows = out_1[0].rearrange("p t i -> p (t i)").bitcast(I32)

        def round_columns(move, s, lo, hi):
            move(rounded[:, lo:hi, ORDER[s]], windows[s % 3][:, lo:hi])

        def round_pairs(move, s, lo, hi):
            halves = pairs[:].bitcast(BF16).rearrange("p u (c e) -> p u c e", e=2)
            move(halves[:, ORDER[s] // 2, lo:hi, ORDER[s] % 2], windows[s % 3][:, lo:hi])

        def round_on_gpsimd(out, source):
            nc.gpsimd.tensor_scalar(out, source, 1.0, 0.0, MULT, ADD)

        def weave(lo, hi):
            nc.vector.tensor_copy(
                rounded[:, lo:hi, :].rearrange("p c i -> p (c i)").bitcast(F32).rearrange("p (c u) -> p c u", u=2),
                pairs[:].rearrange("p u c -> p c u")[:, lo:hi],
            )

        round_pairs(nc.scalar.copy, 0, 0, CHUNK)
        round_pairs(nc.scalar.copy, 1, 0, SHARE)
        for s in range(2):
            nc.gpsimd.tensor_scalar(rows[:, ORDER[s], :].bitcast(BF16), windows[s][:, SHARE:T], 1.0, 0.0, MULT, ADD)
        round_pairs(round_on_gpsimd, 0, CHUNK, SHARE)
        nc.scalar.copy(rows[:, ORDER[2], :].bitcast(BF16), windows[2][:, SHARE:T])
        round_pairs(nc.scalar.copy, 2, 0, SHARE)
        for lo in (0, CHUNK):
            nc.scalar.copy(
                rounded[:, SHARE + lo : SHARE + lo + CHUNK, 0 : PACK - 1].rearrange("p (c i) t -> p c t i", i=PACK),
                rows.bitcast(BF16)[:, :, lo : lo + CHUNK].rearrange("p t (c i) -> p c t i", i=PACK),
            )
        last = PACK - 1
        nc.vector.tensor_tensor(listed(windows[0], 0, J), picked[last], last_sums, ADD)
        nc.sync.dma_start(out=y_rows[ORDER[last]], in_=windows[0][:])
        round_pairs(nc.vector.tensor_copy, last, 0, CHUNK)
        round_pairs(nc.vector.tensor_copy, last, CHUNK, SHARE)
        weave(0, CHUNK)
        weave(CHUNK, SHARE)
        cuts = (2 * CHUNK, 3 * CHUNK, T - CHUNK // 2, T)
        for lo, hi in zip(cuts, cuts[1:]):
            round_columns(nc.scalar.copy, last, lo, hi)

        def quantise_columns(lo, hi):
            h = lo // (T // 2)
            nc.vector.quantize_mx(
                out=y_codes[:, lo:hi].bitcast(FP8X4),
                scales=y_plane[4 * h : P, lo - T // 2 * h : hi - T // 2 * h],
                in_=rounded[:, lo:hi, :].rearrange("p c i -> p (c i)"),
            )

        def store_codes(lo, hi):
            nc.sync.dma_start(out=code_rows[:, lo:hi], in_=y_codes[:, lo:hi])

        quantise_columns(0, CHUNK)
        store_codes(0, CHUNK)
        quantise_columns(CHUNK, 2 * CHUNK)
        store_codes(CHUNK, 2 * CHUNK)
        quantise_columns(2 * CHUNK, 3 * CHUNK)
        store_codes(2 * CHUNK, 3 * CHUNK)
        quantise_columns(3 * CHUNK, T - CHUNK // 2)
        store_codes(3 * CHUNK, T - CHUNK // 2)
        quantise_columns(T - CHUNK // 2, T)
        store_codes(T - CHUNK // 2, T)
        scale_rows = out_2[0].bitcast(I32)
        for q in range(4):
            queue = nc.scalar if q % 2 else nc.sync
            queue.dma_start(
                out=scale_rows[4 * q : 4 * q + 4, :].rearrange("r (h j) -> h r j", h=2),
                in_=y_plane[32 * q : 32 * q + 8, :].bitcast(I32),
            )
